import numpy as np
import ml_dtypes


def mxq(x, axis, fmt="e4m3"):
    dtype, down = {"e4m3": (ml_dtypes.float8_e4m3fn, 7), "e5m2": (ml_dtypes.float8_e5m2, 14)}[fmt]
    v = np.moveaxis(np.asarray(x, np.float32).astype(ml_dtypes.bfloat16).astype(np.float64), axis, -1)
    blocks = v.reshape(v.shape[:-1] + (-1, 32))
    amax = np.abs(blocks).max(-1, keepdims=True)
    byte = np.maximum(np.where(amax > 0, np.frexp(amax)[1] - 1 + 127, 0) - down, 1)
    scale = np.exp2(byte - 127.0)
    codes = (blocks / scale).astype(np.float32).astype(dtype).astype(np.float64)
    return np.moveaxis((codes * scale).reshape(v.shape), -1, axis)


WIDE = False


def mx_kscale(k):
    if not WIDE:
        return np.ones(k)
    levels = np.array([10, -10, 5, -5, 0])
    if k % 512:
        return np.exp2(np.random.permutation(np.resize(levels, k // 32))).repeat(32)
    a = np.empty((k // 512, 16))
    for p in range(k // 512):
        a[p, :8] = np.random.permutation(np.resize(levels, 8))
        for g in range(8):
            far = levels[np.abs(levels - a[p, g]) >= 10]
            a[p, g + 8] = far[np.random.randint(len(far))]
    return np.exp2(a.ravel()).repeat(32)


def f64(x):
    return np.asarray(x).astype(np.float64)


def striped(idx):
    return np.tile(np.asarray(idx).reshape(-1, 16).T, (8, 1)).astype(np.uint16)


def unstriped(offs):
    return offs[:16].T.reshape(-1).astype(np.int64)


B, N, T, D, DV, NQ = 1, 1024, 4096, 512, 128, 256


def setup_inputs():
    n = np.random.standard_normal
    idx = np.random.permutation(T)[:B * N]
    s = mx_kscale(D)[:, None]
    u = np.ones(T)
    u[idx] = mx_kscale(B * N)
    r = np.random.uniform(0.5, 2.0, T)
    k = n((D, T)) / s
    v = n((DV, T)) / (u * r)
    return {
        "qT": (n((B, D, NQ)) * s * (0.80 / np.sqrt(D))).astype(np.float32),
        "kT": k.astype(np.float32),
        "vT": v.astype(np.float32),
        "vs": np.tile(u * r, (128, 1)).astype(np.float32),
        "sink": (2.0 + 3.0 * n((B, NQ, 1))).astype(np.float32),
        "offs": striped(idx),
    }


def reference(qT, kT, vT, vs, sink, offs):
    idx = unstriped(offs)
    k = f64(kT)
    v = f64(vT)
    pick = lambda x: x[:, idx].reshape(x.shape[0], B, N).transpose(1, 0, 2)
    q = f64(qT)
    score = mxq(q, 1, "e4m3").transpose(0, 2, 1) @ mxq(pick(k), 1, "e4m3")
    m = np.maximum(score.max(-1, keepdims=True), f64(sink))
    p = np.exp(score - m)
    total = p.sum(-1, keepdims=True) + np.exp(f64(sink) - m)
    w = p * pick(f64(vs))[:, :1, :]
    y = mxq(w, 2, "e4m3") @ mxq(pick(v).transpose(0, 2, 1), 1, "e4m3")
    y = y / total
    return y

@@ -1,0 +1,236 @@
+from contextlib import ExitStack
+
+import concourse.mybir as mybir
+from concourse.masks import make_identity
+
+D, DV, NQ, T, N = 512, 128, 256, 4096, 1024
+
+FLOPS = 2 * NQ * N * (D + DV)
+BYTES = 4 * (D * T + DV * T + T + D * NQ + NQ + NQ * DV) + 2 * 128 * (N // 16)
+
+F32 = mybir.dt.float32
+BF16 = mybir.dt.bfloat16
+U32 = mybir.dt.uint32
+U16 = mybir.dt.uint16
+U8 = mybir.dt.uint8
+FP8X4 = mybir.dt.float8_e4m3fn_x4
+ALU = mybir.AluOpType
+ACT = mybir.ActivationFunctionType
+AX = mybir.AxisListType
+
+P = 128
+PACK = 4
+HALF = 512
+
+
+def tile_attend_sink_topk_kernel(tc, qT, kT, vT, vs, sink, offs, out):
+    nc = tc.nc
+    with ExitStack() as ctx:
+        lists = ctx.enter_context(tc.tile_pool(name="lists", bufs=1))
+        keep = ctx.enter_context(tc.tile_pool(name="keep", bufs=1))
+        score_banks = ctx.enter_context(tc.psum_pool(name="score_banks", bufs=4))
+        turn_banks = ctx.enter_context(tc.psum_pool(name="turn_banks", bufs=4))
+
+        offsets = lists.tile([P, N // 16], U16, name="offsets")
+        nc.sync.dma_start(offsets[:], offs)
+
+        vs_table = keep.tile([P, T], F32, name="vs_table")
+        nc.vector.memset(vs_table[:], 0.0)
+        sink_raw = keep.tile([P, 2], F32, name="sink_raw")
+        nc.scalar.dma_start(out=sink_raw[:], in_=sink[0].rearrange("(m j) x -> m (j x)", j=2))
+        warm = keep.tile([P, 1], F32, name="warm")
+        nc.gpsimd.memset(warm[:], 0.0)
+        warmed = keep.tile([P, 1], F32, name="warmed")
+        nc.scalar.activation(out=warmed[:], in_=warm[:], func=ACT.Exp)
+
+        k_rows = kT.rearrange("(p t) c -> p t c", t=PACK)
+        k_table = [keep.tile([P, T], F32, name=f"k_table{t}") for t in range(PACK)]
+        for t in range(PACK):
+            nc.sync.dma_start(out=k_table[t][:], in_=k_rows[:, t, :])
+            if t == 0:
+                nc.sync.dma_start(out=vs_table[0:1, :], in_=vs[0:1, :])
+        q_raw = keep.tile([P, PACK, NQ], F32, name="q_raw")
+        nc.sync.dma_start(out=q_raw[:], in_=qT[0].rearrange("(p t) q -> p t q", t=PACK))
+        v_table = keep.tile([P, T], F32, name="v_table")
+        nc.sync.dma_start(out=v_table[:], in_=vT)
+
+        ident = keep.tile([P, P], F32, name="ident")
+        make_identity(nc, ident[:])
+
+        nsink = keep.tile([P, 2], F32, name="nsink")
+        nc.scalar.activation(out=nsink[:], in_=sink_raw[:], func=ACT.Copy, scale=-1.0)
+
+        k_grouped = [keep.tile([P, HALF, PACK], BF16, name=f"k_grouped{h}", align_bytes=64) for h in range(2)]
+        k_low = keep.tile([P, 2, N], F32, name="k_low")
+        k_high = keep.tile([P, 2, HALF], F32, name="k_high")
+        nc.vector.tensor_copy(k_low[:, 0, :], k_table[0][:].indirect(offsets[:]))
+
+        vs_picked = keep.tile([P, N], F32, name="vs_picked")
+        nc.vector.tensor_copy(vs_picked[:], vs_table[:].indirect(offsets[:]))
+        vcol = keep.tile([P, 2 * PACK], F32, name="vcol")
+        for g in range(2):
+            turned = turn_banks.tile([P, PACK, P], F32, name="turned")
+            for t in range(PACK):
+                nc.tensor.transpose(turned[:, t, :], vs_picked[:, g * HALF + t : (g + 1) * HALF : PACK], ident[:])
+            nc.scalar.copy(out=vcol[:, g * PACK : (g + 1) * PACK], in_=turned[:, :, 0])
+
+        nc.vector.tensor_copy(k_low[:, 1, :], k_table[1][:].indirect(offsets[:]))
+        for h in (1, 0):
+            nc.scalar.activation(
+                out=k_grouped[h][:, :, 0:2], in_=k_low[:, :, h * HALF : (h + 1) * HALF].rearrange("p t n -> p n t"), func=ACT.Copy
+            )
+        for t in (2, 3):
+            nc.vector.tensor_copy(k_high[:, t - 2, :], k_table[t][:].indirect(offsets[:, 0 : HALF // 16]))
+            nc.vector.tensor_copy(k_grouped[1][:, :, t], k_table[t][:].indirect(offsets[:, HALF // 16 : N // 16]))
+        nc.scalar.activation(out=k_grouped[0][:, :, 2:4], in_=k_high[:].rearrange("p t n -> p n t"), func=ACT.Copy)
+
+        for rep in range(4):
+            turned = turn_banks.tile([P, PACK, P], F32, name="turned")
+            for t in range(PACK):
+                nc.tensor.transpose(turned[:, t, :], q_raw[:, t, 0:P], ident[:])
+
+        q_grouped = keep.tile([P, NQ, PACK], BF16, name="q_grouped", align_bytes=64)
+        nc.gpsimd.tensor_scalar(
+            out=q_grouped[:].rearrange("p (j m) t -> p j m t", j=2),
+            in0=q_raw[:].rearrange("p t (m j) -> p j m t", j=2),
+            scalar1=-1.0,
+            scalar2=0.0,
+            op0=ALU.mult,
+            op1=ALU.add,
+        )
+        q_codes = keep.tile([P, NQ], U32, name="q_codes", align_bytes=64)
+        q_scales = keep.tile([P, NQ], U8, name="q_scales", align_bytes=64)
+
+        k_codes = keep.tile([P, N], U32, name="k_codes", align_bytes=64)
+        k_scales = keep.tile([P, N], U8, name="k_scales", align_bytes=64)
+        scores = {}
+        for h in (1, 0):
+            cols = slice(h * HALF, (h + 1) * HALF)
+            nc.vector.quantize_mx(
+                out=k_codes[:, cols].bitcast(FP8X4),
+                scales=k_scales[:, cols],
+                in_=k_grouped[h][:].rearrange("p n t -> p (n t)"),
+            )
+            if h == 1:
+                nc.vector.quantize_mx(
+                    out=q_codes[:].bitcast(FP8X4), scales=q_scales[:], in_=q_grouped[:].rearrange("p n t -> p (n t)")
+                )
+            for j in range(2):
+                queries = slice(j * P, (j + 1) * P)
+                scores[j, h] = score_banks.tile([P, HALF], F32, name="score")
+                nc.tensor.matmul_mx(
+                    out=scores[j, h][:],
+                    lhsT=q_codes[:, queries].bitcast(FP8X4),
+                    lhsT_scale=q_scales[:, queries],
+                    rhs=k_codes[:, cols].bitcast(FP8X4),
+                    rhs_scale=k_scales[:, cols],
+                    start=True,
+                    stop=True,
+                )
+
+        low = {}
+        for h in (1, 0):
+            for j in range(2):
+                unused = keep.tile([P, HALF], F32, name=f"unused{j}{h}")
+                low[j, h] = keep.tile([P, 1], F32, name=f"low{j}{h}")
+                nc.vector.tensor_scalar(
+                    out=unused[:],
+                    in0=scores[j, h][:],
+                    scalar1=1.0,
+                    scalar2=nsink[:, j : j + 1] if h == 1 else low[j, 1][:],
+                    op0=ALU.mult,
+                    op1=ALU.min,
+                    accum_out=low[j, h][:],
+                )
+
+        v_picked = keep.tile([P, N], F32, name="v_picked")
+        v_pairs = keep.tile([P, 2, 2, P, 2], BF16, name="v_pairs")
+        v_turned = turn_banks.tile([P, 2, 2, P], F32, name="turned")
+        v_grouped = keep.tile([P, 2, P, PACK], BF16, name="v_grouped", align_bytes=64)
+        for g in range(2):
+            nc.vector.tensor_copy(
+                v_picked[:, g * HALF : (g + 1) * HALF],
+                v_table[:].indirect(offsets[:, g * (HALF // 16) : (g + 1) * (HALF // 16)]),
+            )
+
+        sums = keep.tile([P, 2, 3], F32, name="sums")
+        probs = {}
+        for j in range(2):
+            for h in range(2):
+                probs[j, h] = keep.tile([P, PACK, P], F32, name=f"probs{j}{h}")
+                nc.scalar.activation(
+                    out=probs[j, h][:],
+                    in_=scores[j, h][:].rearrange("p (s t) -> p t s", t=PACK),
+                    func=ACT.Exp,
+                    bias=low[j, 0][:],
+                    scale=-1.0,
+                    accum_out=sums[:, j, h : h + 1],
+                )
+                if (j, h) in ((0, 1), (1, 0)):
+                    g = j
+                    nc.scalar.activation(
+                        out=v_pairs[:, g, :, :, :],
+                        in_=v_picked[:, g * HALF : (g + 1) * HALF].rearrange("p (s u w) -> p u s w", u=2, w=2),
+                        func=ACT.Copy,
+                    )
+        for j in range(2):
+            nc.scalar.activation(out=sums[:, j, 2:3], in_=nsink[:, j : j + 1], func=ACT.Exp, bias=low[j, 0][:], scale=-1.0)
+
+        parts = [(j, g) for j in range(2) for g in range(2)]
+        w_grouped = {(j, g): keep.tile([P, P, PACK], BF16, name=f"w_grouped{j}{g}", align_bytes=64) for j, g in parts}
+        w_codes = {(j, g): keep.tile([P, P], U32, name=f"w_codes{j}{g}", align_bytes=64) for j, g in parts}
+        w_scales = {(j, g): keep.tile([P, P], U8, name=f"w_scales{j}{g}", align_bytes=64) for j, g in parts}
+        v_codes = keep.tile([P, 2, P], U32, name="v_codes", align_bytes=64)
+        v_scales = keep.tile([P, 2, P], U8, name="v_scales", align_bytes=64)
+        total = keep.tile([P, 2], F32, name="total")
+        share = keep.tile([P, 2], F32, name="share")
+
+        for j in range(2):
+            for g in range(2):
+                turned = turn_banks.tile([P, PACK, P], F32, name="turned")
+                for t in range(PACK):
+                    nc.tensor.transpose(turned[:, t, :], probs[j, g][:, t, :], ident[:])
+                nc.vector.tensor_tensor(
+                    w_grouped[j, g][:],
+                    turned[:].rearrange("p t q -> p q t"),
+                    vcol[:, g * PACK : (g + 1) * PACK].unsqueeze(1).to_broadcast([P, P, PACK]),
+                    ALU.mult,
+                )
+            if j == 0:
+                v_words = v_pairs[:].rearrange("p g u s w -> p (g u s w)").bitcast(F32)
+                for g in range(2):
+                    for u in range(2):
+                        first = (2 * g + u) * P
+                        nc.tensor.transpose(v_turned[:, g, u, :], v_words[:, first : first + P], ident[:])
+                nc.scalar.copy(
+                    out=v_grouped[:].rearrange("p g e t -> p (g e t)").bitcast(F32).rearrange("p (g e u) -> p g e u", g=2, u=2),
+                    in_=v_turned[:].rearrange("p g u e -> p g e u"),
+                )
+            else:
+                nc.vector.quantize_mx(
+                    out=v_codes[:].rearrange("p g e -> p (g e)").bitcast(FP8X4),
+                    scales=v_scales[:].rearrange("p g e -> p (g e)"),
+                    in_=v_grouped[:].rearrange("p g e t -> p (g e t)"),
+                )
+                nc.vector.tensor_reduce(out=total[:], in_=sums[:], axis=AX.X, op=ALU.add)
+            for g in range(2):
+                nc.vector.quantize_mx(
+                    out=w_codes[j, g][:].bitcast(FP8X4), scales=w_scales[j, g][:], in_=w_grouped[j, g][:].rearrange("p q t -> p (q t)")
+                )
+                if (j, g) == (1, 0):
+                    nc.vector.reciprocal(share[:], total[:])
+        for j in range(2):
+            acc = score_banks.tile([P, DV], F32, name="score")
+            for g in range(2):
+                nc.tensor.matmul_mx(
+                    out=acc[:],
+                    lhsT=w_codes[j, g][:].bitcast(FP8X4),
+                    lhsT_scale=w_scales[j, g][:],
+                    rhs=v_codes[:, g, :].bitcast(FP8X4),
+                    rhs_scale=v_scales[:, g, :],
+                    start=(g == 0),
+                    stop=(g == 1),
+                )
+            result = keep.tile([P, DV], F32, name=f"result{j}")
+            nc.scalar.activation(out=result[:], in_=acc[:], func=ACT.Copy, scale=share[:, j : j + 1])
+            nc.sync.dma_start(out=out[0].rearrange("(m j) e -> m j e", j=2)[:, j, :], in_=result[:])

@@ -73,6 +73,13 @@ def tile_attend_sink_topk_kernel(tc, qT, kT, vT, vs, sink, offs, out):
             for t in range(PACK):
                 nc.tensor.transpose(turned[:, t, :], vs_picked[:, g * HALF + t : (g + 1) * HALF : PACK], ident[:])
             nc.scalar.copy(out=vcol[:, g * PACK : (g + 1) * PACK], in_=turned[:, :, 0])
+        vs_rows = [keep.tile([P, 2, P, 2], F32, name=f"vs_rows{g}") for g in range(2)]
+        for g in range(2):
+            turned = turn_banks.tile([P, PACK, P], F32, name="turned")
+            for t in range(PACK):
+                c = g * PACK + t
+                nc.tensor.transpose(turned[:, t, :], vcol[:, c : c + 1].to_broadcast([P, P]), ident[:])
+            nc.scalar.copy(out=vs_rows[g][:], in_=turned[:].rearrange("p (u w) s -> p u s w", u=2))
 
         nc.vector.tensor_copy(k_low[:, 1, :], k_table[1][:].indirect(offsets[:]))
         for h in (1, 0):
@@ -83,11 +90,6 @@ def tile_attend_sink_topk_kernel(tc, qT, kT, vT, vs, sink, offs, out):
             nc.vector.tensor_copy(k_high[:, t - 2, :], k_table[t][:].indirect(offsets[:, 0 : HALF // 16]))
             nc.vector.tensor_copy(k_grouped[1][:, :, t], k_table[t][:].indirect(offsets[:, HALF // 16 : N // 16]))
         nc.scalar.activation(out=k_grouped[0][:, :, 2:4], in_=k_high[:].rearrange("p t n -> p n t"), func=ACT.Copy)
-
-        for rep in range(4):
-            turned = turn_banks.tile([P, PACK, P], F32, name="turned")
-            for t in range(PACK):
-                nc.tensor.transpose(turned[:, t, :], q_raw[:, t, 0:P], ident[:])
 
         q_grouped = keep.tile([P, NQ, PACK], BF16, name="q_grouped", align_bytes=64)
         nc.gpsimd.tensor_scalar(
@@ -143,13 +145,10 @@ def tile_attend_sink_topk_kernel(tc, qT, kT, vT, vs, sink, offs, out):
                     accum_out=low[j, h][:],
                 )
 
-        v_picked = keep.tile([P, N], F32, name="v_picked")
-        v_pairs = keep.tile([P, 2, 2, P, 2], BF16, name="v_pairs")
-        v_turned = turn_banks.tile([P, 2, 2, P], F32, name="turned")
-        v_grouped = keep.tile([P, 2, P, PACK], BF16, name="v_grouped", align_bytes=64)
+        v_picked = [keep.tile([P, HALF], BF16, name=f"v_picked{g}") for g in range(2)]
         for g in range(2):
             nc.vector.tensor_copy(
-                v_picked[:, g * HALF : (g + 1) * HALF],
+                v_picked[g][:],
                 v_table[:].indirect(offsets[:, g * (HALF // 16) : (g + 1) * (HALF // 16)]),
             )
 
@@ -158,76 +157,79 @@ def tile_attend_sink_topk_kernel(tc, qT, kT, vT, vs, sink, offs, out):
         for j in range(2):
             for h in range(2):
                 probs[j, h] = keep.tile([P, PACK, P], F32, name=f"probs{j}{h}")
+                if j == 0:
+                    laid = probs[j, h][:].rearrange("p t s -> p (t s)").rearrange("p (u s w) -> p u s w", u=2, w=2)
+                    read = scores[j, h][:].rearrange("p (s u w) -> p u s w", u=2, w=2)
+                else:
+                    laid = probs[j, h][:]
+                    read = scores[j, h][:].rearrange("p (s t) -> p t s", t=PACK)
                 nc.scalar.activation(
-                    out=probs[j, h][:],
-                    in_=scores[j, h][:].rearrange("p (s t) -> p t s", t=PACK),
+                    out=laid,
+                    in_=read,
                     func=ACT.Exp,
                     bias=low[j, 0][:],
                     scale=-1.0,
                     accum_out=sums[:, j, h : h + 1],
                 )
-                if (j, h) in ((0, 1), (1, 0)):
-                    g = j
-                    nc.scalar.activation(
-                        out=v_pairs[:, g, :, :, :],
-                        in_=v_picked[:, g * HALF : (g + 1) * HALF].rearrange("p (s u w) -> p u s w", u=2, w=2),
-                        func=ACT.Copy,
-                    )
-        for j in range(2):
-            nc.scalar.activation(out=sums[:, j, 2:3], in_=nsink[:, j : j + 1], func=ACT.Exp, bias=low[j, 0][:], scale=-1.0)
 
-        parts = [(j, g) for j in range(2) for g in range(2)]
+        parts = [(1, g) for g in range(2)]
         w_grouped = {(j, g): keep.tile([P, P, PACK], BF16, name=f"w_grouped{j}{g}", align_bytes=64) for j, g in parts}
         w_codes = {(j, g): keep.tile([P, P], U32, name=f"w_codes{j}{g}", align_bytes=64) for j, g in parts}
         w_scales = {(j, g): keep.tile([P, P], U8, name=f"w_scales{j}{g}", align_bytes=64) for j, g in parts}
-        v_codes = keep.tile([P, 2, P], U32, name="v_codes", align_bytes=64)
-        v_scales = keep.tile([P, 2, P], U8, name="v_scales", align_bytes=64)
+        wv_grouped = [keep.tile([P, 2, P, PACK], BF16, name=f"wv_grouped{g}", align_bytes=64) for g in range(2)]
+        wv_codes = [keep.tile([P, 2, P], U32, name=f"wv_codes{g}", align_bytes=64) for g in range(2)]
+        wv_scales = [keep.tile([P, 2, P], U8, name=f"wv_scales{g}", align_bytes=64) for g in range(2)]
         total = keep.tile([P, 2], F32, name="total")
         share = keep.tile([P, 2], F32, name="share")
 
+        w_pairs = [keep.tile([P, HALF], BF16, name=f"w_pairs{g}") for g in range(2)]
+        for g in range(2):
+            nc.gpsimd.tensor_tensor(
+                w_pairs[g][:], probs[0, g][:].rearrange("p t s -> p (t s)"), vs_rows[g][:].rearrange("p u s w -> p (u s w)"), ALU.mult
+            )
+        for g in range(2):
+            turned = turn_banks.tile([P, PACK, P], F32, name="turned")
+            for t in range(PACK):
+                nc.tensor.transpose(turned[:, t, :], probs[1, g][:, t, :], ident[:])
+            nc.vector.tensor_tensor(
+                w_grouped[1, g][:],
+                turned[:].rearrange("p t q -> p q t"),
+                vcol[:, g * PACK : (g + 1) * PACK].unsqueeze(1).to_broadcast([P, P, PACK]),
+                ALU.mult,
+            )
+            words = turn_banks.tile([P, 2, 2, P], F32, name="turned")
+            for u in range(2):
+                nc.tensor.transpose(words[:, 0, u, :], w_pairs[g][:].bitcast(F32)[:, u * P : (u + 1) * P], ident[:])
+            for u in range(2):
+                nc.tensor.transpose(words[:, 1, u, :], v_picked[g][:].bitcast(F32)[:, u : 2 * P : 2], ident[:])
+            nc.scalar.copy(
+                out=wv_grouped[g][:].rearrange("p a e t -> p (a e t)").bitcast(F32).rearrange("p (a e u) -> p a e u", a=2, u=2),
+                in_=words[:].rearrange("p a u e -> p a e u"),
+            )
         for j in range(2):
-            for g in range(2):
-                turned = turn_banks.tile([P, PACK, P], F32, name="turned")
-                for t in range(PACK):
-                    nc.tensor.transpose(turned[:, t, :], probs[j, g][:, t, :], ident[:])
-                nc.vector.tensor_tensor(
-                    w_grouped[j, g][:],
-                    turned[:].rearrange("p t q -> p q t"),
-                    vcol[:, g * PACK : (g + 1) * PACK].unsqueeze(1).to_broadcast([P, P, PACK]),
-                    ALU.mult,
-                )
-            if j == 0:
-                v_words = v_pairs[:].rearrange("p g u s w -> p (g u s w)").bitcast(F32)
-                for g in range(2):
-                    for u in range(2):
-                        first = (2 * g + u) * P
-                        nc.tensor.transpose(v_turned[:, g, u, :], v_words[:, first : first + P], ident[:])
-                nc.scalar.copy(
-                    out=v_grouped[:].rearrange("p g e t -> p (g e t)").bitcast(F32).rearrange("p (g e u) -> p g e u", g=2, u=2),
-                    in_=v_turned[:].rearrange("p g u e -> p g e u"),
-                )
-            else:
-                nc.vector.quantize_mx(
-                    out=v_codes[:].rearrange("p g e -> p (g e)").bitcast(FP8X4),
-                    scales=v_scales[:].rearrange("p g e -> p (g e)"),
-                    in_=v_grouped[:].rearrange("p g e t -> p (g e t)"),
-                )
+            nc.scalar.activation(out=sums[:, j, 2:3], in_=nsink[:, j : j + 1], func=ACT.Exp, bias=low[j, 0][:], scale=-1.0)
+        for g in range(2):
+            nc.vector.quantize_mx(
+                out=w_codes[1, g][:].bitcast(FP8X4), scales=w_scales[1, g][:], in_=w_grouped[1, g][:].rearrange("p q t -> p (q t)")
+            )
+            if g == 0:
                 nc.vector.tensor_reduce(out=total[:], in_=sums[:], axis=AX.X, op=ALU.add)
-            for g in range(2):
-                nc.vector.quantize_mx(
-                    out=w_codes[j, g][:].bitcast(FP8X4), scales=w_scales[j, g][:], in_=w_grouped[j, g][:].rearrange("p q t -> p (q t)")
-                )
-                if (j, g) == (1, 0):
-                    nc.vector.reciprocal(share[:], total[:])
-        for j in range(2):
+            nc.vector.quantize_mx(
+                out=wv_codes[g][:].rearrange("p a e -> p (a e)").bitcast(FP8X4),
+                scales=wv_scales[g][:].rearrange("p a e -> p (a e)"),
+                in_=wv_grouped[g][:].rearrange("p a e t -> p (a e t)"),
+            )
+            if g == 0:
+                nc.vector.reciprocal(share[:], total[:])
+        for j in (1, 0):
             acc = score_banks.tile([P, DV], F32, name="score")
             for g in range(2):
                 nc.tensor.matmul_mx(
                     out=acc[:],
-                    lhsT=w_codes[j, g][:].bitcast(FP8X4),
-                    lhsT_scale=w_scales[j, g][:],
-                    rhs=v_codes[:, g, :].bitcast(FP8X4),
-                    rhs_scale=v_scales[:, g, :],
+                    lhsT=(w_codes[j, g][:] if j else wv_codes[g][:, 0, :]).bitcast(FP8X4),
+                    lhsT_scale=w_scales[j, g][:] if j else wv_scales[g][:, 0, :],
+                    rhs=wv_codes[g][:, 1, :].bitcast(FP8X4),
+                    rhs_scale=wv_scales[g][:, 1, :],
                     start=(g == 0),
                     stop=(g == 1),
                 )

@@ -32,10 +32,9 @@ def tile_attend_sink_topk_kernel(tc, qT, kT, vT, vs, sink, offs, out):
         turn_banks = ctx.enter_context(tc.psum_pool(name="turn_banks", bufs=4))
 
         offsets = lists.tile([P, N // 16], U16, name="offsets")
-        nc.sync.dma_start(offsets[:], offs)
-
-        vs_table = keep.tile([P, T], F32, name="vs_table")
-        nc.vector.memset(vs_table[:], 0.0)
+        RUN = T // P
+        vs_runs = keep.tile([P, RUN], F32, name="vs_runs")
+        nc.sync.dma_start(out=vs_runs[:], in_=vs[0].rearrange("(p c) -> p c", c=RUN))
         sink_raw = keep.tile([P, 2], F32, name="sink_raw")
         nc.scalar.dma_start(out=sink_raw[:], in_=sink[0].rearrange("(m j) x -> m (j x)", j=2))
         warm = keep.tile([P, 1], F32, name="warm")
@@ -48,7 +47,7 @@ def tile_attend_sink_topk_kernel(tc, qT, kT, vT, vs, sink, offs, out):
         for t in range(PACK):
             nc.sync.dma_start(out=k_table[t][:], in_=k_rows[:, t, :])
             if t == 0:
-                nc.sync.dma_start(out=vs_table[0:1, :], in_=vs[0:1, :])
+                nc.sync.dma_start(offsets[:], offs)
         q_raw = keep.tile([P, PACK, NQ], F32, name="q_raw")
         nc.sync.dma_start(out=q_raw[:], in_=qT[0].rearrange("(p t) q -> p t q", t=PACK))
         v_table = keep.tile([P, T], F32, name="v_table")
@@ -59,6 +58,16 @@ def tile_attend_sink_topk_kernel(tc, qT, kT, vT, vs, sink, offs, out):
 
         nsink = keep.tile([P, 2], F32, name="nsink")
         nc.scalar.activation(out=nsink[:], in_=sink_raw[:], func=ACT.Copy, scale=-1.0)
+
+        vs_table = keep.tile([P, T], F32, name="vs_table")
+        for b in range(RUN // PACK):
+            turned = turn_banks.tile([P, PACK, P], F32, name="turned")
+            for c in range(PACK):
+                nc.tensor.transpose(turned[:, c, :], vs_runs[:, b * PACK + c : b * PACK + c + 1].to_broadcast([P, P]), ident[:])
+            nc.scalar.copy(
+                out=vs_table[:].rearrange("r (p b c) -> r b p c", c=PACK, b=RUN // PACK)[:, b, :, :],
+                in_=turned[:].rearrange("r c p -> r p c"),
+            )
 
         k_grouped = [keep.tile([P, HALF, PACK], BF16, name=f"k_grouped{h}", align_bytes=64) for h in range(2)]
         k_low = keep.tile([P, 2, N], F32, name="k_low")
@@ -75,11 +84,9 @@ def tile_attend_sink_topk_kernel(tc, qT, kT, vT, vs, sink, offs, out):
             nc.scalar.copy(out=vcol[:, g * PACK : (g + 1) * PACK], in_=turned[:, :, 0])
         vs_rows = [keep.tile([P, 2, P, 2], F32, name=f"vs_rows{g}") for g in range(2)]
         for g in range(2):
-            turned = turn_banks.tile([P, PACK, P], F32, name="turned")
-            for t in range(PACK):
-                c = g * PACK + t
-                nc.tensor.transpose(turned[:, t, :], vcol[:, c : c + 1].to_broadcast([P, P]), ident[:])
-            nc.scalar.copy(out=vs_rows[g][:], in_=turned[:].rearrange("p (u w) s -> p u s w", u=2))
+            nc.scalar.copy(
+                out=vs_rows[g][:], in_=vs_picked[:, g * HALF : (g + 1) * HALF].rearrange("r (s u w) -> r u s w", u=2, w=2)
+            )
 
         nc.vector.tensor_copy(k_low[:, 1, :], k_table[1][:].indirect(offsets[:]))
         for h in (1, 0):

@@ -36,7 +36,8 @@ def tile_attend_sink_topk_kernel(tc, qT, kT, vT, vs, sink, offs, out):
         vs_runs = keep.tile([P, RUN], F32, name="vs_runs")
         nc.sync.dma_start(out=vs_runs[:], in_=vs[0].rearrange("(p c) -> p c", c=RUN))
         sink_raw = keep.tile([P, 2], F32, name="sink_raw")
-        nc.scalar.dma_start(out=sink_raw[:], in_=sink[0].rearrange("(m j) x -> m (j x)", j=2))
+        with nc.allow_non_contiguous_dma(reason="256 sinks, two to a partition"):
+            nc.scalar.dma_start(out=sink_raw[:], in_=sink[0].rearrange("(j m) x -> m (j x)", j=2))
         warm = keep.tile([P, 1], F32, name="warm")
         nc.gpsimd.memset(warm[:], 0.0)
         warmed = keep.tile([P, 1], F32, name="warmed")
@@ -48,8 +49,9 @@ def tile_attend_sink_topk_kernel(tc, qT, kT, vT, vs, sink, offs, out):
             nc.sync.dma_start(out=k_table[t][:], in_=k_rows[:, t, :])
             if t == 0:
                 nc.sync.dma_start(offsets[:], offs)
-        q_raw = keep.tile([P, PACK, NQ], F32, name="q_raw")
-        nc.sync.dma_start(out=q_raw[:], in_=qT[0].rearrange("(p t) q -> p t q", t=PACK))
+        q_raw = [keep.tile([P, PACK, P], F32, name=f"q_raw{j}") for j in range(2)]
+        for j in range(2):
+            nc.sync.dma_start(out=q_raw[j][:], in_=qT[0].rearrange("(p t) q -> p t q", t=PACK)[:, :, j * P : (j + 1) * P])
         v_table = keep.tile([P, T], F32, name="v_table")
         nc.sync.dma_start(out=v_table[:], in_=vT)
 
@@ -98,59 +100,54 @@ def tile_attend_sink_topk_kernel(tc, qT, kT, vT, vs, sink, offs, out):
             nc.vector.tensor_copy(k_grouped[1][:, :, t], k_table[t][:].indirect(offsets[:, HALF // 16 : N // 16]))
         nc.scalar.activation(out=k_grouped[0][:, :, 2:4], in_=k_high[:].rearrange("p t n -> p n t"), func=ACT.Copy)
 
-        q_grouped = keep.tile([P, NQ, PACK], BF16, name="q_grouped", align_bytes=64)
+        q_grouped = [keep.tile([P, P, PACK], BF16, name=f"q_grouped{j}", align_bytes=64) for j in range(2)]
         nc.gpsimd.tensor_scalar(
-            out=q_grouped[:].rearrange("p (j m) t -> p j m t", j=2),
-            in0=q_raw[:].rearrange("p t (m j) -> p j m t", j=2),
-            scalar1=-1.0,
-            scalar2=0.0,
-            op0=ALU.mult,
-            op1=ALU.add,
+            out=q_grouped[0][:], in0=q_raw[0][:].rearrange("p t m -> p m t"), scalar1=-1.0, scalar2=0.0, op0=ALU.mult, op1=ALU.add
         )
-        q_codes = keep.tile([P, NQ], U32, name="q_codes", align_bytes=64)
-        q_scales = keep.tile([P, NQ], U8, name="q_scales", align_bytes=64)
-
-        k_codes = keep.tile([P, N], U32, name="k_codes", align_bytes=64)
-        k_scales = keep.tile([P, N], U8, name="k_scales", align_bytes=64)
-        scores = {}
-        for h in (1, 0):
-            cols = slice(h * HALF, (h + 1) * HALF)
+        nc.scalar.activation(out=q_grouped[1][:], in_=q_raw[1][:].rearrange("p t m -> p m t"), func=ACT.Copy, scale=-1.0)
+        q_codes = [keep.tile([P, P], U32, name=f"q_codes{j}", align_bytes=64) for j in range(2)]
+        q_scales = [keep.tile([P, P], U8, name=f"q_scales{j}", align_bytes=64) for j in range(2)]
+        k_scales = [keep.tile([P, HALF], U8, name=f"k_scales{h}", align_bytes=64) for h in range(2)]
+        k_codes = {}
+        for h, j in ((1, 0), (0, 1)):
+            k_codes[h] = keep.tile([P, HALF], U32, name=f"k_codes{h}", align_bytes=64)
             nc.vector.quantize_mx(
-                out=k_codes[:, cols].bitcast(FP8X4),
-                scales=k_scales[:, cols],
-                in_=k_grouped[h][:].rearrange("p n t -> p (n t)"),
+                out=k_codes[h][:].bitcast(FP8X4), scales=k_scales[h][:], in_=k_grouped[h][:].rearrange("p n t -> p (n t)")
             )
-            if h == 1:
-                nc.vector.quantize_mx(
-                    out=q_codes[:].bitcast(FP8X4), scales=q_scales[:], in_=q_grouped[:].rearrange("p n t -> p (n t)")
-                )
-            for j in range(2):
-                queries = slice(j * P, (j + 1) * P)
+            nc.vector.quantize_mx(
+                out=q_codes[j][:].bitcast(FP8X4), scales=q_scales[j][:], in_=q_grouped[j][:].rearrange("p n t -> p (n t)")
+            )
+        scores = {}
+        for j in range(2):
+            for h in (1, 0):
                 scores[j, h] = score_banks.tile([P, HALF], F32, name="score")
                 nc.tensor.matmul_mx(
                     out=scores[j, h][:],
-                    lhsT=q_codes[:, queries].bitcast(FP8X4),
-                    lhsT_scale=q_scales[:, queries],
-                    rhs=k_codes[:, cols].bitcast(FP8X4),
-                    rhs_scale=k_scales[:, cols],
+                    lhsT=q_codes[j][:].bitcast(FP8X4),
+                    lhsT_scale=q_scales[j][:],
+                    rhs=k_codes[h][:].bitcast(FP8X4),
+                    rhs_scale=k_scales[h][:],
                     start=True,
                     stop=True,
                 )
 
         low = {}
-        for h in (1, 0):
-            for j in range(2):
+        for j in range(2):
+            for h in (1, 0):
                 unused = keep.tile([P, HALF], F32, name=f"unused{j}{h}")
                 low[j, h] = keep.tile([P, 1], F32, name=f"low{j}{h}")
                 nc.vector.tensor_scalar(
                     out=unused[:],
                     in0=scores[j, h][:],
                     scalar1=1.0,
-                    scalar2=nsink[:, j : j + 1] if h == 1 else low[j, 1][:],
+                    scalar2=low[1, 1][:] if (j, h) == (1, 0) else nsink[:, j : j + 1],
                     op0=ALU.mult,
                     op1=ALU.min,
                     accum_out=low[j, h][:],
                 )
+        joined = keep.tile([P, 1], F32, name="joined")
+        nc.gpsimd.tensor_scalar(out=joined[:], in0=low[0, 0][:], scalar1=low[0, 1][:], scalar2=0.0, op0=ALU.min, op1=ALU.add)
+        lowest = [joined, low[1, 0]]
 
         v_picked = [keep.tile([P, HALF], BF16, name=f"v_picked{g}") for g in range(2)]
         for g in range(2):
@@ -174,11 +171,13 @@ def tile_attend_sink_topk_kernel(tc, qT, kT, vT, vs, sink, offs, out):
                     out=laid,
                     in_=read,
                     func=ACT.Exp,
-                    bias=low[j, 0][:],
+                    bias=lowest[j][:],
                     scale=-1.0,
                     accum_out=sums[:, j, h : h + 1],
                 )
 
+        for j in range(2):
+            nc.scalar.activation(out=sums[:, j, 2:3], in_=nsink[:, j : j + 1], func=ACT.Exp, bias=lowest[j][:], scale=-1.0)
         parts = [(1, g) for g in range(2)]
         w_grouped = {(j, g): keep.tile([P, P, PACK], BF16, name=f"w_grouped{j}{g}", align_bytes=64) for j, g in parts}
         w_codes = {(j, g): keep.tile([P, P], U32, name=f"w_codes{j}{g}", align_bytes=64) for j, g in parts}
@@ -213,21 +212,17 @@ def tile_attend_sink_topk_kernel(tc, qT, kT, vT, vs, sink, offs, out):
                 out=wv_grouped[g][:].rearrange("p a e t -> p (a e t)").bitcast(F32).rearrange("p (a e u) -> p a e u", a=2, u=2),
                 in_=words[:].rearrange("p a u e -> p a e u"),
             )
-        for j in range(2):
-            nc.scalar.activation(out=sums[:, j, 2:3], in_=nsink[:, j : j + 1], func=ACT.Exp, bias=low[j, 0][:], scale=-1.0)
         for g in range(2):
             nc.vector.quantize_mx(
                 out=w_codes[1, g][:].bitcast(FP8X4), scales=w_scales[1, g][:], in_=w_grouped[1, g][:].rearrange("p q t -> p (q t)")
             )
-            if g == 0:
-                nc.vector.tensor_reduce(out=total[:], in_=sums[:], axis=AX.X, op=ALU.add)
             nc.vector.quantize_mx(
                 out=wv_codes[g][:].rearrange("p a e -> p (a e)").bitcast(FP8X4),
                 scales=wv_scales[g][:].rearrange("p a e -> p (a e)"),
                 in_=wv_grouped[g][:].rearrange("p a e t -> p (a e t)"),
             )
-            if g == 0:
-                nc.vector.reciprocal(share[:], total[:])
+        nc.vector.tensor_reduce(out=total[:], in_=sums[:], axis=AX.X, op=ALU.add)
+        nc.vector.reciprocal(share[:], total[:])
         for j in (1, 0):
             acc = score_banks.tile([P, DV], F32, name="score")
             for g in range(2):
@@ -242,4 +237,4 @@ def tile_attend_sink_topk_kernel(tc, qT, kT, vT, vs, sink, offs, out):
                 )
             result = keep.tile([P, DV], F32, name=f"result{j}")
             nc.scalar.activation(out=result[:], in_=acc[:], func=ACT.Copy, scale=share[:, j : j + 1])
-            nc.sync.dma_start(out=out[0].rearrange("(m j) e -> m j e", j=2)[:, j, :], in_=result[:])
+            nc.sync.dma_start(out=out[0][j * P : (j + 1) * P, :], in_=result[:])

@@ -45,10 +45,13 @@ def tile_attend_sink_topk_kernel(tc, qT, kT, vT, vs, sink, offs, out):
 
         k_rows = kT.rearrange("(p t) c -> p t c", t=PACK)
         k_table = [keep.tile([P, T], F32, name=f"k_table{t}") for t in range(PACK)]
-        for t in range(PACK):
+        for t in range(PACK - 1):
             nc.sync.dma_start(out=k_table[t][:], in_=k_rows[:, t, :])
             if t == 0:
                 nc.sync.dma_start(offsets[:], offs)
+        pieces = [slice(0, 1536), slice(1536, 3072), slice(3072, 3840), slice(3840, T)]
+        for piece in pieces:
+            nc.sync.dma_start(out=k_table[3][:, piece], in_=k_rows[:, 3, piece])
         q_raw = [keep.tile([P, PACK, P], F32, name=f"q_raw{j}") for j in range(2)]
         for j in range(2):
             nc.sync.dma_start(out=q_raw[j][:], in_=qT[0].rearrange("(p t) q -> p t q", t=PACK)[:, :, j * P : (j + 1) * P])
@@ -73,7 +76,6 @@ def tile_attend_sink_topk_kernel(tc, qT, kT, vT, vs, sink, offs, out):
 
         k_grouped = [keep.tile([P, HALF, PACK], BF16, name=f"k_grouped{h}", align_bytes=64) for h in range(2)]
         k_low = keep.tile([P, 2, N], F32, name="k_low")
-        k_high = keep.tile([P, 2, HALF], F32, name="k_high")
         nc.vector.tensor_copy(k_low[:, 0, :], k_table[0][:].indirect(offsets[:]))
 
         vs_picked = keep.tile([P, N], F32, name="vs_picked")
@@ -86,8 +88,13 @@ def tile_attend_sink_topk_kernel(tc, qT, kT, vT, vs, sink, offs, out):
             nc.scalar.copy(out=vcol[:, g * PACK : (g + 1) * PACK], in_=turned[:, :, 0])
         vs_rows = [keep.tile([P, 2, P, 2], F32, name=f"vs_rows{g}") for g in range(2)]
         for g in range(2):
-            nc.scalar.copy(
-                out=vs_rows[g][:], in_=vs_picked[:, g * HALF : (g + 1) * HALF].rearrange("r (s u w) -> r u s w", u=2, w=2)
+            nc.gpsimd.tensor_scalar(
+                out=vs_rows[g][:],
+                in0=vs_picked[:, g * HALF : (g + 1) * HALF].rearrange("r (s u w) -> r u s w", u=2, w=2),
+                scalar1=1.0,
+                scalar2=0.0,
+                op0=ALU.mult,
+                op1=ALU.add,
             )
 
         nc.vector.tensor_copy(k_low[:, 1, :], k_table[1][:].indirect(offsets[:]))
@@ -95,10 +102,15 @@ def tile_attend_sink_topk_kernel(tc, qT, kT, vT, vs, sink, offs, out):
             nc.scalar.activation(
                 out=k_grouped[h][:, :, 0:2], in_=k_low[:, :, h * HALF : (h + 1) * HALF].rearrange("p t n -> p n t"), func=ACT.Copy
             )
-        for t in (2, 3):
-            nc.vector.tensor_copy(k_high[:, t - 2, :], k_table[t][:].indirect(offsets[:, 0 : HALF // 16]))
-            nc.vector.tensor_copy(k_grouped[1][:, :, t], k_table[t][:].indirect(offsets[:, HALF // 16 : N // 16]))
-        nc.scalar.activation(out=k_grouped[0][:, :, 2:4], in_=k_high[:].rearrange("p t n -> p n t"), func=ACT.Copy)
+        for h in range(2):
+            nc.vector.tensor_copy(k_grouped[h][:, :, 2], k_table[2][:].indirect(offsets[:, h * (HALF // 16) : (h + 1) * (HALF // 16)]))
+        k_last = keep.tile([P, T], BF16, name="k_last")
+        nc.scalar.activation(out=k_last[:, pieces[0]], in_=k_table[3][:, pieces[0]], func=ACT.Copy)
+        for piece in pieces[1:3]:
+            nc.vector.tensor_copy(k_last[:, piece], k_table[3][:, piece])
+        nc.scalar.activation(out=k_last[:, pieces[3]], in_=k_table[3][:, pieces[3]], func=ACT.Copy)
+        nc.vector.tensor_copy(k_grouped[1][:, :, 3], k_table[3][:].indirect(offsets[:, HALF // 16 : N // 16]))
+        nc.scalar.activation(out=k_grouped[0][:, :, 3], in_=k_last[:].indirect(offsets[:, 0 : HALF // 16]), func=ACT.Copy)
 
         q_grouped = [keep.tile([P, P, PACK], BF16, name=f"q_grouped{j}", align_bytes=64) for j in range(2)]
         nc.gpsimd.tensor_scalar(
@@ -188,6 +200,8 @@ def tile_attend_sink_topk_kernel(tc, qT, kT, vT, vs, sink, offs, out):
         total = keep.tile([P, 2], F32, name="total")
         share = keep.tile([P, 2], F32, name="share")
 
+        nc.vector.tensor_reduce(out=total[:], in_=sums[:], axis=AX.X, op=ALU.add)
+        nc.vector.reciprocal(share[:], total[:])
         w_pairs = [keep.tile([P, HALF], BF16, name=f"w_pairs{g}") for g in range(2)]
         for g in range(2):
             nc.gpsimd.tensor_tensor(
@@ -221,8 +235,6 @@ def tile_attend_sink_topk_kernel(tc, qT, kT, vT, vs, sink, offs, out):
                 scales=wv_scales[g][:].rearrange("p a e -> p (a e)"),
                 in_=wv_grouped[g][:].rearrange("p a e t -> p (a e t)"),
             )
-        nc.vector.tensor_reduce(out=total[:], in_=sums[:], axis=AX.X, op=ALU.add)
-        nc.vector.reciprocal(share[:], total[:])
         for j in (1, 0):
             acc = score_banks.tile([P, DV], F32, name="score")
             for g in range(2):

@@ -98,7 +98,7 @@ def tile_attend_sink_topk_kernel(tc, qT, kT, vT, vs, sink, offs, out):
             )
 
         nc.vector.tensor_copy(k_low[:, 1, :], k_table[1][:].indirect(offsets[:]))
-        for h in (1, 0):
+        for h in range(2):
             nc.scalar.activation(
                 out=k_grouped[h][:, :, 0:2], in_=k_low[:, :, h * HALF : (h + 1) * HALF].rearrange("p t n -> p n t"), func=ACT.Copy
             )

@@ -81,7 +81,7 @@ def tile_attend_sink_topk_kernel(tc, qT, kT, vT, vs, sink, offs, out):
         vs_picked = keep.tile([P, N], F32, name="vs_picked")
         nc.vector.tensor_copy(vs_picked[:], vs_table[:].indirect(offsets[:]))
         vcol = keep.tile([P, 2 * PACK], F32, name="vcol")
-        for g in range(2):
+        for g in (1,):
             turned = turn_banks.tile([P, PACK, P], F32, name="turned")
             for t in range(PACK):
                 nc.tensor.transpose(turned[:, t, :], vs_picked[:, g * HALF + t : (g + 1) * HALF : PACK], ident[:])
@@ -173,7 +173,7 @@ def tile_attend_sink_topk_kernel(tc, qT, kT, vT, vs, sink, offs, out):
         for j in range(2):
             for h in range(2):
                 probs[j, h] = keep.tile([P, PACK, P], F32, name=f"probs{j}{h}")
-                if j == 0:
+                if (j, h) != (1, 1):
                     laid = probs[j, h][:].rearrange("p t s -> p (t s)").rearrange("p (u s w) -> p u s w", u=2, w=2)
                     read = scores[j, h][:].rearrange("p (s u w) -> p u s w", u=2, w=2)
                 else:
@@ -202,50 +202,68 @@ def tile_attend_sink_topk_kernel(tc, qT, kT, vT, vs, sink, offs, out):
 
         nc.vector.tensor_reduce(out=total[:], in_=sums[:], axis=AX.X, op=ALU.add)
         nc.vector.reciprocal(share[:], total[:])
-        w_pairs = [keep.tile([P, HALF], BF16, name=f"w_pairs{g}") for g in range(2)]
-        for g in range(2):
+        early = [(0, 0), (0, 1), (1, 0)]
+        w_pairs = {(j, g): keep.tile([P, HALF], BF16, name=f"w_pairs{j}{g}") for j, g in early}
+        for j, g in early:
             nc.gpsimd.tensor_tensor(
-                w_pairs[g][:], probs[0, g][:].rearrange("p t s -> p (t s)"), vs_rows[g][:].rearrange("p u s w -> p (u s w)"), ALU.mult
+                w_pairs[j, g][:], probs[j, g][:].rearrange("p t s -> p (t s)"), vs_rows[g][:].rearrange("p u s w -> p (u s w)"), ALU.mult
             )
         for g in range(2):
-            turned = turn_banks.tile([P, PACK, P], F32, name="turned")
-            for t in range(PACK):
-                nc.tensor.transpose(turned[:, t, :], probs[1, g][:, t, :], ident[:])
-            nc.vector.tensor_tensor(
-                w_grouped[1, g][:],
-                turned[:].rearrange("p t q -> p q t"),
-                vcol[:, g * PACK : (g + 1) * PACK].unsqueeze(1).to_broadcast([P, P, PACK]),
-                ALU.mult,
-            )
+            if g == 1:
+                turned = turn_banks.tile([P, PACK, P], F32, name="turned")
+                for t in range(PACK):
+                    nc.tensor.transpose(turned[:, t, :], probs[1, g][:, t, :], ident[:])
+                nc.vector.tensor_tensor(
+                    w_grouped[1, g][:],
+                    turned[:].rearrange("p t q -> p q t"),
+                    vcol[:, g * PACK : (g + 1) * PACK].unsqueeze(1).to_broadcast([P, P, PACK]),
+                    ALU.mult,
+                )
             words = turn_banks.tile([P, 2, 2, P], F32, name="turned")
             for u in range(2):
-                nc.tensor.transpose(words[:, 0, u, :], w_pairs[g][:].bitcast(F32)[:, u * P : (u + 1) * P], ident[:])
+                nc.tensor.transpose(words[:, 0, u, :], w_pairs[0, g][:].bitcast(F32)[:, u * P : (u + 1) * P], ident[:])
             for u in range(2):
                 nc.tensor.transpose(words[:, 1, u, :], v_picked[g][:].bitcast(F32)[:, u : 2 * P : 2], ident[:])
             nc.scalar.copy(
                 out=wv_grouped[g][:].rearrange("p a e t -> p (a e t)").bitcast(F32).rearrange("p (a e u) -> p a e u", a=2, u=2),
                 in_=words[:].rearrange("p a u e -> p a e u"),
             )
-        for g in range(2):
+        words = turn_banks.tile([P, 2, P], F32, name="turned")
+        for u in range(2):
+            nc.tensor.transpose(words[:, u, :], w_pairs[1, 0][:].bitcast(F32)[:, u * P : (u + 1) * P], ident[:])
+        nc.scalar.copy(
+            out=w_grouped[1, 0][:].rearrange("p q t -> p (q t)").bitcast(F32).rearrange("p (q u) -> p q u", u=2),
+            in_=words[:].rearrange("p u q -> p q u"),
+        )
+
+        def quantise_w(g):
             nc.vector.quantize_mx(
                 out=w_codes[1, g][:].bitcast(FP8X4), scales=w_scales[1, g][:], in_=w_grouped[1, g][:].rearrange("p q t -> p (q t)")
             )
+
+        def quantise_wv(g):
             nc.vector.quantize_mx(
                 out=wv_codes[g][:].rearrange("p a e -> p (a e)").bitcast(FP8X4),
                 scales=wv_scales[g][:].rearrange("p a e -> p (a e)"),
                 in_=wv_grouped[g][:].rearrange("p a e t -> p (a e t)"),
             )
-        for j in (1, 0):
+
+        quantise_wv(0)
+        quantise_w(1)
+        quantise_wv(1)
+        quantise_w(0)
+        for j in range(2):
             acc = score_banks.tile([P, DV], F32, name="score")
-            for g in range(2):
+            order = (1, 0) if j else (0, 1)
+            for g in order:
                 nc.tensor.matmul_mx(
                     out=acc[:],
                     lhsT=(w_codes[j, g][:] if j else wv_codes[g][:, 0, :]).bitcast(FP8X4),
                     lhsT_scale=w_scales[j, g][:] if j else wv_scales[g][:, 0, :],
                     rhs=wv_codes[g][:, 1, :].bitcast(FP8X4),
                     rhs_scale=wv_scales[g][:, 1, :],
-                    start=(g == 0),
-                    stop=(g == 1),
+                    start=(g == order[0]),
+                    stop=(g == order[1]),
                 )
             result = keep.tile([P, DV], F32, name=f"result{j}")
             nc.scalar.activation(out=result[:], in_=acc[:], func=ACT.Copy, scale=share[:, j : j + 1])

@@ -28,20 +28,20 @@ def tile_attend_sink_topk_kernel(tc, qT, kT, vT, vs, sink, offs, out):
     with ExitStack() as ctx:
         lists = ctx.enter_context(tc.tile_pool(name="lists", bufs=1))
         keep = ctx.enter_context(tc.tile_pool(name="keep", bufs=1))
-        score_banks = ctx.enter_context(tc.psum_pool(name="score_banks", bufs=4))
+        score_banks = ctx.enter_context(tc.psum_pool(name="score_banks", bufs=1))
         turn_banks = ctx.enter_context(tc.psum_pool(name="turn_banks", bufs=4))
 
         offsets = lists.tile([P, N // 16], U16, name="offsets")
         RUN = T // P
         vs_runs = keep.tile([P, RUN], F32, name="vs_runs")
         nc.sync.dma_start(out=vs_runs[:], in_=vs[0].rearrange("(p c) -> p c", c=RUN))
-        sink_raw = keep.tile([P, 2], F32, name="sink_raw")
-        with nc.allow_non_contiguous_dma(reason="256 sinks, two to a partition"):
-            nc.scalar.dma_start(out=sink_raw[:], in_=sink[0].rearrange("(j m) x -> m (j x)", j=2))
         warm = keep.tile([P, 1], F32, name="warm")
         nc.gpsimd.memset(warm[:], 0.0)
         warmed = keep.tile([P, 1], F32, name="warmed")
         nc.scalar.activation(out=warmed[:], in_=warm[:], func=ACT.Exp)
+        sink_rows = keep.tile([P, P], F32, name="sink_rows")
+        nc.gpsimd.memset(sink_rows[:], 0.0)
+        nc.scalar.dma_start(out=sink_rows[0:2, :], in_=sink[0].rearrange("(j m) x -> j (m x)", j=2))
 
         k_rows = kT.rearrange("(p t) c -> p t c", t=PACK)
         k_table = [keep.tile([P, T], F32, name=f"k_table{t}") for t in range(PACK)]
@@ -62,7 +62,6 @@ def tile_attend_sink_topk_kernel(tc, qT, kT, vT, vs, sink, offs, out):
         make_identity(nc, ident[:])
 
         nsink = keep.tile([P, 2], F32, name="nsink")
-        nc.scalar.activation(out=nsink[:], in_=sink_raw[:], func=ACT.Copy, scale=-1.0)
 
         vs_table = keep.tile([P, T], F32, name="vs_table")
         for b in range(RUN // PACK):
@@ -74,6 +73,10 @@ def tile_attend_sink_topk_kernel(tc, qT, kT, vT, vs, sink, offs, out):
                 in_=turned[:].rearrange("r c p -> r p c"),
             )
 
+        turned = turn_banks.tile([P, P], F32, name="turned")
+        nc.tensor.transpose(turned[:], sink_rows[:], ident[:])
+        nc.scalar.activation(out=nsink[:], in_=turned[:, 0:2], func=ACT.Copy, scale=-1.0)
+
         k_grouped = [keep.tile([P, HALF, PACK], BF16, name=f"k_grouped{h}", align_bytes=64) for h in range(2)]
         k_low = keep.tile([P, 2, N], F32, name="k_low")
         nc.vector.tensor_copy(k_low[:, 0, :], k_table[0][:].indirect(offsets[:]))
@@ -81,7 +84,7 @@ def tile_attend_sink_topk_kernel(tc, qT, kT, vT, vs, sink, offs, out):
         vs_picked = keep.tile([P, N], F32, name="vs_picked")
         nc.vector.tensor_copy(vs_picked[:], vs_table[:].indirect(offsets[:]))
         vcol = keep.tile([P, 2 * PACK], F32, name="vcol")
-        for g in (1,):
+        for g in range(2):
             turned = turn_banks.tile([P, PACK, P], F32, name="turned")
             for t in range(PACK):
                 nc.tensor.transpose(turned[:, t, :], vs_picked[:, g * HALF + t : (g + 1) * HALF : PACK], ident[:])
@@ -132,7 +135,7 @@ def tile_attend_sink_topk_kernel(tc, qT, kT, vT, vs, sink, offs, out):
         scores = {}
         for j in range(2):
             for h in (1, 0):
-                scores[j, h] = score_banks.tile([P, HALF], F32, name="score")
+                scores[j, h] = score_banks.tile([P, HALF], F32, name=f"score{j}{h}")
                 nc.tensor.matmul_mx(
                     out=scores[j, h][:],
                     lhsT=q_codes[j][:].bitcast(FP8X4),
@@ -203,11 +206,24 @@ def tile_attend_sink_topk_kernel(tc, qT, kT, vT, vs, sink, offs, out):
         nc.vector.tensor_reduce(out=total[:], in_=sums[:], axis=AX.X, op=ALU.add)
         nc.vector.reciprocal(share[:], total[:])
         early = [(0, 0), (0, 1), (1, 0)]
-        w_pairs = {(j, g): keep.tile([P, HALF], BF16, name=f"w_pairs{j}{g}") for j, g in early}
+        widths = {(0, 0): HALF, (0, 1): HALF, (1, 0): HALF // 2}
+        w_pairs = {(j, g): keep.tile([P, widths[j, g]], BF16, name=f"w_pairs{j}{g}") for j, g in early}
         for j, g in early:
             nc.gpsimd.tensor_tensor(
-                w_pairs[j, g][:], probs[j, g][:].rearrange("p t s -> p (t s)"), vs_rows[g][:].rearrange("p u s w -> p (u s w)"), ALU.mult
+                w_pairs[j, g][:],
+                probs[j, g][:].rearrange("p t s -> p (t s)")[:, 0 : widths[j, g]],
+                vs_rows[g][:].rearrange("p u s w -> p (u s w)")[:, 0 : widths[j, g]],
+                ALU.mult,
             )
+        turned = score_banks.tile([P, 2, P], F32, name="score10")
+        for w in range(2):
+            nc.tensor.transpose(turned[:, w, :], probs[1, 0][:].rearrange("p t s -> p (t s)")[:, HALF // 2 + w : HALF : 2], ident[:])
+        nc.vector.tensor_tensor(
+            w_grouped[1, 0][:, :, 2:4],
+            turned[:].rearrange("p w q -> p q w"),
+            vcol[:, 2:4].unsqueeze(1).to_broadcast([P, P, 2]),
+            ALU.mult,
+        )
         for g in range(2):
             if g == 1:
                 turned = turn_banks.tile([P, PACK, P], F32, name="turned")
@@ -219,21 +235,25 @@ def tile_attend_sink_topk_kernel(tc, qT, kT, vT, vs, sink, offs, out):
                     vcol[:, g * PACK : (g + 1) * PACK].unsqueeze(1).to_broadcast([P, P, PACK]),
                     ALU.mult,
                 )
+            laid = wv_grouped[g][:].rearrange("p a e t -> p (a e t)").bitcast(F32).rearrange("p (a e u) -> p a e u", a=2, u=2)
             words = turn_banks.tile([P, 2, 2, P], F32, name="turned")
             for u in range(2):
                 nc.tensor.transpose(words[:, 0, u, :], w_pairs[0, g][:].bitcast(F32)[:, u * P : (u + 1) * P], ident[:])
-            for u in range(2):
-                nc.tensor.transpose(words[:, 1, u, :], v_picked[g][:].bitcast(F32)[:, u : 2 * P : 2], ident[:])
-            nc.scalar.copy(
-                out=wv_grouped[g][:].rearrange("p a e t -> p (a e t)").bitcast(F32).rearrange("p (a e u) -> p a e u", a=2, u=2),
-                in_=words[:].rearrange("p a u e -> p a e u"),
-            )
-        words = turn_banks.tile([P, 2, P], F32, name="turned")
-        for u in range(2):
-            nc.tensor.transpose(words[:, u, :], w_pairs[1, 0][:].bitcast(F32)[:, u * P : (u + 1) * P], ident[:])
+            if g == 0:
+                for u in range(2):
+                    nc.tensor.transpose(words[:, 1, u, :], v_picked[g][:].bitcast(F32)[:, u : 2 * P : 2], ident[:])
+                nc.scalar.copy(out=laid, in_=words[:].rearrange("p a u e -> p a e u"))
+            else:
+                nc.scalar.copy(out=laid[:, 0, :, :], in_=words[:, 0, :, :].rearrange("p u e -> p e u"))
+                late = score_banks.tile([P, 2, P], F32, name="score11")
+                for u in range(2):
+                    nc.tensor.transpose(late[:, u, :], v_picked[g][:].bitcast(F32)[:, u : 2 * P : 2], ident[:])
+                nc.scalar.copy(out=laid[:, 1, :, :], in_=late[:].rearrange("p u e -> p e u"))
+        words = turn_banks.tile([P, P], F32, name="turned")
+        nc.tensor.transpose(words[:], w_pairs[1, 0][:].bitcast(F32), ident[:])
         nc.scalar.copy(
-            out=w_grouped[1, 0][:].rearrange("p q t -> p (q t)").bitcast(F32).rearrange("p (q u) -> p q u", u=2),
-            in_=words[:].rearrange("p u q -> p q u"),
+            out=w_grouped[1, 0][:].rearrange("p q t -> p (q t)").bitcast(F32).rearrange("p (q u) -> p q u", u=2)[:, :, 0],
+            in_=words[:],
         )
 
         def quantise_w(g):
@@ -253,7 +273,7 @@ def tile_attend_sink_topk_kernel(tc, qT, kT, vT, vs, sink, offs, out):
         quantise_wv(1)
         quantise_w(0)
         for j in range(2):
-            acc = score_banks.tile([P, DV], F32, name="score")
+            acc = score_banks.tile([P, DV], F32, name=f"score0{j}")
             order = (1, 0) if j else (0, 1)
             for g in order:
                 nc.tensor.matmul_mx(

@@ -49,7 +49,7 @@ def tile_attend_sink_topk_kernel(tc, qT, kT, vT, vs, sink, offs, out):
             nc.sync.dma_start(out=k_table[t][:], in_=k_rows[:, t, :])
             if t == 0:
                 nc.sync.dma_start(offsets[:], offs)
-        pieces = [slice(0, 1536), slice(1536, 3072), slice(3072, 3840), slice(3840, T)]
+        pieces = [slice(0, 1536), slice(1536, 3072), slice(3072, 3584), slice(3584, T)]
         for piece in pieces:
             nc.sync.dma_start(out=k_table[3][:, piece], in_=k_rows[:, 3, piece])
         q_raw = [keep.tile([P, PACK, P], F32, name=f"q_raw{j}") for j in range(2)]
@@ -109,9 +109,9 @@ def tile_attend_sink_topk_kernel(tc, qT, kT, vT, vs, sink, offs, out):
             nc.vector.tensor_copy(k_grouped[h][:, :, 2], k_table[2][:].indirect(offsets[:, h * (HALF // 16) : (h + 1) * (HALF // 16)]))
         k_last = keep.tile([P, T], BF16, name="k_last")
         nc.scalar.activation(out=k_last[:, pieces[0]], in_=k_table[3][:, pieces[0]], func=ACT.Copy)
-        for piece in pieces[1:3]:
-            nc.vector.tensor_copy(k_last[:, piece], k_table[3][:, piece])
-        nc.scalar.activation(out=k_last[:, pieces[3]], in_=k_table[3][:, pieces[3]], func=ACT.Copy)
+        nc.vector.tensor_copy(k_last[:, pieces[1]], k_table[3][:, pieces[1]])
+        for piece in pieces[2:4]:
+            nc.scalar.activation(out=k_last[:, piece], in_=k_table[3][:, piece], func=ACT.Copy)
         nc.vector.tensor_copy(k_grouped[1][:, :, 3], k_table[3][:].indirect(offsets[:, HALF // 16 : N // 16]))
         nc.scalar.activation(out=k_grouped[0][:, :, 3], in_=k_last[:].indirect(offsets[:, 0 : HALF // 16]), func=ACT.Copy)
 

@@ -35,10 +35,6 @@ def tile_attend_sink_topk_kernel(tc, qT, kT, vT, vs, sink, offs, out):
         RUN = T // P
         vs_runs = keep.tile([P, RUN], F32, name="vs_runs")
         nc.sync.dma_start(out=vs_runs[:], in_=vs[0].rearrange("(p c) -> p c", c=RUN))
-        warm = keep.tile([P, 1], F32, name="warm")
-        nc.gpsimd.memset(warm[:], 0.0)
-        warmed = keep.tile([P, 1], F32, name="warmed")
-        nc.scalar.activation(out=warmed[:], in_=warm[:], func=ACT.Exp)
         sink_rows = keep.tile([P, P], F32, name="sink_rows")
         nc.gpsimd.memset(sink_rows[:], 0.0)
         nc.scalar.dma_start(out=sink_rows[0:2, :], in_=sink[0].rearrange("(j m) x -> j (m x)", j=2))
@@ -52,7 +48,7 @@ def tile_attend_sink_topk_kernel(tc, qT, kT, vT, vs, sink, offs, out):
         pieces = [slice(0, 1536), slice(1536, 3072), slice(3072, 3584), slice(3584, T)]
         for piece in pieces:
             nc.sync.dma_start(out=k_table[3][:, piece], in_=k_rows[:, 3, piece])
-        q_raw = [keep.tile([P, PACK, P], F32, name=f"q_raw{j}") for j in range(2)]
+        q_raw = [keep.tile([P, PACK, P], F32, name=f"q_raw{j}", align_bytes=64) for j in range(2)]
         for j in range(2):
             nc.sync.dma_start(out=q_raw[j][:], in_=qT[0].rearrange("(p t) q -> p t q", t=PACK)[:, :, j * P : (j + 1) * P])
         v_table = keep.tile([P, T], F32, name="v_table")
@@ -84,11 +80,11 @@ def tile_attend_sink_topk_kernel(tc, qT, kT, vT, vs, sink, offs, out):
         vs_picked = keep.tile([P, N], F32, name="vs_picked")
         nc.vector.tensor_copy(vs_picked[:], vs_table[:].indirect(offsets[:]))
         vcol = keep.tile([P, 2 * PACK], F32, name="vcol")
-        for g in range(2):
+        for g, first in ((0, 2), (1, 0)):
             turned = turn_banks.tile([P, PACK, P], F32, name="turned")
-            for t in range(PACK):
+            for t in range(first, PACK):
                 nc.tensor.transpose(turned[:, t, :], vs_picked[:, g * HALF + t : (g + 1) * HALF : PACK], ident[:])
-            nc.scalar.copy(out=vcol[:, g * PACK : (g + 1) * PACK], in_=turned[:, :, 0])
+            nc.scalar.copy(out=vcol[:, g * PACK + first : (g + 1) * PACK], in_=turned[:, first:PACK, 0])
         vs_rows = [keep.tile([P, 2, P, 2], F32, name=f"vs_rows{g}") for g in range(2)]
         for g in range(2):
             nc.gpsimd.tensor_scalar(
@@ -122,46 +118,56 @@ def tile_attend_sink_topk_kernel(tc, qT, kT, vT, vs, sink, offs, out):
         nc.scalar.activation(out=q_grouped[1][:], in_=q_raw[1][:].rearrange("p t m -> p m t"), func=ACT.Copy, scale=-1.0)
         q_codes = [keep.tile([P, P], U32, name=f"q_codes{j}", align_bytes=64) for j in range(2)]
         q_scales = [keep.tile([P, P], U8, name=f"q_scales{j}", align_bytes=64) for j in range(2)]
-        k_scales = [keep.tile([P, HALF], U8, name=f"k_scales{h}", align_bytes=64) for h in range(2)]
-        k_codes = {}
-        for h, j in ((1, 0), (0, 1)):
-            k_codes[h] = keep.tile([P, HALF], U32, name=f"k_codes{h}", align_bytes=64)
-            nc.vector.quantize_mx(
-                out=k_codes[h][:].bitcast(FP8X4), scales=k_scales[h][:], in_=k_grouped[h][:].rearrange("p n t -> p (n t)")
-            )
+        k_scales = keep.tile([P, 2, HALF], U8, name="q_raw0", align_bytes=64)
+        k_codes = [keep.tile([P, HALF], U32, name=f"k_codes{h}", align_bytes=64) for h in range(2)]
+        QUARTER = HALF // 2
+
+        def quantise_q(j):
             nc.vector.quantize_mx(
                 out=q_codes[j][:].bitcast(FP8X4), scales=q_scales[j][:], in_=q_grouped[j][:].rearrange("p n t -> p (n t)")
             )
+
+        quantise_q(0)
+        for h in (1, 0):
+            for c in range(2):
+                cols = slice(c * QUARTER, (c + 1) * QUARTER)
+                nc.vector.quantize_mx(
+                    out=k_codes[h][:, cols].bitcast(FP8X4),
+                    scales=k_scales[:, h, cols],
+                    in_=k_grouped[h][:, cols, :].rearrange("p n t -> p (n t)"),
+                )
+        quantise_q(1)
         scores = {}
         for j in range(2):
             for h in (1, 0):
                 scores[j, h] = score_banks.tile([P, HALF], F32, name=f"score{j}{h}")
-                nc.tensor.matmul_mx(
-                    out=scores[j, h][:],
-                    lhsT=q_codes[j][:].bitcast(FP8X4),
-                    lhsT_scale=q_scales[j][:],
-                    rhs=k_codes[h][:].bitcast(FP8X4),
-                    rhs_scale=k_scales[h][:],
-                    start=True,
-                    stop=True,
-                )
+                for cols in ([slice(0, HALF)] if j else [slice(0, QUARTER), slice(QUARTER, HALF)]):
+                    nc.tensor.matmul_mx(
+                        out=scores[j, h][:, cols],
+                        lhsT=q_codes[j][:].bitcast(FP8X4),
+                        lhsT_scale=q_scales[j][:],
+                        rhs=k_codes[h][:, cols].bitcast(FP8X4),
+                        rhs_scale=k_scales[:, h, cols],
+                        start=True,
+                        stop=True,
+                    )
 
-        low = {}
-        for j in range(2):
-            for h in (1, 0):
-                unused = keep.tile([P, HALF], F32, name=f"unused{j}{h}")
-                low[j, h] = keep.tile([P, 1], F32, name=f"low{j}{h}")
-                nc.vector.tensor_scalar(
-                    out=unused[:],
-                    in0=scores[j, h][:],
-                    scalar1=1.0,
-                    scalar2=low[1, 1][:] if (j, h) == (1, 0) else nsink[:, j : j + 1],
-                    op0=ALU.mult,
-                    op1=ALU.min,
-                    accum_out=low[j, h][:],
-                )
+        low = {(j, h): keep.tile([P, 1], F32, name=f"low{j}{h}") for j in range(2) for h in range(2)}
+        for h in (1, 0):
+            nc.vector.tensor_reduce(out=low[0, h][:], in_=scores[0, h][:], axis=AX.X, op=ALU.min)
+        for h in (1, 0):
+            unused = keep.tile([P, HALF], F32, name=f"unused{h}")
+            nc.vector.tensor_scalar(
+                out=unused[:],
+                in0=scores[1, h][:],
+                scalar1=1.0,
+                scalar2=nsink[:, 1:2] if h else low[1, 1][:],
+                op0=ALU.mult,
+                op1=ALU.min,
+                accum_out=low[1, h][:],
+            )
         joined = keep.tile([P, 1], F32, name="joined")
-        nc.gpsimd.tensor_scalar(out=joined[:], in0=low[0, 0][:], scalar1=low[0, 1][:], scalar2=0.0, op0=ALU.min, op1=ALU.add)
+        nc.gpsimd.tensor_scalar(out=joined[:], in0=low[0, 0][:], scalar1=low[0, 1][:], scalar2=nsink[:, 0:1], op0=ALU.min, op1=ALU.min)
         lowest = [joined, low[1, 0]]
 
         v_picked = [keep.tile([P, HALF], BF16, name=f"v_picked{g}") for g in range(2)]

@@ -48,9 +48,8 @@ def tile_attend_sink_topk_kernel(tc, qT, kT, vT, vs, sink, offs, out):
         pieces = [slice(0, 1536), slice(1536, 3072), slice(3072, 3584), slice(3584, T)]
         for piece in pieces:
             nc.sync.dma_start(out=k_table[3][:, piece], in_=k_rows[:, 3, piece])
-        q_raw = [keep.tile([P, PACK, P], F32, name=f"q_raw{j}", align_bytes=64) for j in range(2)]
-        for j in range(2):
-            nc.sync.dma_start(out=q_raw[j][:], in_=qT[0].rearrange("(p t) q -> p t q", t=PACK)[:, :, j * P : (j + 1) * P])
+        q_raw = keep.tile([P, PACK, NQ], F32, name="q_raw")
+        nc.sync.dma_start(out=q_raw[:], in_=qT[0].rearrange("(p t) q -> p t q", t=PACK))
         v_table = keep.tile([P, T], F32, name="v_table")
         nc.sync.dma_start(out=v_table[:], in_=vT)
 
@@ -112,13 +111,21 @@ def tile_attend_sink_topk_kernel(tc, qT, kT, vT, vs, sink, offs, out):
         nc.scalar.activation(out=k_grouped[0][:, :, 3], in_=k_last[:].indirect(offsets[:, 0 : HALF // 16]), func=ACT.Copy)
 
         q_grouped = [keep.tile([P, P, PACK], BF16, name=f"q_grouped{j}", align_bytes=64) for j in range(2)]
+        signs = keep.tile([P, 2], F32, name="signs", align_bytes=64)
+        nc.gpsimd.memset(signs[:, 0:1], -1.0)
+        nc.gpsimd.memset(signs[:, 1:2], 0.0)
         nc.gpsimd.tensor_scalar(
-            out=q_grouped[0][:], in0=q_raw[0][:].rearrange("p t m -> p m t"), scalar1=-1.0, scalar2=0.0, op0=ALU.mult, op1=ALU.add
+            out=q_grouped[0][:],
+            in0=q_raw[:, :, 0:P].rearrange("p t m -> p m t"),
+            scalar1=signs[:, 0:1],
+            scalar2=signs[:, 1:2],
+            op0=ALU.mult,
+            op1=ALU.add,
         )
-        nc.scalar.activation(out=q_grouped[1][:], in_=q_raw[1][:].rearrange("p t m -> p m t"), func=ACT.Copy, scale=-1.0)
+        nc.scalar.activation(out=q_grouped[1][:], in_=q_raw[:, :, P:NQ].rearrange("p t m -> p m t"), func=ACT.Copy, scale=-1.0)
         q_codes = [keep.tile([P, P], U32, name=f"q_codes{j}", align_bytes=64) for j in range(2)]
         q_scales = [keep.tile([P, P], U8, name=f"q_scales{j}", align_bytes=64) for j in range(2)]
-        k_scales = keep.tile([P, 2, HALF], U8, name="q_raw0", align_bytes=64)
+        k_scales = keep.tile([P, 2, HALF], U8, name="signs", align_bytes=64)
         k_codes = [keep.tile([P, HALF], U32, name=f"k_codes{h}", align_bytes=64) for h in range(2)]
         QUARTER = HALF // 2
 

@@ -49,7 +49,8 @@ def tile_attend_sink_topk_kernel(tc, qT, kT, vT, vs, sink, offs, out):
         for piece in pieces:
             nc.sync.dma_start(out=k_table[3][:, piece], in_=k_rows[:, 3, piece])
         q_raw = keep.tile([P, PACK, NQ], F32, name="q_raw")
-        nc.sync.dma_start(out=q_raw[:], in_=qT[0].rearrange("(p t) q -> p t q", t=PACK))
+        for u in range(2):
+            nc.sync.dma_start(out=q_raw[:, 2 * u : 2 * u + 2, :], in_=qT[0].rearrange("(p t) q -> p t q", t=PACK)[:, 2 * u : 2 * u + 2, :])
         v_table = keep.tile([P, T], F32, name="v_table")
         nc.sync.dma_start(out=v_table[:], in_=vT)
 
@@ -114,14 +115,15 @@ def tile_attend_sink_topk_kernel(tc, qT, kT, vT, vs, sink, offs, out):
         signs = keep.tile([P, 2], F32, name="signs", align_bytes=64)
         nc.gpsimd.memset(signs[:, 0:1], -1.0)
         nc.gpsimd.memset(signs[:, 1:2], 0.0)
-        nc.gpsimd.tensor_scalar(
-            out=q_grouped[0][:],
-            in0=q_raw[:, :, 0:P].rearrange("p t m -> p m t"),
-            scalar1=signs[:, 0:1],
-            scalar2=signs[:, 1:2],
-            op0=ALU.mult,
-            op1=ALU.add,
-        )
+        for u in range(2):
+            nc.gpsimd.tensor_scalar(
+                out=q_grouped[0][:, :, 2 * u : 2 * u + 2],
+                in0=q_raw[:, 2 * u : 2 * u + 2, 0:P].rearrange("p t m -> p m t"),
+                scalar1=signs[:, 0:1],
+                scalar2=signs[:, 1:2],
+                op0=ALU.mult,
+                op1=ALU.add,
+            )
         nc.scalar.activation(out=q_grouped[1][:], in_=q_raw[:, :, P:NQ].rearrange("p t m -> p m t"), func=ACT.Copy, scale=-1.0)
         q_codes = [keep.tile([P, P], U32, name=f"q_codes{j}", align_bytes=64) for j in range(2)]
         q_scales = [keep.tile([P, P], U8, name=f"q_scales{j}", align_bytes=64) for j in range(2)]

@@ -164,27 +164,28 @@ def tile_attend_sink_topk_kernel(tc, qT, kT, vT, vs, sink, offs, out):
         low = {(j, h): keep.tile([P, 1], F32, name=f"low{j}{h}") for j in range(2) for h in range(2)}
         for h in (1, 0):
             nc.vector.tensor_reduce(out=low[0, h][:], in_=scores[0, h][:], axis=AX.X, op=ALU.min)
-        for h in (1, 0):
-            unused = keep.tile([P, HALF], F32, name=f"unused{h}")
-            nc.vector.tensor_scalar(
-                out=unused[:],
-                in0=scores[1, h][:],
-                scalar1=1.0,
-                scalar2=nsink[:, 1:2] if h else low[1, 1][:],
-                op0=ALU.mult,
-                op1=ALU.min,
-                accum_out=low[1, h][:],
-            )
+        EARLY = 128
+        v_first = keep.tile([P, EARLY + 2 * HALF], BF16, name="v_first")
+        nc.vector.tensor_reduce(out=low[1, 1][:], in_=scores[1, 1][:], axis=AX.X, op=ALU.min)
+        nc.vector.tensor_scalar(
+            out=v_first[:, EARLY:].bitcast(F32),
+            in0=scores[1, 0][:],
+            scalar1=1.0,
+            scalar2=nsink[:, 1:2],
+            op0=ALU.mult,
+            op1=ALU.min,
+            accum_out=low[1, 0][:],
+        )
         joined = keep.tile([P, 1], F32, name="joined")
         nc.gpsimd.tensor_scalar(out=joined[:], in0=low[0, 0][:], scalar1=low[0, 1][:], scalar2=nsink[:, 0:1], op0=ALU.min, op1=ALU.min)
-        lowest = [joined, low[1, 0]]
+        lowest = [joined, keep.tile([P, 1], F32, name="joined1")]
 
-        v_picked = [keep.tile([P, HALF], BF16, name=f"v_picked{g}") for g in range(2)]
-        for g in range(2):
-            nc.vector.tensor_copy(
-                v_picked[g][:],
-                v_table[:].indirect(offsets[:, g * (HALF // 16) : (g + 1) * (HALF // 16)]),
-            )
+        v_second = keep.tile([P, HALF], BF16, name="v_second")
+        v_picked = [v_first[:, 0:HALF], v_second[:]]
+        nc.vector.tensor_copy(v_first[:, 0:EARLY], v_table[:].indirect(offsets[:, 0 : EARLY // 16]))
+        nc.vector.tensor_tensor(lowest[1][:], low[1, 0][:], low[1, 1][:], ALU.min)
+        nc.vector.tensor_copy(v_first[:, EARLY:HALF], v_table[:].indirect(offsets[:, EARLY // 16 : HALF // 16]))
+        nc.vector.tensor_copy(v_second[:], v_table[:].indirect(offsets[:, HALF // 16 : N // 16]))
 
         sums = keep.tile([P, 2, 3], F32, name="sums")
         probs = {}
@@ -256,13 +257,13 @@ def tile_attend_sink_topk_kernel(tc, qT, kT, vT, vs, sink, offs, out):
                 nc.tensor.transpose(words[:, 0, u, :], w_pairs[0, g][:].bitcast(F32)[:, u * P : (u + 1) * P], ident[:])
             if g == 0:
                 for u in range(2):
-                    nc.tensor.transpose(words[:, 1, u, :], v_picked[g][:].bitcast(F32)[:, u : 2 * P : 2], ident[:])
+                    nc.tensor.transpose(words[:, 1, u, :], v_picked[g].bitcast(F32)[:, u : 2 * P : 2], ident[:])
                 nc.scalar.copy(out=laid, in_=words[:].rearrange("p a u e -> p a e u"))
             else:
                 nc.scalar.copy(out=laid[:, 0, :, :], in_=words[:, 0, :, :].rearrange("p u e -> p e u"))
                 late = score_banks.tile([P, 2, P], F32, name="score11")
                 for u in range(2):
-                    nc.tensor.transpose(late[:, u, :], v_picked[g][:].bitcast(F32)[:, u : 2 * P : 2], ident[:])
+                    nc.tensor.transpose(late[:, u, :], v_picked[g].bitcast(F32)[:, u : 2 * P : 2], ident[:])
                 nc.scalar.copy(out=laid[:, 1, :, :], in_=late[:].rearrange("p u e -> p e u"))
         words = turn_banks.tile([P, P], F32, name="turned")
         nc.tensor.transpose(words[:], w_pairs[1, 0][:].bitcast(F32), ident[:])

@@ -29,7 +29,7 @@ def tile_attend_sink_topk_kernel(tc, qT, kT, vT, vs, sink, offs, out):
         lists = ctx.enter_context(tc.tile_pool(name="lists", bufs=1))
         keep = ctx.enter_context(tc.tile_pool(name="keep", bufs=1))
         score_banks = ctx.enter_context(tc.psum_pool(name="score_banks", bufs=1))
-        turn_banks = ctx.enter_context(tc.psum_pool(name="turn_banks", bufs=4))
+        turn_banks = ctx.enter_context(tc.psum_pool(name="turn_banks", bufs=1))
 
         offsets = lists.tile([P, N // 16], U16, name="offsets")
         RUN = T // P
@@ -51,7 +51,7 @@ def tile_attend_sink_topk_kernel(tc, qT, kT, vT, vs, sink, offs, out):
         q_raw = keep.tile([P, PACK, NQ], F32, name="q_raw")
         for u in range(2):
             nc.sync.dma_start(out=q_raw[:, 2 * u : 2 * u + 2, :], in_=qT[0].rearrange("(p t) q -> p t q", t=PACK)[:, 2 * u : 2 * u + 2, :])
-        v_table = keep.tile([P, T], F32, name="v_table")
+        v_table = keep.tile([P, T], F32, name="v_table", align_bytes=64)
         nc.sync.dma_start(out=v_table[:], in_=vT)
 
         ident = keep.tile([P, P], F32, name="ident")
@@ -61,7 +61,7 @@ def tile_attend_sink_topk_kernel(tc, qT, kT, vT, vs, sink, offs, out):
 
         vs_table = keep.tile([P, T], F32, name="vs_table")
         for b in range(RUN // PACK):
-            turned = turn_banks.tile([P, PACK, P], F32, name="turned")
+            turned = turn_banks.tile([P, PACK, P], F32, name=f"turned{b % 4}")
             for c in range(PACK):
                 nc.tensor.transpose(turned[:, c, :], vs_runs[:, b * PACK + c : b * PACK + c + 1].to_broadcast([P, P]), ident[:])
             nc.scalar.copy(
@@ -69,7 +69,7 @@ def tile_attend_sink_topk_kernel(tc, qT, kT, vT, vs, sink, offs, out):
                 in_=turned[:].rearrange("r c p -> r p c"),
             )
 
-        turned = turn_banks.tile([P, P], F32, name="turned")
+        turned = turn_banks.tile([P, P], F32, name="turned0")
         nc.tensor.transpose(turned[:], sink_rows[:], ident[:])
         nc.scalar.activation(out=nsink[:], in_=turned[:, 0:2], func=ACT.Copy, scale=-1.0)
 
@@ -79,17 +79,17 @@ def tile_attend_sink_topk_kernel(tc, qT, kT, vT, vs, sink, offs, out):
 
         vs_picked = keep.tile([P, N], F32, name="vs_picked")
         nc.vector.tensor_copy(vs_picked[:], vs_table[:].indirect(offsets[:]))
-        vcol = keep.tile([P, 2 * PACK], F32, name="vcol")
-        for g, first in ((0, 2), (1, 0)):
-            turned = turn_banks.tile([P, PACK, P], F32, name="turned")
+        vcol = keep.tile([P, PACK], F32, name="vcol")
+        for g, first in ((1, 0),):
+            turned = turn_banks.tile([P, PACK, P], F32, name="turned1")
             for t in range(first, PACK):
                 nc.tensor.transpose(turned[:, t, :], vs_picked[:, g * HALF + t : (g + 1) * HALF : PACK], ident[:])
-            nc.scalar.copy(out=vcol[:, g * PACK + first : (g + 1) * PACK], in_=turned[:, first:PACK, 0])
-        vs_rows = [keep.tile([P, 2, P, 2], F32, name=f"vs_rows{g}") for g in range(2)]
+            nc.scalar.copy(out=vcol[:, first:PACK], in_=turned[:, first:PACK, 0])
+        vs_rows = [keep.tile([P, 2 - g, P, 2], F32, name=f"vs_rows{g}") for g in range(2)]
         for g in range(2):
             nc.gpsimd.tensor_scalar(
                 out=vs_rows[g][:],
-                in0=vs_picked[:, g * HALF : (g + 1) * HALF].rearrange("r (s u w) -> r u s w", u=2, w=2),
+                in0=vs_picked[:, g * HALF : (g + 1) * HALF].rearrange("r (s u w) -> r u s w", u=2, w=2)[:, 0 : 2 - g, :, :],
                 scalar1=1.0,
                 scalar2=0.0,
                 op0=ALU.mult,
@@ -164,11 +164,10 @@ def tile_attend_sink_topk_kernel(tc, qT, kT, vT, vs, sink, offs, out):
         low = {(j, h): keep.tile([P, 1], F32, name=f"low{j}{h}") for j in range(2) for h in range(2)}
         for h in (1, 0):
             nc.vector.tensor_reduce(out=low[0, h][:], in_=scores[0, h][:], axis=AX.X, op=ALU.min)
-        EARLY = 128
-        v_first = keep.tile([P, EARLY + 2 * HALF], BF16, name="v_first")
+        v_first = keep.tile([P, 2 * HALF], BF16, name="v_first")
         nc.vector.tensor_reduce(out=low[1, 1][:], in_=scores[1, 1][:], axis=AX.X, op=ALU.min)
         nc.vector.tensor_scalar(
-            out=v_first[:, EARLY:].bitcast(F32),
+            out=v_first[:].bitcast(F32),
             in0=scores[1, 0][:],
             scalar1=1.0,
             scalar2=nsink[:, 1:2],
@@ -182,17 +181,19 @@ def tile_attend_sink_topk_kernel(tc, qT, kT, vT, vs, sink, offs, out):
 
         v_second = keep.tile([P, HALF], BF16, name="v_second")
         v_picked = [v_first[:, 0:HALF], v_second[:]]
-        nc.vector.tensor_copy(v_first[:, 0:EARLY], v_table[:].indirect(offsets[:, 0 : EARLY // 16]))
         nc.vector.tensor_tensor(lowest[1][:], low[1, 0][:], low[1, 1][:], ALU.min)
-        nc.vector.tensor_copy(v_first[:, EARLY:HALF], v_table[:].indirect(offsets[:, EARLY // 16 : HALF // 16]))
-        nc.vector.tensor_copy(v_second[:], v_table[:].indirect(offsets[:, HALF // 16 : N // 16]))
+        for g in range(2):
+            nc.vector.tensor_copy(
+                v_picked[g].rearrange("p (u s w) -> p s u w", u=2, w=2),
+                v_table[:].indirect(offsets[:, g * (HALF // 16) : (g + 1) * (HALF // 16)]),
+            )
 
         sums = keep.tile([P, 2, 3], F32, name="sums")
         probs = {}
         for j in range(2):
             for h in range(2):
                 probs[j, h] = keep.tile([P, PACK, P], F32, name=f"probs{j}{h}")
-                if (j, h) != (1, 1):
+                if (j, h) in ((0, 0), (1, 0)):
                     laid = probs[j, h][:].rearrange("p t s -> p (t s)").rearrange("p (u s w) -> p u s w", u=2, w=2)
                     read = scores[j, h][:].rearrange("p (s u w) -> p u s w", u=2, w=2)
                 else:
@@ -209,97 +210,79 @@ def tile_attend_sink_topk_kernel(tc, qT, kT, vT, vs, sink, offs, out):
 
         for j in range(2):
             nc.scalar.activation(out=sums[:, j, 2:3], in_=nsink[:, j : j + 1], func=ACT.Exp, bias=lowest[j][:], scale=-1.0)
-        parts = [(1, g) for g in range(2)]
-        w_grouped = {(j, g): keep.tile([P, P, PACK], BF16, name=f"w_grouped{j}{g}", align_bytes=64) for j, g in parts}
-        w_codes = {(j, g): keep.tile([P, P], U32, name=f"w_codes{j}{g}", align_bytes=64) for j, g in parts}
-        w_scales = {(j, g): keep.tile([P, P], U8, name=f"w_scales{j}{g}", align_bytes=64) for j, g in parts}
-        wv_grouped = [keep.tile([P, 2, P, PACK], BF16, name=f"wv_grouped{g}", align_bytes=64) for g in range(2)]
-        wv_codes = [keep.tile([P, 2, P], U32, name=f"wv_codes{g}", align_bytes=64) for g in range(2)]
-        wv_scales = [keep.tile([P, 2, P], U8, name=f"wv_scales{g}", align_bytes=64) for g in range(2)]
         total = keep.tile([P, 2], F32, name="total")
         share = keep.tile([P, 2], F32, name="share")
 
-        nc.vector.tensor_reduce(out=total[:], in_=sums[:], axis=AX.X, op=ALU.add)
-        nc.vector.reciprocal(share[:], total[:])
-        early = [(0, 0), (0, 1), (1, 0)]
-        widths = {(0, 0): HALF, (0, 1): HALF, (1, 0): HALF // 2}
-        w_pairs = {(j, g): keep.tile([P, widths[j, g]], BF16, name=f"w_pairs{j}{g}") for j, g in early}
-        for j, g in early:
+        w_pairs = {j: keep.tile([P, HALF], BF16, name=f"w_pairs{j}") for j in range(2)}
+        for j in range(2):
             nc.gpsimd.tensor_tensor(
-                w_pairs[j, g][:],
-                probs[j, g][:].rearrange("p t s -> p (t s)")[:, 0 : widths[j, g]],
-                vs_rows[g][:].rearrange("p u s w -> p (u s w)")[:, 0 : widths[j, g]],
+                w_pairs[j][:],
+                probs[j, 0][:].rearrange("p t s -> p (t s)"),
+                vs_rows[0][:].rearrange("p u s w -> p (u s w)"),
                 ALU.mult,
             )
-        turned = score_banks.tile([P, 2, P], F32, name="score10")
-        for w in range(2):
-            nc.tensor.transpose(turned[:, w, :], probs[1, 0][:].rearrange("p t s -> p (t s)")[:, HALF // 2 + w : HALF : 2], ident[:])
-        nc.vector.tensor_tensor(
-            w_grouped[1, 0][:, :, 2:4],
-            turned[:].rearrange("p w q -> p q w"),
-            vcol[:, 2:4].unsqueeze(1).to_broadcast([P, P, 2]),
-            ALU.mult,
-        )
-        for g in range(2):
-            if g == 1:
-                turned = turn_banks.tile([P, PACK, P], F32, name="turned")
-                for t in range(PACK):
-                    nc.tensor.transpose(turned[:, t, :], probs[1, g][:, t, :], ident[:])
-                nc.vector.tensor_tensor(
-                    w_grouped[1, g][:],
-                    turned[:].rearrange("p t q -> p q t"),
-                    vcol[:, g * PACK : (g + 1) * PACK].unsqueeze(1).to_broadcast([P, P, PACK]),
-                    ALU.mult,
-                )
-            laid = wv_grouped[g][:].rearrange("p a e t -> p (a e t)").bitcast(F32).rearrange("p (a e u) -> p a e u", a=2, u=2)
-            words = turn_banks.tile([P, 2, 2, P], F32, name="turned")
+        w_half = keep.tile([P, P, 2], BF16, name="w_half")
+        nc.gpsimd.tensor_tensor(w_half[:], probs[1, 1][:, 0:2, :].rearrange("p w s -> p s w"), vs_rows[1][:, 0, :, :], ALU.mult)
+
+        w_late = keep.tile([P, 2, P, PACK], BF16, name="v_table", align_bytes=64)
+        w01 = w_late[:, 0, :, :]
+        w11 = w_late[:, 1, :, :]
+        turned = turn_banks.tile([P, PACK, P], F32, name="turned0")
+        for t in range(PACK):
+            nc.tensor.transpose(turned[:, t, :], probs[0, 1][:, t, :], ident[:])
+        nc.vector.tensor_tensor(w01, turned[:].rearrange("p t q -> p q t"), vcol[:].unsqueeze(1).to_broadcast([P, P, PACK]), ALU.mult)
+
+        vw_grouped = [keep.tile([P, 2, P, PACK], BF16, name=f"vw_grouped{g}", align_bytes=64) for g in range(2)]
+
+        def turn_group(g):
+            laid = vw_grouped[g][:].rearrange("p a e t -> p (a e t)").bitcast(F32).rearrange("p (a e u) -> p a e u", a=2, u=2)
+            words = turn_banks.tile([P, 2, 2, P], F32, name=f"turned{1 + g}")
             for u in range(2):
-                nc.tensor.transpose(words[:, 0, u, :], w_pairs[0, g][:].bitcast(F32)[:, u * P : (u + 1) * P], ident[:])
-            if g == 0:
-                for u in range(2):
-                    nc.tensor.transpose(words[:, 1, u, :], v_picked[g].bitcast(F32)[:, u : 2 * P : 2], ident[:])
-                nc.scalar.copy(out=laid, in_=words[:].rearrange("p a u e -> p a e u"))
-            else:
-                nc.scalar.copy(out=laid[:, 0, :, :], in_=words[:, 0, :, :].rearrange("p u e -> p e u"))
-                late = score_banks.tile([P, 2, P], F32, name="score11")
-                for u in range(2):
-                    nc.tensor.transpose(late[:, u, :], v_picked[g].bitcast(F32)[:, u : 2 * P : 2], ident[:])
-                nc.scalar.copy(out=laid[:, 1, :, :], in_=late[:].rearrange("p u e -> p e u"))
-        words = turn_banks.tile([P, P], F32, name="turned")
-        nc.tensor.transpose(words[:], w_pairs[1, 0][:].bitcast(F32), ident[:])
+                nc.tensor.transpose(words[:, 0, u, :], v_picked[g].bitcast(F32)[:, u * P : (u + 1) * P], ident[:])
+            for u in range(2):
+                nc.tensor.transpose(words[:, 1, u, :], w_pairs[g][:].bitcast(F32)[:, u * P : (u + 1) * P], ident[:])
+            nc.scalar.copy(out=laid, in_=words[:].rearrange("p a u e -> p a e u"))
+
+        turn_group(0)
+        turned = turn_banks.tile([P, 2, P], F32, name="turned3")
+        for w in range(2):
+            nc.tensor.transpose(turned[:, w, :], probs[1, 1][:, 2 + w, :], ident[:])
+        nc.vector.tensor_tensor(
+            w11[:, :, 2:4], turned[:].rearrange("p w q -> p q w"), vcol[:, 2:4].unsqueeze(1).to_broadcast([P, P, 2]), ALU.mult
+        )
+        turn_group(1)
+        words = turn_banks.tile([P, P], F32, name="turned0")
+        nc.tensor.transpose(words[:], w_half[:].rearrange("p s w -> p (s w)").bitcast(F32), ident[:])
         nc.scalar.copy(
-            out=w_grouped[1, 0][:].rearrange("p q t -> p (q t)").bitcast(F32).rearrange("p (q u) -> p q u", u=2)[:, :, 0],
+            out=w11.rearrange("p q t -> p (q t)").bitcast(F32).rearrange("p (q u) -> p q u", u=2)[:, :, 0],
             in_=words[:],
         )
 
-        def quantise_w(g):
+        vw_codes = [keep.tile([P, 2, P], U32, name=f"vw_codes{g}", align_bytes=64) for g in range(2)]
+        vw_scales = [keep.tile([P, 2, P], U8, name=f"vw_scales{g}", align_bytes=64) for g in range(2)]
+        w_codes = [keep.tile([P, P], U32, name=f"w_codes{j}", align_bytes=64) for j in range(2)]
+        w_scales = [keep.tile([P, P], U8, name=f"w_scales{j}", align_bytes=64) for j in range(2)]
+        late = [w01, w11]
+        for g in range(2):
             nc.vector.quantize_mx(
-                out=w_codes[1, g][:].bitcast(FP8X4), scales=w_scales[1, g][:], in_=w_grouped[1, g][:].rearrange("p q t -> p (q t)")
+                out=vw_codes[g][:].rearrange("p a e -> p (a e)").bitcast(FP8X4),
+                scales=vw_scales[g][:].rearrange("p a e -> p (a e)"),
+                in_=vw_grouped[g][:].rearrange("p a e t -> p (a e t)"),
             )
-
-        def quantise_wv(g):
-            nc.vector.quantize_mx(
-                out=wv_codes[g][:].rearrange("p a e -> p (a e)").bitcast(FP8X4),
-                scales=wv_scales[g][:].rearrange("p a e -> p (a e)"),
-                in_=wv_grouped[g][:].rearrange("p a e t -> p (a e t)"),
-            )
-
-        quantise_wv(0)
-        quantise_w(1)
-        quantise_wv(1)
-        quantise_w(0)
+            nc.vector.quantize_mx(out=w_codes[g][:].bitcast(FP8X4), scales=w_scales[g][:], in_=late[g].rearrange("p q t -> p (q t)"))
+        nc.vector.tensor_reduce(out=total[:], in_=sums[:], axis=AX.X, op=ALU.add)
+        nc.vector.reciprocal(share[:], total[:])
         for j in range(2):
             acc = score_banks.tile([P, DV], F32, name=f"score0{j}")
-            order = (1, 0) if j else (0, 1)
-            for g in order:
+            for g in range(2):
                 nc.tensor.matmul_mx(
                     out=acc[:],
-                    lhsT=(w_codes[j, g][:] if j else wv_codes[g][:, 0, :]).bitcast(FP8X4),
-                    lhsT_scale=w_scales[j, g][:] if j else wv_scales[g][:, 0, :],
-                    rhs=wv_codes[g][:, 1, :].bitcast(FP8X4),
-                    rhs_scale=wv_scales[g][:, 1, :],
-                    start=(g == order[0]),
-                    stop=(g == order[1]),
+                    lhsT=(w_codes[j][:] if g else vw_codes[j][:, 1, :]).bitcast(FP8X4),
+                    lhsT_scale=w_scales[j][:] if g else vw_scales[j][:, 1, :],
+                    rhs=vw_codes[g][:, 0, :].bitcast(FP8X4),
+                    rhs_scale=vw_scales[g][:, 0, :],
+                    start=(g == 0),
+                    stop=(g == 1),
                 )
             result = keep.tile([P, DV], F32, name=f"result{j}")
             nc.scalar.activation(out=result[:], in_=acc[:], func=ACT.Copy, scale=share[:, j : j + 1])

@@ -28,6 +28,7 @@ def tile_attend_sink_topk_kernel(tc, qT, kT, vT, vs, sink, offs, out):
     with ExitStack() as ctx:
         lists = ctx.enter_context(tc.tile_pool(name="lists", bufs=1))
         keep = ctx.enter_context(tc.tile_pool(name="keep", bufs=1))
+        placed = ctx.enter_context(tc.tile_pool(name="placed", bufs=1))
         score_banks = ctx.enter_context(tc.psum_pool(name="score_banks", bufs=1))
         turn_banks = ctx.enter_context(tc.psum_pool(name="turn_banks", bufs=1))
 
@@ -51,7 +52,7 @@ def tile_attend_sink_topk_kernel(tc, qT, kT, vT, vs, sink, offs, out):
         q_raw = keep.tile([P, PACK, NQ], F32, name="q_raw")
         for u in range(2):
             nc.sync.dma_start(out=q_raw[:, 2 * u : 2 * u + 2, :], in_=qT[0].rearrange("(p t) q -> p t q", t=PACK)[:, 2 * u : 2 * u + 2, :])
-        v_table = keep.tile([P, T], F32, name="v_table", align_bytes=64)
+        v_table = placed.tile([P, T], F32, name="v_table", align_bytes=64, offset=0)
         nc.sync.dma_start(out=v_table[:], in_=vT)
 
         ident = keep.tile([P, P], F32, name="ident")
@@ -85,6 +86,9 @@ def tile_attend_sink_topk_kernel(tc, qT, kT, vT, vs, sink, offs, out):
             for t in range(first, PACK):
                 nc.tensor.transpose(turned[:, t, :], vs_picked[:, g * HALF + t : (g + 1) * HALF : PACK], ident[:])
             nc.scalar.copy(out=vcol[:, first:PACK], in_=turned[:, first:PACK, 0])
+        vs_bank = turn_banks.tile([P, 2, P], F32, name="turned3")
+        for w in range(2):
+            nc.tensor.transpose(vs_bank[:, w, :], vcol[:, 2 + w : 3 + w].to_broadcast([P, P]), ident[:])
         vs_rows = [keep.tile([P, 2 - g, P, 2], F32, name=f"vs_rows{g}") for g in range(2)]
         for g in range(2):
             nc.gpsimd.tensor_scalar(
@@ -177,7 +181,7 @@ def tile_attend_sink_topk_kernel(tc, qT, kT, vT, vs, sink, offs, out):
         )
         joined = keep.tile([P, 1], F32, name="joined")
         nc.gpsimd.tensor_scalar(out=joined[:], in0=low[0, 0][:], scalar1=low[0, 1][:], scalar2=nsink[:, 0:1], op0=ALU.min, op1=ALU.min)
-        lowest = [joined, keep.tile([P, 1], F32, name="joined1")]
+        lowest = [joined, placed.tile([P, 1], F32, name="joined1", align_bytes=64, offset=4 * T)]
 
         v_second = keep.tile([P, HALF], BF16, name="v_second")
         v_picked = [v_first[:, 0:HALF], v_second[:]]
@@ -193,7 +197,7 @@ def tile_attend_sink_topk_kernel(tc, qT, kT, vT, vs, sink, offs, out):
         for j in range(2):
             for h in range(2):
                 probs[j, h] = keep.tile([P, PACK, P], F32, name=f"probs{j}{h}")
-                if (j, h) in ((0, 0), (1, 0)):
+                if (j, h) != (0, 1):
                     laid = probs[j, h][:].rearrange("p t s -> p (t s)").rearrange("p (u s w) -> p u s w", u=2, w=2)
                     read = scores[j, h][:].rearrange("p (s u w) -> p u s w", u=2, w=2)
                 else:
@@ -221,12 +225,16 @@ def tile_attend_sink_topk_kernel(tc, qT, kT, vT, vs, sink, offs, out):
                 vs_rows[0][:].rearrange("p u s w -> p (u s w)"),
                 ALU.mult,
             )
+        last = probs[1, 1][:].rearrange("p t s -> p (t s)").rearrange("p (u s w) -> p u s w", u=2, w=2)
         w_half = keep.tile([P, P, 2], BF16, name="w_half")
-        nc.gpsimd.tensor_tensor(w_half[:], probs[1, 1][:, 0:2, :].rearrange("p w s -> p s w"), vs_rows[1][:, 0, :, :], ALU.mult)
+        nc.gpsimd.tensor_tensor(w_half[:], last[:, 0, :, :], vs_rows[1][:, 0, :, :], ALU.mult)
 
-        w_late = keep.tile([P, 2, P, PACK], BF16, name="v_table", align_bytes=64)
-        w01 = w_late[:, 0, :, :]
-        w11 = w_late[:, 1, :, :]
+        w_other = placed.tile([P, 2 * P], BF16, name="w_other", align_bytes=64, offset=0)[:]
+        w01 = placed.tile([P, P, PACK], BF16, name="w01", align_bytes=64, offset=4 * T)[:]
+        w11 = keep.tile([P, P, PACK], BF16, name="w11", align_bytes=64)[:]
+        nc.vector.tensor_tensor(
+            w_other.rearrange("p (s w) -> p s w", w=2), last[:, 1, :, :], vs_bank[:].rearrange("p w s -> p s w"), ALU.mult
+        )
         turned = turn_banks.tile([P, PACK, P], F32, name="turned0")
         for t in range(PACK):
             nc.tensor.transpose(turned[:, t, :], probs[0, 1][:, t, :], ident[:])
@@ -244,18 +252,13 @@ def tile_attend_sink_topk_kernel(tc, qT, kT, vT, vs, sink, offs, out):
             nc.scalar.copy(out=laid, in_=words[:].rearrange("p a u e -> p a e u"))
 
         turn_group(0)
-        turned = turn_banks.tile([P, 2, P], F32, name="turned3")
-        for w in range(2):
-            nc.tensor.transpose(turned[:, w, :], probs[1, 1][:, 2 + w, :], ident[:])
-        nc.vector.tensor_tensor(
-            w11[:, :, 2:4], turned[:].rearrange("p w q -> p q w"), vcol[:, 2:4].unsqueeze(1).to_broadcast([P, P, 2]), ALU.mult
-        )
         turn_group(1)
-        words = turn_banks.tile([P, P], F32, name="turned0")
-        nc.tensor.transpose(words[:], w_half[:].rearrange("p s w -> p (s w)").bitcast(F32), ident[:])
+        words = turn_banks.tile([P, 2, P], F32, name="turned3")
+        nc.tensor.transpose(words[:, 1, :], w_other.bitcast(F32), ident[:])
+        nc.tensor.transpose(words[:, 0, :], w_half[:].rearrange("p s w -> p (s w)").bitcast(F32), ident[:])
         nc.scalar.copy(
-            out=w11.rearrange("p q t -> p (q t)").bitcast(F32).rearrange("p (q u) -> p q u", u=2)[:, :, 0],
-            in_=words[:],
+            out=w11.rearrange("p q t -> p (q t)").bitcast(F32).rearrange("p (q u) -> p q u", u=2),
+            in_=words[:].rearrange("p u q -> p q u"),
         )
 
         vw_codes = [keep.tile([P, 2, P], U32, name=f"vw_codes{g}", align_bytes=64) for g in range(2)]

@@ -86,14 +86,16 @@ def tile_attend_sink_topk_kernel(tc, qT, kT, vT, vs, sink, offs, out):
             for t in range(first, PACK):
                 nc.tensor.transpose(turned[:, t, :], vs_picked[:, g * HALF + t : (g + 1) * HALF : PACK], ident[:])
             nc.scalar.copy(out=vcol[:, first:PACK], in_=turned[:, first:PACK, 0])
-        vs_bank = turn_banks.tile([P, 2, P], F32, name="turned3")
-        for w in range(2):
-            nc.tensor.transpose(vs_bank[:, w, :], vcol[:, 2 + w : 3 + w].to_broadcast([P, P]), ident[:])
-        vs_rows = [keep.tile([P, 2 - g, P, 2], F32, name=f"vs_rows{g}") for g in range(2)]
+        vs_bank = turn_banks.tile([P, 2, 2, P], F32, name="turned3")
+        for u in range(2):
+            for w in range(2):
+                nc.tensor.transpose(vs_bank[:, w, u, :], vcol[:, 2 * u + w : 2 * u + w + 1].to_broadcast([P, P]), ident[:])
+        SHARE = 64
+        vs_rows = [keep.tile([P, 2 - g, (P, SHARE)[g], 2], F32, name=f"vs_rows{g}") for g in range(2)]
         for g in range(2):
             nc.gpsimd.tensor_scalar(
                 out=vs_rows[g][:],
-                in0=vs_picked[:, g * HALF : (g + 1) * HALF].rearrange("r (s u w) -> r u s w", u=2, w=2)[:, 0 : 2 - g, :, :],
+                in0=vs_picked[:, g * HALF : (g + 1) * HALF].rearrange("r (s u w) -> r u s w", u=2, w=2)[:, 0 : 2 - g, 0 : (P, SHARE)[g], :],
                 scalar1=1.0,
                 scalar2=0.0,
                 op0=ALU.mult,
@@ -225,63 +227,66 @@ def tile_attend_sink_topk_kernel(tc, qT, kT, vT, vs, sink, offs, out):
                 vs_rows[0][:].rearrange("p u s w -> p (u s w)"),
                 ALU.mult,
             )
-        last = probs[1, 1][:].rearrange("p t s -> p (t s)").rearrange("p (u s w) -> p u s w", u=2, w=2)
-        w_half = keep.tile([P, P, 2], BF16, name="w_half")
-        nc.gpsimd.tensor_tensor(w_half[:], last[:, 0, :, :], vs_rows[1][:, 0, :, :], ALU.mult)
+        last = probs[1, 1][:].rearrange("p t s -> p (t s)").rearrange("p (x w) -> p x w", w=2)
+        w_last = placed.tile([P, 2 * P, 2], BF16, name="w_last", align_bytes=64, offset=0)
 
-        w_other = placed.tile([P, 2 * P], BF16, name="w_other", align_bytes=64, offset=0)[:]
-        w01 = placed.tile([P, P, PACK], BF16, name="w01", align_bytes=64, offset=4 * T)[:]
-        w11 = keep.tile([P, P, PACK], BF16, name="w11", align_bytes=64)[:]
+        vw_grouped = [
+            keep.tile([P, 2, P, PACK], BF16, name="vw_grouped0", align_bytes=64),
+            placed.tile([P, 2, P, PACK], BF16, name="vw_grouped1", align_bytes=64, offset=4 * T),
+        ]
+        late = [keep.tile([P, P, PACK], BF16, name=f"w1{g}", align_bytes=64) for g in range(2)]
         nc.vector.tensor_tensor(
-            w_other.rearrange("p (s w) -> p s w", w=2), last[:, 1, :, :], vs_bank[:].rearrange("p w s -> p s w"), ALU.mult
+            w_last[:, SHARE:, :], last[:, SHARE:, :], vs_bank[:].rearrange("p w u s -> p (u s) w")[:, SHARE:, :], ALU.mult
         )
+        nc.gpsimd.tensor_tensor(w_last[:, 0:SHARE, :], last[:, 0:SHARE, :], vs_rows[1][:, 0, :, :], ALU.mult)
+        nc.vector.tensor_reduce(out=total[:], in_=sums[:], axis=AX.X, op=ALU.add)
         turned = turn_banks.tile([P, PACK, P], F32, name="turned0")
         for t in range(PACK):
             nc.tensor.transpose(turned[:, t, :], probs[0, 1][:, t, :], ident[:])
-        nc.vector.tensor_tensor(w01, turned[:].rearrange("p t q -> p q t"), vcol[:].unsqueeze(1).to_broadcast([P, P, PACK]), ALU.mult)
+        nc.vector.tensor_tensor(
+            vw_grouped[1][:, 1, :, :], turned[:].rearrange("p t q -> p q t"), vcol[:].unsqueeze(1).to_broadcast([P, P, PACK]), ALU.mult
+        )
 
-        vw_grouped = [keep.tile([P, 2, P, PACK], BF16, name=f"vw_grouped{g}", align_bytes=64) for g in range(2)]
+        nc.vector.reciprocal(share[:], total[:])
 
-        def turn_group(g):
-            laid = vw_grouped[g][:].rearrange("p a e t -> p (a e t)").bitcast(F32).rearrange("p (a e u) -> p a e u", a=2, u=2)
-            words = turn_banks.tile([P, 2, 2, P], F32, name=f"turned{1 + g}")
-            for u in range(2):
-                nc.tensor.transpose(words[:, 0, u, :], v_picked[g].bitcast(F32)[:, u * P : (u + 1) * P], ident[:])
-            for u in range(2):
-                nc.tensor.transpose(words[:, 1, u, :], w_pairs[g][:].bitcast(F32)[:, u * P : (u + 1) * P], ident[:])
-            nc.scalar.copy(out=laid, in_=words[:].rearrange("p a u e -> p a e u"))
+        def turn(sources, bank, grouped, order=(0, 1)):
+            for a, source in enumerate(sources):
+                for u in order:
+                    nc.tensor.transpose(bank[:, a, u, :], source.bitcast(F32)[:, u * P : (u + 1) * P], ident[:])
+            nc.scalar.copy(
+                out=grouped.bitcast(F32).rearrange("p (a e u) -> p a e u", a=len(sources), u=2),
+                in_=bank[:].rearrange("p a u e -> p a e u"),
+            )
 
-        turn_group(0)
-        turn_group(1)
-        words = turn_banks.tile([P, 2, P], F32, name="turned3")
-        nc.tensor.transpose(words[:, 1, :], w_other.bitcast(F32), ident[:])
-        nc.tensor.transpose(words[:, 0, :], w_half[:].rearrange("p s w -> p (s w)").bitcast(F32), ident[:])
-        nc.scalar.copy(
-            out=w11.rearrange("p q t -> p (q t)").bitcast(F32).rearrange("p (q u) -> p q u", u=2),
-            in_=words[:].rearrange("p u q -> p q u"),
+        turn([v_picked[0], w_pairs[0][:]], turn_banks.tile([P, 2, 2, P], F32, name="turned1"), vw_grouped[0][:].rearrange("p a e t -> p (a e t)"))
+        turn([v_picked[1]], turn_banks.tile([P, 1, 2, P], F32, name="turned2"), vw_grouped[1][:, 0, :, :].rearrange("p e t -> p (e t)"))
+        turn([w_pairs[1][:]], score_banks.tile([P, 1, 2, P], F32, name="score10"), late[0][:].rearrange("p e t -> p (e t)"))
+        turn(
+            [w_last[:].rearrange("p x w -> p (x w)")],
+            turn_banks.tile([P, 1, 2, P], F32, name="turned3"),
+            late[1][:].rearrange("p e t -> p (e t)"),
+            (1, 0),
         )
 
         vw_codes = [keep.tile([P, 2, P], U32, name=f"vw_codes{g}", align_bytes=64) for g in range(2)]
         vw_scales = [keep.tile([P, 2, P], U8, name=f"vw_scales{g}", align_bytes=64) for g in range(2)]
-        w_codes = [keep.tile([P, P], U32, name=f"w_codes{j}", align_bytes=64) for j in range(2)]
-        w_scales = [keep.tile([P, P], U8, name=f"w_scales{j}", align_bytes=64) for j in range(2)]
-        late = [w01, w11]
+        w_codes = [keep.tile([P, P], U32, name=f"w_codes{g}", align_bytes=64) for g in range(2)]
+        w_scales = [keep.tile([P, P], U8, name=f"w_scales{g}", align_bytes=64) for g in range(2)]
         for g in range(2):
             nc.vector.quantize_mx(
                 out=vw_codes[g][:].rearrange("p a e -> p (a e)").bitcast(FP8X4),
                 scales=vw_scales[g][:].rearrange("p a e -> p (a e)"),
                 in_=vw_grouped[g][:].rearrange("p a e t -> p (a e t)"),
             )
-            nc.vector.quantize_mx(out=w_codes[g][:].bitcast(FP8X4), scales=w_scales[g][:], in_=late[g].rearrange("p q t -> p (q t)"))
-        nc.vector.tensor_reduce(out=total[:], in_=sums[:], axis=AX.X, op=ALU.add)
-        nc.vector.reciprocal(share[:], total[:])
+        for g in range(2):
+            nc.vector.quantize_mx(out=w_codes[g][:].bitcast(FP8X4), scales=w_scales[g][:], in_=late[g][:].rearrange("p q t -> p (q t)"))
         for j in range(2):
             acc = score_banks.tile([P, DV], F32, name=f"score0{j}")
             for g in range(2):
                 nc.tensor.matmul_mx(
                     out=acc[:],
-                    lhsT=(w_codes[j][:] if g else vw_codes[j][:, 1, :]).bitcast(FP8X4),
-                    lhsT_scale=w_scales[j][:] if g else vw_scales[j][:, 1, :],
+                    lhsT=(w_codes[g][:] if j else vw_codes[g][:, 1, :]).bitcast(FP8X4),
+                    lhsT_scale=w_scales[g][:] if j else vw_scales[g][:, 1, :],
                     rhs=vw_codes[g][:, 0, :].bitcast(FP8X4),
                     rhs_scale=vw_scales[g][:, 0, :],
                     start=(g == 0),

@@ -90,7 +90,7 @@ def tile_attend_sink_topk_kernel(tc, qT, kT, vT, vs, sink, offs, out):
         for u in range(2):
             for w in range(2):
                 nc.tensor.transpose(vs_bank[:, w, u, :], vcol[:, 2 * u + w : 2 * u + w + 1].to_broadcast([P, P]), ident[:])
-        SHARE = 64
+        SHARE = 96
         vs_rows = [keep.tile([P, 2 - g, (P, SHARE)[g], 2], F32, name=f"vs_rows{g}") for g in range(2)]
         for g in range(2):
             nc.gpsimd.tensor_scalar(
@@ -217,6 +217,9 @@ def tile_attend_sink_topk_kernel(tc, qT, kT, vT, vs, sink, offs, out):
         for j in range(2):
             nc.scalar.activation(out=sums[:, j, 2:3], in_=nsink[:, j : j + 1], func=ACT.Exp, bias=lowest[j][:], scale=-1.0)
         total = keep.tile([P, 2], F32, name="total")
+        summed = keep.tile([P, 2, 3], F32, name="summed")
+        for j in range(2):
+            nc.scalar.activation(out=summed[:, j, :], in_=sums[:, j, :], func=ACT.Copy, accum_out=total[:, j : j + 1])
         share = keep.tile([P, 2], F32, name="share")
 
         w_pairs = {j: keep.tile([P, HALF], BF16, name=f"w_pairs{j}") for j in range(2)}
@@ -239,7 +242,6 @@ def tile_attend_sink_topk_kernel(tc, qT, kT, vT, vs, sink, offs, out):
             w_last[:, SHARE:, :], last[:, SHARE:, :], vs_bank[:].rearrange("p w u s -> p (u s) w")[:, SHARE:, :], ALU.mult
         )
         nc.gpsimd.tensor_tensor(w_last[:, 0:SHARE, :], last[:, 0:SHARE, :], vs_rows[1][:, 0, :, :], ALU.mult)
-        nc.vector.tensor_reduce(out=total[:], in_=sums[:], axis=AX.X, op=ALU.add)
         turned = turn_banks.tile([P, PACK, P], F32, name="turned0")
         for t in range(PACK):
             nc.tensor.transpose(turned[:, t, :], probs[0, 1][:, t, :], ident[:])

@@ -90,7 +90,7 @@ def tile_attend_sink_topk_kernel(tc, qT, kT, vT, vs, sink, offs, out):
         for u in range(2):
             for w in range(2):
                 nc.tensor.transpose(vs_bank[:, w, u, :], vcol[:, 2 * u + w : 2 * u + w + 1].to_broadcast([P, P]), ident[:])
-        SHARE = 96
+        SHARE = 64
         vs_rows = [keep.tile([P, 2 - g, (P, SHARE)[g], 2], F32, name=f"vs_rows{g}") for g in range(2)]
         for g in range(2):
             nc.gpsimd.tensor_scalar(

@@ -60,23 +60,20 @@ def tile_attend_sink_topk_kernel(tc, qT, kT, vT, vs, sink, offs, out):
 
         nsink = keep.tile([P, 2], F32, name="nsink")
 
-        vs_table = keep.tile([P, T], F32, name="vs_table")
+        vs_table = placed.tile([P, T], F32, name="vs_table", align_bytes=64, offset=5 * T)
         for b in range(RUN // PACK):
             turned = turn_banks.tile([P, PACK, P], F32, name=f"turned{b % 4}")
             for c in range(PACK):
                 nc.tensor.transpose(turned[:, c, :], vs_runs[:, b * PACK + c : b * PACK + c + 1].to_broadcast([P, P]), ident[:])
-            nc.scalar.copy(
-                out=vs_table[:].rearrange("r (p b c) -> r b p c", c=PACK, b=RUN // PACK)[:, b, :, :],
-                in_=turned[:].rearrange("r c p -> r p c"),
-            )
+            leave = nc.vector.tensor_copy if b % 2 else nc.scalar.copy
+            leave(vs_table[:].rearrange("r (p b c) -> r b p c", c=PACK, b=RUN // PACK)[:, b, :, :], turned[:].rearrange("r c p -> r p c"))
 
         turned = turn_banks.tile([P, P], F32, name="turned0")
         nc.tensor.transpose(turned[:], sink_rows[:], ident[:])
         nc.scalar.activation(out=nsink[:], in_=turned[:, 0:2], func=ACT.Copy, scale=-1.0)
 
         k_grouped = [keep.tile([P, HALF, PACK], BF16, name=f"k_grouped{h}", align_bytes=64) for h in range(2)]
-        k_low = keep.tile([P, 2, N], F32, name="k_low")
-        nc.vector.tensor_copy(k_low[:, 0, :], k_table[0][:].indirect(offsets[:]))
+        k_low = placed.tile([P, 2, N], F32, name="k_low", align_bytes=64, offset=5 * T)
 
         vs_picked = keep.tile([P, N], F32, name="vs_picked")
         nc.vector.tensor_copy(vs_picked[:], vs_table[:].indirect(offsets[:]))
@@ -102,16 +99,18 @@ def tile_attend_sink_topk_kernel(tc, qT, kT, vT, vs, sink, offs, out):
                 op1=ALU.add,
             )
 
-        nc.vector.tensor_copy(k_low[:, 1, :], k_table[1][:].indirect(offsets[:]))
-        for h in range(2):
-            nc.scalar.activation(
-                out=k_grouped[h][:, :, 0:2], in_=k_low[:, :, h * HALF : (h + 1) * HALF].rearrange("p t n -> p n t"), func=ACT.Copy
-            )
+        for t in range(2):
+            nc.vector.tensor_copy(k_low[:, t, :], k_table[t][:].indirect(offsets[:]))
+        pairs = [k_low[:, :, h * HALF : (h + 1) * HALF].rearrange("p t n -> p n t") for h in range(2)]
+        nc.vector.tensor_copy(k_grouped[0][:, :, 0:2], pairs[0])
+        nc.scalar.activation(out=k_grouped[1][:, :, 0:2], in_=pairs[1], func=ACT.Copy)
         for h in range(2):
             nc.vector.tensor_copy(k_grouped[h][:, :, 2], k_table[2][:].indirect(offsets[:, h * (HALF // 16) : (h + 1) * (HALF // 16)]))
         k_last = keep.tile([P, T], BF16, name="k_last")
         nc.scalar.activation(out=k_last[:, pieces[0]], in_=k_table[3][:, pieces[0]], func=ACT.Copy)
-        nc.vector.tensor_copy(k_last[:, pieces[1]], k_table[3][:, pieces[1]])
+        shared = slice(1536, 1920)
+        nc.scalar.activation(out=k_last[:, shared], in_=k_table[3][:, shared], func=ACT.Copy)
+        nc.vector.tensor_copy(k_last[:, 1920:3072], k_table[3][:, 1920:3072])
         for piece in pieces[2:4]:
             nc.scalar.activation(out=k_last[:, piece], in_=k_table[3][:, piece], func=ACT.Copy)
         nc.vector.tensor_copy(k_grouped[1][:, :, 3], k_table[3][:].indirect(offsets[:, HALF // 16 : N // 16]))

@@ -20,6 +20,7 @@ AX = mybir.AxisListType
 
 P = 128
 PACK = 4
+RUN16 = 16
 HALF = 512
 
 
@@ -77,27 +78,21 @@ def tile_attend_sink_topk_kernel(tc, qT, kT, vT, vs, sink, offs, out):
 
         vs_picked = keep.tile([P, N], F32, name="vs_picked")
         nc.vector.tensor_copy(vs_picked[:], vs_table[:].indirect(offsets[:]))
+        vs_rows = [keep.tile([P, 2, HALF // 2], F32, name=f"vs_rows{g}") for g in range(2)]
+        laid = [vs_rows[g][:].rearrange("r u (b e) -> r u b e", e=RUN16) for g in range(2)]
+        read = [vs_picked[:, g * HALF : (g + 1) * HALF].rearrange("r (b u e) -> r u b e", u=2, e=RUN16) for g in range(2)]
+        for g in (1, 0):
+            nc.gpsimd.tensor_scalar(out=laid[g], in0=read[g], scalar1=1.0, scalar2=0.0, op0=ALU.mult, op1=ALU.add)
         vcol = keep.tile([P, PACK], F32, name="vcol")
-        for g, first in ((1, 0),):
-            turned = turn_banks.tile([P, PACK, P], F32, name="turned1")
-            for t in range(first, PACK):
-                nc.tensor.transpose(turned[:, t, :], vs_picked[:, g * HALF + t : (g + 1) * HALF : PACK], ident[:])
-            nc.scalar.copy(out=vcol[:, first:PACK], in_=turned[:, first:PACK, 0])
+        turned = turn_banks.tile([P, PACK, P], F32, name="turned1")
+        for t in range(PACK):
+            nc.tensor.transpose(turned[:, t, :], vs_rows[1][:, t // 2, t % 2 : HALF // 2 : 2], ident[:])
+        nc.scalar.copy(out=vcol[:], in_=turned[:, :, 0])
         vs_bank = turn_banks.tile([P, 2, 2, P], F32, name="turned3")
         for u in range(2):
             for w in range(2):
                 nc.tensor.transpose(vs_bank[:, w, u, :], vcol[:, 2 * u + w : 2 * u + w + 1].to_broadcast([P, P]), ident[:])
         SHARE = 64
-        vs_rows = [keep.tile([P, 2 - g, (P, SHARE)[g], 2], F32, name=f"vs_rows{g}") for g in range(2)]
-        for g in range(2):
-            nc.gpsimd.tensor_scalar(
-                out=vs_rows[g][:],
-                in0=vs_picked[:, g * HALF : (g + 1) * HALF].rearrange("r (s u w) -> r u s w", u=2, w=2)[:, 0 : 2 - g, 0 : (P, SHARE)[g], :],
-                scalar1=1.0,
-                scalar2=0.0,
-                op0=ALU.mult,
-                op1=ALU.add,
-            )
 
         for t in range(2):
             nc.vector.tensor_copy(k_low[:, t, :], k_table[t][:].indirect(offsets[:]))
@@ -166,11 +161,12 @@ def tile_attend_sink_topk_kernel(tc, qT, kT, vT, vs, sink, offs, out):
                         stop=True,
                     )
 
-        low = {(j, h): keep.tile([P, 1], F32, name=f"low{j}{h}") for j in range(2) for h in range(2)}
+        lows = [keep.tile([P, 2], F32, name=f"low{j}") for j in range(2)]
+        low = {(j, h): lows[j][:, h : h + 1] for j in range(2) for h in range(2)}
         for h in (1, 0):
-            nc.vector.tensor_reduce(out=low[0, h][:], in_=scores[0, h][:], axis=AX.X, op=ALU.min)
+            nc.vector.tensor_reduce(out=low[0, h], in_=scores[0, h][:], axis=AX.X, op=ALU.min)
         v_first = keep.tile([P, 2 * HALF], BF16, name="v_first")
-        nc.vector.tensor_reduce(out=low[1, 1][:], in_=scores[1, 1][:], axis=AX.X, op=ALU.min)
+        nc.vector.tensor_reduce(out=low[1, 1], in_=scores[1, 1][:], axis=AX.X, op=ALU.min)
         nc.vector.tensor_scalar(
             out=v_first[:].bitcast(F32),
             in0=scores[1, 0][:],
@@ -178,18 +174,18 @@ def tile_attend_sink_topk_kernel(tc, qT, kT, vT, vs, sink, offs, out):
             scalar2=nsink[:, 1:2],
             op0=ALU.mult,
             op1=ALU.min,
-            accum_out=low[1, 0][:],
+            accum_out=low[1, 0],
         )
         joined = keep.tile([P, 1], F32, name="joined")
-        nc.gpsimd.tensor_scalar(out=joined[:], in0=low[0, 0][:], scalar1=low[0, 1][:], scalar2=nsink[:, 0:1], op0=ALU.min, op1=ALU.min)
+        nc.gpsimd.tensor_scalar(out=joined[:], in0=low[0, 0], scalar1=low[0, 1], scalar2=nsink[:, 0:1], op0=ALU.min, op1=ALU.min)
         lowest = [joined, placed.tile([P, 1], F32, name="joined1", align_bytes=64, offset=4 * T)]
 
         v_second = keep.tile([P, HALF], BF16, name="v_second")
         v_picked = [v_first[:, 0:HALF], v_second[:]]
-        nc.vector.tensor_tensor(lowest[1][:], low[1, 0][:], low[1, 1][:], ALU.min)
+        nc.vector.tensor_reduce(out=lowest[1][:], in_=lows[1][:], axis=AX.X, op=ALU.min)
         for g in range(2):
             nc.vector.tensor_copy(
-                v_picked[g].rearrange("p (u s w) -> p s u w", u=2, w=2),
+                v_picked[g].rearrange("p (u b e) -> p b u e", u=2, e=RUN16),
                 v_table[:].indirect(offsets[:, g * (HALF // 16) : (g + 1) * (HALF // 16)]),
             )
 
@@ -197,13 +193,10 @@ def tile_attend_sink_topk_kernel(tc, qT, kT, vT, vs, sink, offs, out):
         probs = {}
         for j in range(2):
             for h in range(2):
-                probs[j, h] = keep.tile([P, PACK, P], F32, name=f"probs{j}{h}")
-                if (j, h) != (0, 1):
-                    laid = probs[j, h][:].rearrange("p t s -> p (t s)").rearrange("p (u s w) -> p u s w", u=2, w=2)
-                    read = scores[j, h][:].rearrange("p (s u w) -> p u s w", u=2, w=2)
-                else:
-                    laid = probs[j, h][:]
-                    read = scores[j, h][:].rearrange("p (s t) -> p t s", t=PACK)
+                probs[j, h] = keep.tile([P, HALF], F32, name=f"probs{j}{h}")
+                order = "p (u w b r) -> p u b r w" if (j, h) == (0, 1) else "p (u b r w) -> p u b r w"
+                laid = probs[j, h][:].rearrange(order, u=2, w=2, r=RUN16 // 2)
+                read = scores[j, h][:].rearrange("p (b u r w) -> p u b r w", u=2, w=2, r=RUN16 // 2)
                 nc.scalar.activation(
                     out=laid,
                     in_=read,
@@ -225,11 +218,11 @@ def tile_attend_sink_topk_kernel(tc, qT, kT, vT, vs, sink, offs, out):
         for j in range(2):
             nc.gpsimd.tensor_tensor(
                 w_pairs[j][:],
-                probs[j, 0][:].rearrange("p t s -> p (t s)"),
-                vs_rows[0][:].rearrange("p u s w -> p (u s w)"),
+                probs[j, 0][:],
+                vs_rows[0][:].rearrange("p u x -> p (u x)"),
                 ALU.mult,
             )
-        last = probs[1, 1][:].rearrange("p t s -> p (t s)").rearrange("p (x w) -> p x w", w=2)
+        last = probs[1, 1][:].rearrange("p (x w) -> p x w", w=2)
         w_last = placed.tile([P, 2 * P, 2], BF16, name="w_last", align_bytes=64, offset=0)
 
         vw_grouped = [
@@ -240,10 +233,10 @@ def tile_attend_sink_topk_kernel(tc, qT, kT, vT, vs, sink, offs, out):
         nc.vector.tensor_tensor(
             w_last[:, SHARE:, :], last[:, SHARE:, :], vs_bank[:].rearrange("p w u s -> p (u s) w")[:, SHARE:, :], ALU.mult
         )
-        nc.gpsimd.tensor_tensor(w_last[:, 0:SHARE, :], last[:, 0:SHARE, :], vs_rows[1][:, 0, :, :], ALU.mult)
+        nc.gpsimd.tensor_tensor(w_last[:, 0:SHARE, :], last[:, 0:SHARE, :], vs_rows[1][:, 0, 0 : 2 * SHARE].rearrange("p (x w) -> p x w", w=2), ALU.mult)
         turned = turn_banks.tile([P, PACK, P], F32, name="turned0")
         for t in range(PACK):
-            nc.tensor.transpose(turned[:, t, :], probs[0, 1][:, t, :], ident[:])
+            nc.tensor.transpose(turned[:, t, :], probs[0, 1][:, t * P : (t + 1) * P], ident[:])
         nc.vector.tensor_tensor(
             vw_grouped[1][:, 1, :, :], turned[:].rearrange("p t q -> p q t"), vcol[:].unsqueeze(1).to_broadcast([P, P, PACK]), ALU.mult
         )

@@ -59,7 +59,7 @@ def tile_attend_sink_topk_kernel(tc, qT, kT, vT, vs, sink, offs, out):
         ident = keep.tile([P, P], F32, name="ident")
         make_identity(nc, ident[:])
 
-        nsink = keep.tile([P, 2], F32, name="nsink")
+        lows = [keep.tile([P, 3], F32, name=f"low{j}") for j in range(2)]
 
         vs_table = placed.tile([P, T], F32, name="vs_table", align_bytes=64, offset=5 * T)
         for b in range(RUN // PACK):
@@ -71,7 +71,8 @@ def tile_attend_sink_topk_kernel(tc, qT, kT, vT, vs, sink, offs, out):
 
         turned = turn_banks.tile([P, P], F32, name="turned0")
         nc.tensor.transpose(turned[:], sink_rows[:], ident[:])
-        nc.scalar.activation(out=nsink[:], in_=turned[:, 0:2], func=ACT.Copy, scale=-1.0)
+        for j in range(2):
+            nc.scalar.activation(out=lows[j][:, 2:3], in_=turned[:, j : j + 1], func=ACT.Copy, scale=-1.0)
 
         k_grouped = [keep.tile([P, HALF, PACK], BF16, name=f"k_grouped{h}", align_bytes=64) for h in range(2)]
         k_low = placed.tile([P, 2, N], F32, name="k_low", align_bytes=64, offset=5 * T)
@@ -161,27 +162,17 @@ def tile_attend_sink_topk_kernel(tc, qT, kT, vT, vs, sink, offs, out):
                         stop=True,
                     )
 
-        lows = [keep.tile([P, 2], F32, name=f"low{j}") for j in range(2)]
         low = {(j, h): lows[j][:, h : h + 1] for j in range(2) for h in range(2)}
-        for h in (1, 0):
-            nc.vector.tensor_reduce(out=low[0, h], in_=scores[0, h][:], axis=AX.X, op=ALU.min)
-        v_first = keep.tile([P, 2 * HALF], BF16, name="v_first")
-        nc.vector.tensor_reduce(out=low[1, 1], in_=scores[1, 1][:], axis=AX.X, op=ALU.min)
-        nc.vector.tensor_scalar(
-            out=v_first[:].bitcast(F32),
-            in0=scores[1, 0][:],
-            scalar1=1.0,
-            scalar2=nsink[:, 1:2],
-            op0=ALU.mult,
-            op1=ALU.min,
-            accum_out=low[1, 0],
-        )
+        for j in range(2):
+            for h in (1, 0):
+                nc.vector.tensor_reduce(out=low[j, h], in_=scores[j, h][:], axis=AX.X, op=ALU.min)
+        v_first = placed.tile([P, HALF], BF16, name="v_first", align_bytes=64, offset=9 * T)
         joined = keep.tile([P, 1], F32, name="joined")
-        nc.gpsimd.tensor_scalar(out=joined[:], in0=low[0, 0], scalar1=low[0, 1], scalar2=nsink[:, 0:1], op0=ALU.min, op1=ALU.min)
+        nc.gpsimd.tensor_scalar(out=joined[:], in0=low[0, 0], scalar1=low[0, 1], scalar2=lows[0][:, 2:3], op0=ALU.min, op1=ALU.min)
         lowest = [joined, placed.tile([P, 1], F32, name="joined1", align_bytes=64, offset=4 * T)]
 
         v_second = keep.tile([P, HALF], BF16, name="v_second")
-        v_picked = [v_first[:, 0:HALF], v_second[:]]
+        v_picked = [v_first[:], v_second[:]]
         nc.vector.tensor_reduce(out=lowest[1][:], in_=lows[1][:], axis=AX.X, op=ALU.min)
         for g in range(2):
             nc.vector.tensor_copy(
@@ -207,7 +198,7 @@ def tile_attend_sink_topk_kernel(tc, qT, kT, vT, vs, sink, offs, out):
                 )
 
         for j in range(2):
-            nc.scalar.activation(out=sums[:, j, 2:3], in_=nsink[:, j : j + 1], func=ACT.Exp, bias=lowest[j][:], scale=-1.0)
+            nc.scalar.activation(out=sums[:, j, 2:3], in_=lows[j][:, 2:3], func=ACT.Exp, bias=lowest[j][:], scale=-1.0)
         total = keep.tile([P, 2], F32, name="total")
         summed = keep.tile([P, 2, 3], F32, name="summed")
         for j in range(2):
@@ -223,7 +214,7 @@ def tile_attend_sink_topk_kernel(tc, qT, kT, vT, vs, sink, offs, out):
                 ALU.mult,
             )
         last = probs[1, 1][:].rearrange("p (x w) -> p x w", w=2)
-        w_last = placed.tile([P, 2 * P, 2], BF16, name="w_last", align_bytes=64, offset=0)
+        w_last = placed.tile([P, 2 * P, 2], BF16, name="w_last", align_bytes=64, offset=9 * T)
 
         vw_grouped = [
             keep.tile([P, 2, P, PACK], BF16, name="vw_grouped0", align_bytes=64),

@@ -20,8 +20,19 @@ AX = mybir.AxisListType
 
 P = 128
 PACK = 4
-RUN16 = 16
 HALF = 512
+QUARTER = HALF // 2
+RUN = 16
+PER_ROW = T // P
+LIST_HALF = HALF // 16
+
+PIECES = [slice(0, 1536), slice(1536, 3072), slice(3072, 3584), slice(3584, T)]
+CAST_SHARE = 384
+
+AT_VALUES = 0
+AT_LOWEST = 4 * T
+AT_VS = 5 * T
+AT_FIRST = 9 * T
 
 
 def tile_attend_sink_topk_kernel(tc, qT, kT, vT, vs, sink, offs, out):
@@ -33,10 +44,10 @@ def tile_attend_sink_topk_kernel(tc, qT, kT, vT, vs, sink, offs, out):
         score_banks = ctx.enter_context(tc.psum_pool(name="score_banks", bufs=1))
         turn_banks = ctx.enter_context(tc.psum_pool(name="turn_banks", bufs=1))
 
+
         offsets = lists.tile([P, N // 16], U16, name="offsets")
-        RUN = T // P
-        vs_runs = keep.tile([P, RUN], F32, name="vs_runs")
-        nc.sync.dma_start(out=vs_runs[:], in_=vs[0].rearrange("(p c) -> p c", c=RUN))
+        vs_runs = keep.tile([P, PER_ROW], F32, name="vs_runs")
+        nc.sync.dma_start(out=vs_runs[:], in_=vs[0].rearrange("(p c) -> p c", c=PER_ROW))
         sink_rows = keep.tile([P, P], F32, name="sink_rows")
         nc.gpsimd.memset(sink_rows[:], 0.0)
         nc.scalar.dma_start(out=sink_rows[0:2, :], in_=sink[0].rearrange("(j m) x -> j (m x)", j=2))
@@ -47,13 +58,12 @@ def tile_attend_sink_topk_kernel(tc, qT, kT, vT, vs, sink, offs, out):
             nc.sync.dma_start(out=k_table[t][:], in_=k_rows[:, t, :])
             if t == 0:
                 nc.sync.dma_start(offsets[:], offs)
-        pieces = [slice(0, 1536), slice(1536, 3072), slice(3072, 3584), slice(3584, T)]
-        for piece in pieces:
+        for piece in PIECES:
             nc.sync.dma_start(out=k_table[3][:, piece], in_=k_rows[:, 3, piece])
         q_raw = keep.tile([P, PACK, NQ], F32, name="q_raw")
         for u in range(2):
             nc.sync.dma_start(out=q_raw[:, 2 * u : 2 * u + 2, :], in_=qT[0].rearrange("(p t) q -> p t q", t=PACK)[:, 2 * u : 2 * u + 2, :])
-        v_table = placed.tile([P, T], F32, name="v_table", align_bytes=64, offset=0)
+        v_table = placed.tile([P, T], F32, name="v_table", align_bytes=64, offset=AT_VALUES)
         nc.sync.dma_start(out=v_table[:], in_=vT)
 
         ident = keep.tile([P, P], F32, name="ident")
@@ -61,13 +71,13 @@ def tile_attend_sink_topk_kernel(tc, qT, kT, vT, vs, sink, offs, out):
 
         lows = [keep.tile([P, 3], F32, name=f"low{j}") for j in range(2)]
 
-        vs_table = placed.tile([P, T], F32, name="vs_table", align_bytes=64, offset=5 * T)
-        for b in range(RUN // PACK):
+        vs_table = placed.tile([P, T], F32, name="vs_table", align_bytes=64, offset=AT_VS)
+        for b in range(PER_ROW // PACK):
             turned = turn_banks.tile([P, PACK, P], F32, name=f"turned{b % 4}")
             for c in range(PACK):
                 nc.tensor.transpose(turned[:, c, :], vs_runs[:, b * PACK + c : b * PACK + c + 1].to_broadcast([P, P]), ident[:])
             leave = nc.vector.tensor_copy if b % 2 else nc.scalar.copy
-            leave(vs_table[:].rearrange("r (p b c) -> r b p c", c=PACK, b=RUN // PACK)[:, b, :, :], turned[:].rearrange("r c p -> r p c"))
+            leave(vs_table[:].rearrange("r (p b c) -> r b p c", c=PACK, b=PER_ROW // PACK)[:, b, :, :], turned[:].rearrange("r c p -> r p c"))
 
         turned = turn_banks.tile([P, P], F32, name="turned0")
         nc.tensor.transpose(turned[:], sink_rows[:], ident[:])
@@ -75,25 +85,25 @@ def tile_attend_sink_topk_kernel(tc, qT, kT, vT, vs, sink, offs, out):
             nc.scalar.activation(out=lows[j][:, 2:3], in_=turned[:, j : j + 1], func=ACT.Copy, scale=-1.0)
 
         k_grouped = [keep.tile([P, HALF, PACK], BF16, name=f"k_grouped{h}", align_bytes=64) for h in range(2)]
-        k_low = placed.tile([P, 2, N], F32, name="k_low", align_bytes=64, offset=5 * T)
+        k_low = placed.tile([P, 2, N], F32, name="k_low", align_bytes=64, offset=AT_VS)
 
         vs_picked = keep.tile([P, N], F32, name="vs_picked")
         nc.vector.tensor_copy(vs_picked[:], vs_table[:].indirect(offsets[:]))
-        vs_rows = [keep.tile([P, 2, HALF // 2], F32, name=f"vs_rows{g}") for g in range(2)]
-        laid = [vs_rows[g][:].rearrange("r u (b e) -> r u b e", e=RUN16) for g in range(2)]
-        read = [vs_picked[:, g * HALF : (g + 1) * HALF].rearrange("r (b u e) -> r u b e", u=2, e=RUN16) for g in range(2)]
+        vs_rows = [keep.tile([P, 2, QUARTER], F32, name=f"vs_rows{g}") for g in range(2)]
         for g in (1, 0):
-            nc.gpsimd.tensor_scalar(out=laid[g], in0=read[g], scalar1=1.0, scalar2=0.0, op0=ALU.mult, op1=ALU.add)
-        vcol = keep.tile([P, PACK], F32, name="vcol")
+            nc.gpsimd.tensor_scalar(
+                out=vs_rows[g][:].rearrange("r u (b e) -> r u b e", e=RUN),
+                in0=vs_picked[:, g * HALF : (g + 1) * HALF].rearrange("r (b u e) -> r u b e", u=2, e=RUN),
+                scalar1=1.0,
+                scalar2=0.0,
+                op0=ALU.mult,
+                op1=ALU.add,
+            )
+        vs_column = keep.tile([P, PACK], F32, name="vs_column")
         turned = turn_banks.tile([P, PACK, P], F32, name="turned1")
         for t in range(PACK):
-            nc.tensor.transpose(turned[:, t, :], vs_rows[1][:, t // 2, t % 2 : HALF // 2 : 2], ident[:])
-        nc.scalar.copy(out=vcol[:], in_=turned[:, :, 0])
-        vs_bank = turn_banks.tile([P, 2, 2, P], F32, name="turned3")
-        for u in range(2):
-            for w in range(2):
-                nc.tensor.transpose(vs_bank[:, w, u, :], vcol[:, 2 * u + w : 2 * u + w + 1].to_broadcast([P, P]), ident[:])
-        SHARE = 64
+            nc.tensor.transpose(turned[:, t, :], vs_rows[1][:, t // 2, t % 2 : QUARTER : 2], ident[:])
+        nc.scalar.copy(out=vs_column[:], in_=turned[:, :, 0])
 
         for t in range(2):
             nc.vector.tensor_copy(k_low[:, t, :], k_table[t][:].indirect(offsets[:]))
@@ -101,46 +111,46 @@ def tile_attend_sink_topk_kernel(tc, qT, kT, vT, vs, sink, offs, out):
         nc.vector.tensor_copy(k_grouped[0][:, :, 0:2], pairs[0])
         nc.scalar.activation(out=k_grouped[1][:, :, 0:2], in_=pairs[1], func=ACT.Copy)
         for h in range(2):
-            nc.vector.tensor_copy(k_grouped[h][:, :, 2], k_table[2][:].indirect(offsets[:, h * (HALF // 16) : (h + 1) * (HALF // 16)]))
+            nc.vector.tensor_copy(k_grouped[h][:, :, 2], k_table[2][:].indirect(offsets[:, h * LIST_HALF : (h + 1) * LIST_HALF]))
         k_last = keep.tile([P, T], BF16, name="k_last")
-        nc.scalar.activation(out=k_last[:, pieces[0]], in_=k_table[3][:, pieces[0]], func=ACT.Copy)
-        shared = slice(1536, 1920)
-        nc.scalar.activation(out=k_last[:, shared], in_=k_table[3][:, shared], func=ACT.Copy)
-        nc.vector.tensor_copy(k_last[:, 1920:3072], k_table[3][:, 1920:3072])
-        for piece in pieces[2:4]:
-            nc.scalar.activation(out=k_last[:, piece], in_=k_table[3][:, piece], func=ACT.Copy)
-        nc.vector.tensor_copy(k_grouped[1][:, :, 3], k_table[3][:].indirect(offsets[:, HALF // 16 : N // 16]))
-        nc.scalar.activation(out=k_grouped[0][:, :, 3], in_=k_last[:].indirect(offsets[:, 0 : HALF // 16]), func=ACT.Copy)
+        on_scalar = slice(PIECES[1].start, PIECES[1].start + CAST_SHARE)
+        on_vector = slice(on_scalar.stop, PIECES[1].stop)
+        for cols in (PIECES[0], on_scalar):
+            nc.scalar.activation(out=k_last[:, cols], in_=k_table[3][:, cols], func=ACT.Copy)
+        nc.vector.tensor_copy(k_last[:, on_vector], k_table[3][:, on_vector])
+        for cols in PIECES[2:]:
+            nc.scalar.activation(out=k_last[:, cols], in_=k_table[3][:, cols], func=ACT.Copy)
+        nc.vector.tensor_copy(k_grouped[1][:, :, 3], k_table[3][:].indirect(offsets[:, LIST_HALF : 2 * LIST_HALF]))
+        nc.scalar.activation(out=k_grouped[0][:, :, 3], in_=k_last[:].indirect(offsets[:, 0:LIST_HALF]), func=ACT.Copy)
 
         q_grouped = [keep.tile([P, P, PACK], BF16, name=f"q_grouped{j}", align_bytes=64) for j in range(2)]
-        signs = keep.tile([P, 2], F32, name="signs", align_bytes=64)
-        nc.gpsimd.memset(signs[:, 0:1], -1.0)
-        nc.gpsimd.memset(signs[:, 1:2], 0.0)
+        factors = keep.tile([P, 2], F32, name="factors", align_bytes=64)
+        nc.gpsimd.memset(factors[:, 0:1], -1.0)
+        nc.gpsimd.memset(factors[:, 1:2], 0.0)
         for u in range(2):
             nc.gpsimd.tensor_scalar(
                 out=q_grouped[0][:, :, 2 * u : 2 * u + 2],
                 in0=q_raw[:, 2 * u : 2 * u + 2, 0:P].rearrange("p t m -> p m t"),
-                scalar1=signs[:, 0:1],
-                scalar2=signs[:, 1:2],
+                scalar1=factors[:, 0:1],
+                scalar2=factors[:, 1:2],
                 op0=ALU.mult,
                 op1=ALU.add,
             )
         nc.scalar.activation(out=q_grouped[1][:], in_=q_raw[:, :, P:NQ].rearrange("p t m -> p m t"), func=ACT.Copy, scale=-1.0)
         q_codes = [keep.tile([P, P], U32, name=f"q_codes{j}", align_bytes=64) for j in range(2)]
         q_scales = [keep.tile([P, P], U8, name=f"q_scales{j}", align_bytes=64) for j in range(2)]
-        k_scales = keep.tile([P, 2, HALF], U8, name="signs", align_bytes=64)
+        k_scales = keep.tile([P, 2, HALF], U8, name="factors", align_bytes=64)
         k_codes = [keep.tile([P, HALF], U32, name=f"k_codes{h}", align_bytes=64) for h in range(2)]
-        QUARTER = HALF // 2
 
         def quantise_q(j):
             nc.vector.quantize_mx(
                 out=q_codes[j][:].bitcast(FP8X4), scales=q_scales[j][:], in_=q_grouped[j][:].rearrange("p n t -> p (n t)")
             )
 
+        quarters = [slice(0, QUARTER), slice(QUARTER, HALF)]
         quantise_q(0)
         for h in (1, 0):
-            for c in range(2):
-                cols = slice(c * QUARTER, (c + 1) * QUARTER)
+            for cols in quarters:
                 nc.vector.quantize_mx(
                     out=k_codes[h][:, cols].bitcast(FP8X4),
                     scales=k_scales[:, h, cols],
@@ -151,7 +161,7 @@ def tile_attend_sink_topk_kernel(tc, qT, kT, vT, vs, sink, offs, out):
         for j in range(2):
             for h in (1, 0):
                 scores[j, h] = score_banks.tile([P, HALF], F32, name=f"score{j}{h}")
-                for cols in ([slice(0, HALF)] if j else [slice(0, QUARTER), slice(QUARTER, HALF)]):
+                for cols in ([slice(0, HALF)] if j else quarters):
                     nc.tensor.matmul_mx(
                         out=scores[j, h][:, cols],
                         lhsT=q_codes[j][:].bitcast(FP8X4),
@@ -162,22 +172,22 @@ def tile_attend_sink_topk_kernel(tc, qT, kT, vT, vs, sink, offs, out):
                         stop=True,
                     )
 
-        low = {(j, h): lows[j][:, h : h + 1] for j in range(2) for h in range(2)}
         for j in range(2):
             for h in (1, 0):
-                nc.vector.tensor_reduce(out=low[j, h], in_=scores[j, h][:], axis=AX.X, op=ALU.min)
-        v_first = placed.tile([P, HALF], BF16, name="v_first", align_bytes=64, offset=9 * T)
-        joined = keep.tile([P, 1], F32, name="joined")
-        nc.gpsimd.tensor_scalar(out=joined[:], in0=low[0, 0], scalar1=low[0, 1], scalar2=lows[0][:, 2:3], op0=ALU.min, op1=ALU.min)
-        lowest = [joined, placed.tile([P, 1], F32, name="joined1", align_bytes=64, offset=4 * T)]
-
-        v_second = keep.tile([P, HALF], BF16, name="v_second")
-        v_picked = [v_first[:], v_second[:]]
+                nc.vector.tensor_reduce(out=lows[j][:, h : h + 1], in_=scores[j, h][:], axis=AX.X, op=ALU.min)
+        v_first = placed.tile([P, HALF], BF16, name="v_first", align_bytes=64, offset=AT_FIRST)
+        lowest_first = keep.tile([P, 1], F32, name="lowest0")
+        nc.gpsimd.tensor_scalar(
+            out=lowest_first[:], in0=lows[0][:, 0:1], scalar1=lows[0][:, 1:2], scalar2=lows[0][:, 2:3], op0=ALU.min, op1=ALU.min
+        )
+        lowest = [lowest_first, placed.tile([P, 1], F32, name="lowest1", align_bytes=64, offset=AT_LOWEST)]
+        v_picked = [v_first, keep.tile([P, HALF], BF16, name="v_second")]
         nc.vector.tensor_reduce(out=lowest[1][:], in_=lows[1][:], axis=AX.X, op=ALU.min)
+
         for g in range(2):
             nc.vector.tensor_copy(
-                v_picked[g].rearrange("p (u b e) -> p b u e", u=2, e=RUN16),
-                v_table[:].indirect(offsets[:, g * (HALF // 16) : (g + 1) * (HALF // 16)]),
+                v_picked[g][:].rearrange("p (u b e) -> p b u e", u=2, e=RUN),
+                v_table[:].indirect(offsets[:, g * LIST_HALF : (g + 1) * LIST_HALF]),
             )
 
         sums = keep.tile([P, 2, 3], F32, name="sums")
@@ -185,73 +195,61 @@ def tile_attend_sink_topk_kernel(tc, qT, kT, vT, vs, sink, offs, out):
         for j in range(2):
             for h in range(2):
                 probs[j, h] = keep.tile([P, HALF], F32, name=f"probs{j}{h}")
-                order = "p (u w b r) -> p u b r w" if (j, h) == (0, 1) else "p (u b r w) -> p u b r w"
-                laid = probs[j, h][:].rearrange(order, u=2, w=2, r=RUN16 // 2)
-                read = scores[j, h][:].rearrange("p (b u r w) -> p u b r w", u=2, w=2, r=RUN16 // 2)
+                layout = "p (u w b r) -> p u b r w" if h else "p (u b r w) -> p u b r w"
                 nc.scalar.activation(
-                    out=laid,
-                    in_=read,
+                    out=probs[j, h][:].rearrange(layout, u=2, w=2, r=RUN // 2),
+                    in_=scores[j, h][:].rearrange("p (b u r w) -> p u b r w", u=2, w=2, r=RUN // 2),
                     func=ACT.Exp,
                     bias=lowest[j][:],
                     scale=-1.0,
                     accum_out=sums[:, j, h : h + 1],
                 )
-
         for j in range(2):
             nc.scalar.activation(out=sums[:, j, 2:3], in_=lows[j][:, 2:3], func=ACT.Exp, bias=lowest[j][:], scale=-1.0)
         total = keep.tile([P, 2], F32, name="total")
-        summed = keep.tile([P, 2, 3], F32, name="summed")
+        unread = keep.tile([P, 2, 3], F32, name="unread")
         for j in range(2):
-            nc.scalar.activation(out=summed[:, j, :], in_=sums[:, j, :], func=ACT.Copy, accum_out=total[:, j : j + 1])
-        share = keep.tile([P, 2], F32, name="share")
+            nc.scalar.activation(out=unread[:, j, :], in_=sums[:, j, :], func=ACT.Copy, accum_out=total[:, j : j + 1])
+        inverse = keep.tile([P, 2], F32, name="inverse")
 
-        w_pairs = {j: keep.tile([P, HALF], BF16, name=f"w_pairs{j}") for j in range(2)}
+        w_pairs = [keep.tile([P, HALF], BF16, name=f"w_pairs{j}") for j in range(2)]
         for j in range(2):
-            nc.gpsimd.tensor_tensor(
-                w_pairs[j][:],
-                probs[j, 0][:],
-                vs_rows[0][:].rearrange("p u x -> p (u x)"),
-                ALU.mult,
-            )
-        last = probs[1, 1][:].rearrange("p (x w) -> p x w", w=2)
-        w_last = placed.tile([P, 2 * P, 2], BF16, name="w_last", align_bytes=64, offset=9 * T)
+            nc.gpsimd.tensor_tensor(w_pairs[j][:], probs[j, 0][:], vs_rows[0][:].rearrange("p u x -> p (u x)"), ALU.mult)
 
         vw_grouped = [
             keep.tile([P, 2, P, PACK], BF16, name="vw_grouped0", align_bytes=64),
-            placed.tile([P, 2, P, PACK], BF16, name="vw_grouped1", align_bytes=64, offset=4 * T),
+            placed.tile([P, 2, P, PACK], BF16, name="vw_grouped1", align_bytes=64, offset=AT_LOWEST),
         ]
-        late = [keep.tile([P, P, PACK], BF16, name=f"w1{g}", align_bytes=64) for g in range(2)]
-        nc.vector.tensor_tensor(
-            w_last[:, SHARE:, :], last[:, SHARE:, :], vs_bank[:].rearrange("p w u s -> p (u s) w")[:, SHARE:, :], ALU.mult
-        )
-        nc.gpsimd.tensor_tensor(w_last[:, 0:SHARE, :], last[:, 0:SHARE, :], vs_rows[1][:, 0, 0 : 2 * SHARE].rearrange("p (x w) -> p x w", w=2), ALU.mult)
-        turned = turn_banks.tile([P, PACK, P], F32, name="turned0")
-        for t in range(PACK):
-            nc.tensor.transpose(turned[:, t, :], probs[0, 1][:, t * P : (t + 1) * P], ident[:])
-        nc.vector.tensor_tensor(
-            vw_grouped[1][:, 1, :, :], turned[:].rearrange("p t q -> p q t"), vcol[:].unsqueeze(1).to_broadcast([P, P, PACK]), ALU.mult
-        )
+        w_grouped = [
+            keep.tile([P, P, PACK], BF16, name="w_grouped0", align_bytes=64),
+            placed.tile([P, P, PACK], BF16, name="w_grouped1", align_bytes=64, offset=AT_FIRST),
+        ]
+        for j, (target, bank) in enumerate(((vw_grouped[1][:, 1, :, :], "turned0"), (w_grouped[1][:], "turned3"))):
+            turned = turn_banks.tile([P, PACK, P], F32, name=bank)
+            for t in range(PACK):
+                nc.tensor.transpose(turned[:, t, :], probs[j, 1][:, t * P : (t + 1) * P], ident[:])
+            nc.vector.tensor_tensor(
+                target, turned[:].rearrange("p t q -> p q t"), vs_column[:].unsqueeze(1).to_broadcast([P, P, PACK]), ALU.mult
+            )
 
-        nc.vector.reciprocal(share[:], total[:])
+        nc.vector.reciprocal(inverse[:], total[:])
 
-        def turn(sources, bank, grouped, order=(0, 1)):
+        def turn(sources, bank, grouped):
             for a, source in enumerate(sources):
-                for u in order:
+                for u in range(2):
                     nc.tensor.transpose(bank[:, a, u, :], source.bitcast(F32)[:, u * P : (u + 1) * P], ident[:])
             nc.scalar.copy(
                 out=grouped.bitcast(F32).rearrange("p (a e u) -> p a e u", a=len(sources), u=2),
                 in_=bank[:].rearrange("p a u e -> p a e u"),
             )
 
-        turn([v_picked[0], w_pairs[0][:]], turn_banks.tile([P, 2, 2, P], F32, name="turned1"), vw_grouped[0][:].rearrange("p a e t -> p (a e t)"))
-        turn([v_picked[1]], turn_banks.tile([P, 1, 2, P], F32, name="turned2"), vw_grouped[1][:, 0, :, :].rearrange("p e t -> p (e t)"))
-        turn([w_pairs[1][:]], score_banks.tile([P, 1, 2, P], F32, name="score10"), late[0][:].rearrange("p e t -> p (e t)"))
         turn(
-            [w_last[:].rearrange("p x w -> p (x w)")],
-            turn_banks.tile([P, 1, 2, P], F32, name="turned3"),
-            late[1][:].rearrange("p e t -> p (e t)"),
-            (1, 0),
+            [v_picked[0][:], w_pairs[0][:]],
+            turn_banks.tile([P, 2, 2, P], F32, name="turned1"),
+            vw_grouped[0][:].rearrange("p a e t -> p (a e t)"),
         )
+        turn([v_picked[1][:]], turn_banks.tile([P, 1, 2, P], F32, name="turned2"), vw_grouped[1][:, 0, :, :].rearrange("p e t -> p (e t)"))
+        turn([w_pairs[1][:]], score_banks.tile([P, 1, 2, P], F32, name="score10"), w_grouped[0][:].rearrange("p e t -> p (e t)"))
 
         vw_codes = [keep.tile([P, 2, P], U32, name=f"vw_codes{g}", align_bytes=64) for g in range(2)]
         vw_scales = [keep.tile([P, 2, P], U8, name=f"vw_scales{g}", align_bytes=64) for g in range(2)]
@@ -263,20 +261,20 @@ def tile_attend_sink_topk_kernel(tc, qT, kT, vT, vs, sink, offs, out):
                 scales=vw_scales[g][:].rearrange("p a e -> p (a e)"),
                 in_=vw_grouped[g][:].rearrange("p a e t -> p (a e t)"),
             )
-        for g in range(2):
-            nc.vector.quantize_mx(out=w_codes[g][:].bitcast(FP8X4), scales=w_scales[g][:], in_=late[g][:].rearrange("p q t -> p (q t)"))
+        for g in (1, 0):
+            nc.vector.quantize_mx(out=w_codes[g][:].bitcast(FP8X4), scales=w_scales[g][:], in_=w_grouped[g][:].rearrange("p q t -> p (q t)"))
         for j in range(2):
             acc = score_banks.tile([P, DV], F32, name=f"score0{j}")
-            for g in range(2):
+            for n, g in enumerate((1, 0) if j else (0, 1)):
                 nc.tensor.matmul_mx(
                     out=acc[:],
                     lhsT=(w_codes[g][:] if j else vw_codes[g][:, 1, :]).bitcast(FP8X4),
                     lhsT_scale=w_scales[g][:] if j else vw_scales[g][:, 1, :],
                     rhs=vw_codes[g][:, 0, :].bitcast(FP8X4),
                     rhs_scale=vw_scales[g][:, 0, :],
-                    start=(g == 0),
-                    stop=(g == 1),
+                    start=(n == 0),
+                    stop=(n == 1),
                 )
             result = keep.tile([P, DV], F32, name=f"result{j}")
-            nc.scalar.activation(out=result[:], in_=acc[:], func=ACT.Copy, scale=share[:, j : j + 1])
+            nc.scalar.activation(out=result[:], in_=acc[:], func=ACT.Copy, scale=inverse[:, j : j + 1])
             nc.sync.dma_start(out=out[0][j * P : (j + 1) * P, :], in_=result[:])

@@ -29,10 +29,11 @@ LIST_HALF = HALF // 16
 PIECES = [slice(0, 1536), slice(1536, 3072), slice(3072, 3584), slice(3584, T)]
 CAST_SHARE = 384
 
-AT_VALUES = 0
-AT_LOWEST = 4 * T
-AT_VS = 5 * T
-AT_FIRST = 9 * T
+VALUE_SHARE = 256
+
+AT_PROBS = 6 * T
+AT_VS = T
+AT_FIRST = 5 * T
 
 
 def tile_attend_sink_topk_kernel(tc, qT, kT, vT, vs, sink, offs, out):
@@ -63,8 +64,9 @@ def tile_attend_sink_topk_kernel(tc, qT, kT, vT, vs, sink, offs, out):
         q_raw = keep.tile([P, PACK, NQ], F32, name="q_raw")
         for u in range(2):
             nc.sync.dma_start(out=q_raw[:, 2 * u : 2 * u + 2, :], in_=qT[0].rearrange("(p t) q -> p t q", t=PACK)[:, 2 * u : 2 * u + 2, :])
-        v_table = placed.tile([P, T], F32, name="v_table", align_bytes=64, offset=AT_VALUES)
+        v_table = keep.tile([P, T], F32, name="v_table")
         nc.sync.dma_start(out=v_table[:], in_=vT)
+        halves = [offsets[:, h * LIST_HALF : (h + 1) * LIST_HALF] for h in range(2)]
 
         ident = keep.tile([P, P], F32, name="ident")
         make_identity(nc, ident[:])
@@ -89,20 +91,19 @@ def tile_attend_sink_topk_kernel(tc, qT, kT, vT, vs, sink, offs, out):
 
         vs_picked = keep.tile([P, N], F32, name="vs_picked")
         nc.vector.tensor_copy(vs_picked[:], vs_table[:].indirect(offsets[:]))
-        vs_rows = [keep.tile([P, 2, QUARTER], F32, name=f"vs_rows{g}") for g in range(2)]
-        for g in (1, 0):
-            nc.gpsimd.tensor_scalar(
-                out=vs_rows[g][:].rearrange("r u (b e) -> r u b e", e=RUN),
-                in0=vs_picked[:, g * HALF : (g + 1) * HALF].rearrange("r (b u e) -> r u b e", u=2, e=RUN),
-                scalar1=1.0,
-                scalar2=0.0,
-                op0=ALU.mult,
-                op1=ALU.add,
-            )
+        vs_row = keep.tile([P, 2, QUARTER], F32, name="vs_row")
+        nc.gpsimd.tensor_scalar(
+            out=vs_row[:].rearrange("r u (b e) -> r u b e", e=RUN),
+            in0=vs_picked[:, 0:HALF].rearrange("r (b u e) -> r u b e", u=2, e=RUN),
+            scalar1=1.0,
+            scalar2=0.0,
+            op0=ALU.mult,
+            op1=ALU.add,
+        )
         vs_column = keep.tile([P, PACK], F32, name="vs_column")
         turned = turn_banks.tile([P, PACK, P], F32, name="turned1")
         for t in range(PACK):
-            nc.tensor.transpose(turned[:, t, :], vs_rows[1][:, t // 2, t % 2 : QUARTER : 2], ident[:])
+            nc.tensor.transpose(turned[:, t, :], vs_picked[:, HALF + t : N : PACK], ident[:])
         nc.scalar.copy(out=vs_column[:], in_=turned[:, :, 0])
 
         for t in range(2):
@@ -111,7 +112,7 @@ def tile_attend_sink_topk_kernel(tc, qT, kT, vT, vs, sink, offs, out):
         nc.vector.tensor_copy(k_grouped[0][:, :, 0:2], pairs[0])
         nc.scalar.activation(out=k_grouped[1][:, :, 0:2], in_=pairs[1], func=ACT.Copy)
         for h in range(2):
-            nc.vector.tensor_copy(k_grouped[h][:, :, 2], k_table[2][:].indirect(offsets[:, h * LIST_HALF : (h + 1) * LIST_HALF]))
+            nc.vector.tensor_copy(k_grouped[h][:, :, 2], k_table[2][:].indirect(halves[h]))
         k_last = keep.tile([P, T], BF16, name="k_last")
         on_scalar = slice(PIECES[1].start, PIECES[1].start + CAST_SHARE)
         on_vector = slice(on_scalar.stop, PIECES[1].stop)
@@ -120,8 +121,8 @@ def tile_attend_sink_topk_kernel(tc, qT, kT, vT, vs, sink, offs, out):
         nc.vector.tensor_copy(k_last[:, on_vector], k_table[3][:, on_vector])
         for cols in PIECES[2:]:
             nc.scalar.activation(out=k_last[:, cols], in_=k_table[3][:, cols], func=ACT.Copy)
-        nc.vector.tensor_copy(k_grouped[1][:, :, 3], k_table[3][:].indirect(offsets[:, LIST_HALF : 2 * LIST_HALF]))
-        nc.scalar.activation(out=k_grouped[0][:, :, 3], in_=k_last[:].indirect(offsets[:, 0:LIST_HALF]), func=ACT.Copy)
+        nc.vector.tensor_copy(k_grouped[1][:, :, 3], k_table[3][:].indirect(halves[1]))
+        nc.scalar.activation(out=k_grouped[0][:, :, 3], in_=k_last[:].indirect(halves[0]), func=ACT.Copy)
 
         q_grouped = [keep.tile([P, P, PACK], BF16, name=f"q_grouped{j}", align_bytes=64) for j in range(2)]
         factors = keep.tile([P, 2], F32, name="factors", align_bytes=64)
@@ -142,21 +143,15 @@ def tile_attend_sink_topk_kernel(tc, qT, kT, vT, vs, sink, offs, out):
         k_scales = keep.tile([P, 2, HALF], U8, name="factors", align_bytes=64)
         k_codes = [keep.tile([P, HALF], U32, name=f"k_codes{h}", align_bytes=64) for h in range(2)]
 
-        def quantise_q(j):
-            nc.vector.quantize_mx(
-                out=q_codes[j][:].bitcast(FP8X4), scales=q_scales[j][:], in_=q_grouped[j][:].rearrange("p n t -> p (n t)")
-            )
+        def quantise(codes, scales, grouped):
+            nc.vector.quantize_mx(out=codes.bitcast(FP8X4), scales=scales, in_=grouped.rearrange("p n t -> p (n t)"))
 
         quarters = [slice(0, QUARTER), slice(QUARTER, HALF)]
-        quantise_q(0)
+        quantise(q_codes[0][:], q_scales[0][:], q_grouped[0][:])
         for h in (1, 0):
             for cols in quarters:
-                nc.vector.quantize_mx(
-                    out=k_codes[h][:, cols].bitcast(FP8X4),
-                    scales=k_scales[:, h, cols],
-                    in_=k_grouped[h][:, cols, :].rearrange("p n t -> p (n t)"),
-                )
-        quantise_q(1)
+                quantise(k_codes[h][:, cols], k_scales[:, h, cols], k_grouped[h][:, cols, :])
+        quantise(q_codes[1][:], q_scales[1][:], q_grouped[1][:])
         scores = {}
         for j in range(2):
             for h in (1, 0):
@@ -175,103 +170,115 @@ def tile_attend_sink_topk_kernel(tc, qT, kT, vT, vs, sink, offs, out):
         for j in range(2):
             for h in (1, 0):
                 nc.vector.tensor_reduce(out=lows[j][:, h : h + 1], in_=scores[j, h][:], axis=AX.X, op=ALU.min)
-        v_first = placed.tile([P, HALF], BF16, name="v_first", align_bytes=64, offset=AT_FIRST)
-        lowest_first = keep.tile([P, 1], F32, name="lowest0")
+        lowest = [keep.tile([P, 1], F32, name=f"lowest{j}") for j in range(2)]
         nc.gpsimd.tensor_scalar(
-            out=lowest_first[:], in0=lows[0][:, 0:1], scalar1=lows[0][:, 1:2], scalar2=lows[0][:, 2:3], op0=ALU.min, op1=ALU.min
+            out=lowest[0][:], in0=lows[0][:, 0:1], scalar1=lows[0][:, 1:2], scalar2=lows[0][:, 2:3], op0=ALU.min, op1=ALU.min
         )
-        lowest = [lowest_first, placed.tile([P, 1], F32, name="lowest1", align_bytes=64, offset=AT_LOWEST)]
-        v_picked = [v_first, keep.tile([P, HALF], BF16, name="v_second")]
         nc.vector.tensor_reduce(out=lowest[1][:], in_=lows[1][:], axis=AX.X, op=ALU.min)
 
-        for g in range(2):
-            nc.vector.tensor_copy(
-                v_picked[g][:].rearrange("p (u b e) -> p b u e", u=2, e=RUN),
-                v_table[:].indirect(offsets[:, g * LIST_HALF : (g + 1) * LIST_HALF]),
-            )
+        v_picked = [
+            placed.tile([P, HALF], BF16, name="v_first", align_bytes=64, offset=AT_FIRST),
+            keep.tile([P, HALF], BF16, name="v_second"),
+        ]
+        nc.vector.tensor_copy(v_picked[0][:].rearrange("p (u b e) -> p b u e", u=2, e=RUN), v_table[:].indirect(halves[0]))
+        cut = LIST_HALF + VALUE_SHARE // 16
+        nc.vector.tensor_copy(v_picked[1][:, 0:VALUE_SHARE], v_table[:].indirect(offsets[:, LIST_HALF:cut]))
 
         sums = keep.tile([P, 2, 3], F32, name="sums")
         probs = {}
         for j in range(2):
             for h in range(2):
-                probs[j, h] = keep.tile([P, HALF], F32, name=f"probs{j}{h}")
-                layout = "p (u w b r) -> p u b r w" if h else "p (u b r w) -> p u b r w"
-                nc.scalar.activation(
-                    out=probs[j, h][:].rearrange(layout, u=2, w=2, r=RUN // 2),
-                    in_=scores[j, h][:].rearrange("p (b u r w) -> p u b r w", u=2, w=2, r=RUN // 2),
-                    func=ACT.Exp,
-                    bias=lowest[j][:],
-                    scale=-1.0,
-                    accum_out=sums[:, j, h : h + 1],
-                )
-        for j in range(2):
-            nc.scalar.activation(out=sums[:, j, 2:3], in_=lows[j][:, 2:3], func=ACT.Exp, bias=lowest[j][:], scale=-1.0)
+                if j or h:
+                    probs[j, h] = keep.tile([P, HALF], F32, name=f"probs{j}{h}")
+                else:
+                    probs[j, h] = placed.tile([P, HALF], F32, name="probs00", align_bytes=64, offset=AT_PROBS)
+                if h:
+                    laid = probs[j, h][:].rearrange("p (t s) -> p t s", t=PACK)
+                    read = scores[j, h][:].rearrange("p (s t) -> p t s", t=PACK)
+                else:
+                    laid = probs[j, h][:].rearrange("p (u b e) -> p u b e", u=2, e=RUN)
+                    read = scores[j, h][:].rearrange("p (b u e) -> p u b e", u=2, e=RUN)
+                nc.scalar.activation(out=laid, in_=read, func=ACT.Exp, bias=lowest[j][:], scale=-1.0, accum_out=sums[:, j, h : h + 1])
+        nc.scalar.activation(out=v_picked[1][:, VALUE_SHARE:HALF], in_=v_table[:].indirect(offsets[:, cut : 2 * LIST_HALF]), func=ACT.Copy)
         total = keep.tile([P, 2], F32, name="total")
-        unread = keep.tile([P, 2, 3], F32, name="unread")
-        for j in range(2):
-            nc.scalar.activation(out=unread[:, j, :], in_=sums[:, j, :], func=ACT.Copy, accum_out=total[:, j : j + 1])
         inverse = keep.tile([P, 2], F32, name="inverse")
 
         w_pairs = [keep.tile([P, HALF], BF16, name=f"w_pairs{j}") for j in range(2)]
         for j in range(2):
-            nc.gpsimd.tensor_tensor(w_pairs[j][:], probs[j, 0][:], vs_rows[0][:].rearrange("p u x -> p (u x)"), ALU.mult)
+            nc.gpsimd.tensor_tensor(w_pairs[j][:], probs[j, 0][:], vs_row[:].rearrange("p u x -> p (u x)"), ALU.mult)
 
-        vw_grouped = [
-            keep.tile([P, 2, P, PACK], BF16, name="vw_grouped0", align_bytes=64),
-            placed.tile([P, 2, P, PACK], BF16, name="vw_grouped1", align_bytes=64, offset=AT_LOWEST),
-        ]
-        w_grouped = [
-            keep.tile([P, P, PACK], BF16, name="w_grouped0", align_bytes=64),
-            placed.tile([P, P, PACK], BF16, name="w_grouped1", align_bytes=64, offset=AT_FIRST),
-        ]
-        for j, (target, bank) in enumerate(((vw_grouped[1][:, 1, :, :], "turned0"), (w_grouped[1][:], "turned3"))):
+        first_grouped = keep.tile([P, 2, P, PACK], BF16, name="first_grouped", align_bytes=64)
+        v_grouped = keep.tile([P, P, PACK], BF16, name="v_grouped", align_bytes=64)
+        w_grouped = {
+            (1, 0): keep.tile([P, P, PACK], BF16, name="w_grouped10", align_bytes=64),
+            (0, 1): placed.tile([P, P, PACK], BF16, name="w_grouped01", align_bytes=64, offset=AT_PROBS),
+            (1, 1): placed.tile([P, P, PACK], BF16, name="w_grouped11", align_bytes=64, offset=AT_FIRST),
+        }
+        for j, bank in enumerate(("turned0", "turned3")):
             turned = turn_banks.tile([P, PACK, P], F32, name=bank)
             for t in range(PACK):
                 nc.tensor.transpose(turned[:, t, :], probs[j, 1][:, t * P : (t + 1) * P], ident[:])
             nc.vector.tensor_tensor(
-                target, turned[:].rearrange("p t q -> p q t"), vs_column[:].unsqueeze(1).to_broadcast([P, P, PACK]), ALU.mult
+                w_grouped[j, 1][:], turned[:].rearrange("p t q -> p q t"), vs_column[:].unsqueeze(1).to_broadcast([P, P, PACK]), ALU.mult
             )
 
-        nc.vector.reciprocal(inverse[:], total[:])
-
-        def turn(sources, bank, grouped):
-            for a, source in enumerate(sources):
-                for u in range(2):
-                    nc.tensor.transpose(bank[:, a, u, :], source.bitcast(F32)[:, u * P : (u + 1) * P], ident[:])
+        def turn(runs, bank, grouped):
+            for n, run in enumerate(runs):
+                nc.tensor.transpose(bank[:, n // 2, n % 2, :], run, ident[:])
             nc.scalar.copy(
-                out=grouped.bitcast(F32).rearrange("p (a e u) -> p a e u", a=len(sources), u=2),
+                out=grouped.bitcast(F32).rearrange("p (a e u) -> p a e u", a=len(runs) // 2, u=2),
                 in_=bank[:].rearrange("p a u e -> p a e u"),
             )
 
-        turn(
-            [v_picked[0][:], w_pairs[0][:]],
-            turn_banks.tile([P, 2, 2, P], F32, name="turned1"),
-            vw_grouped[0][:].rearrange("p a e t -> p (a e t)"),
-        )
-        turn([v_picked[1][:]], turn_banks.tile([P, 1, 2, P], F32, name="turned2"), vw_grouped[1][:, 0, :, :].rearrange("p e t -> p (e t)"))
-        turn([w_pairs[1][:]], score_banks.tile([P, 1, 2, P], F32, name="score10"), w_grouped[0][:].rearrange("p e t -> p (e t)"))
+        def side_by_side(source):
+            return [source[:].bitcast(F32)[:, u * P : (u + 1) * P] for u in range(2)]
 
-        vw_codes = [keep.tile([P, 2, P], U32, name=f"vw_codes{g}", align_bytes=64) for g in range(2)]
-        vw_scales = [keep.tile([P, 2, P], U8, name=f"vw_scales{g}", align_bytes=64) for g in range(2)]
-        w_codes = [keep.tile([P, P], U32, name=f"w_codes{g}", align_bytes=64) for g in range(2)]
-        w_scales = [keep.tile([P, P], U8, name=f"w_scales{g}", align_bytes=64) for g in range(2)]
-        for g in range(2):
-            nc.vector.quantize_mx(
-                out=vw_codes[g][:].rearrange("p a e -> p (a e)").bitcast(FP8X4),
-                scales=vw_scales[g][:].rearrange("p a e -> p (a e)"),
-                in_=vw_grouped[g][:].rearrange("p a e t -> p (a e t)"),
-            )
-        for g in (1, 0):
-            nc.vector.quantize_mx(out=w_codes[g][:].bitcast(FP8X4), scales=w_scales[g][:], in_=w_grouped[g][:].rearrange("p q t -> p (q t)"))
+        turn(
+            side_by_side(v_picked[0]) + side_by_side(w_pairs[0]),
+            turn_banks.tile([P, 2, 2, P], F32, name="turned1"),
+            first_grouped[:].rearrange("p a e t -> p (a e t)"),
+        )
+        turn(
+            [v_picked[1][:].bitcast(F32)[:, u:QUARTER:2] for u in range(2)],
+            turn_banks.tile([P, 1, 2, P], F32, name="turned2"),
+            v_grouped[:].rearrange("p e t -> p (e t)"),
+        )
+        turn(side_by_side(w_pairs[1]), score_banks.tile([P, 1, 2, P], F32, name="score10"), w_grouped[1, 0][:].rearrange("p e t -> p (e t)"))
+
+        for j in range(2):
+            nc.scalar.activation(out=sums[:, j, 2:3], in_=lows[j][:, 2:3], func=ACT.Exp, bias=lowest[j][:], scale=-1.0)
+
+        first_codes = keep.tile([P, 2, P], U32, name="first_codes", align_bytes=64)
+        first_scales = keep.tile([P, 2, P], U8, name="first_scales", align_bytes=64)
+        w_operand = {(0, 0): (first_codes[:, 1, :], first_scales[:, 1, :])}
+        v_operand = {0: (first_codes[:, 0, :], first_scales[:, 0, :])}
+
+        def quantised(name, grouped):
+            codes = keep.tile([P, P], U32, name=f"{name}_codes", align_bytes=64)
+            scales = keep.tile([P, P], U8, name=f"{name}_scales", align_bytes=64)
+            quantise(codes[:], scales[:], grouped[:])
+            return codes[:], scales[:]
+
+        for j in range(2):
+            w_operand[j, 1] = quantised(f"w{j}1", w_grouped[j, 1])
+        nc.vector.tensor_reduce(out=total[:], in_=sums[:], axis=AX.X, op=ALU.add)
+        quantise(
+            first_codes[:].rearrange("p a e -> p (a e)"),
+            first_scales[:].rearrange("p a e -> p (a e)"),
+            first_grouped[:].rearrange("p a e t -> p (a e) t"),
+        )
+        nc.vector.reciprocal(inverse[:], total[:])
+        v_operand[1] = quantised("v1", v_grouped)
+        w_operand[1, 0] = quantised("w10", w_grouped[1, 0])
         for j in range(2):
             acc = score_banks.tile([P, DV], F32, name=f"score0{j}")
             for n, g in enumerate((1, 0) if j else (0, 1)):
                 nc.tensor.matmul_mx(
                     out=acc[:],
-                    lhsT=(w_codes[g][:] if j else vw_codes[g][:, 1, :]).bitcast(FP8X4),
-                    lhsT_scale=w_scales[g][:] if j else vw_scales[g][:, 1, :],
-                    rhs=vw_codes[g][:, 0, :].bitcast(FP8X4),
-                    rhs_scale=vw_scales[g][:, 0, :],
+                    lhsT=w_operand[j, g][0].bitcast(FP8X4),
+                    lhsT_scale=w_operand[j, g][1],
+                    rhs=v_operand[g][0].bitcast(FP8X4),
+                    rhs_scale=v_operand[g][1],
                     start=(n == 0),
                     stop=(n == 1),
                 )

@@ -193,8 +193,8 @@ def tile_attend_sink_topk_kernel(tc, qT, kT, vT, vs, sink, offs, out):
                 else:
                     probs[j, h] = placed.tile([P, HALF], F32, name="probs00", align_bytes=64, offset=AT_PROBS)
                 if h:
-                    laid = probs[j, h][:].rearrange("p (t s) -> p t s", t=PACK)
-                    read = scores[j, h][:].rearrange("p (s t) -> p t s", t=PACK)
+                    laid = probs[j, h][:].rearrange("p (t c i) -> p c t i", t=PACK, i=PACK)
+                    read = scores[j, h][:].rearrange("p (c i t) -> p c t i", t=PACK, i=PACK)
                 else:
                     laid = probs[j, h][:].rearrange("p (u b e) -> p u b e", u=2, e=RUN)
                     read = scores[j, h][:].rearrange("p (b u e) -> p u b e", u=2, e=RUN)

@@ -26,14 +26,13 @@ RUN = 16
 PER_ROW = T // P
 LIST_HALF = HALF // 16
 
-PIECES = [slice(0, 1536), slice(1536, 3072), slice(3072, 3584), slice(3584, T)]
-CAST_SHARE = 384
+ROW_START = 256
 
 VALUE_SHARE = 256
 
-AT_PROBS = 6 * T
-AT_VS = T
-AT_FIRST = 5 * T
+AT_PROBS = 2048
+AT_VS = 4096
+AT_FIRST = 0
 
 
 def tile_attend_sink_topk_kernel(tc, qT, kT, vT, vs, sink, offs, out):
@@ -54,17 +53,15 @@ def tile_attend_sink_topk_kernel(tc, qT, kT, vT, vs, sink, offs, out):
         nc.scalar.dma_start(out=sink_rows[0:2, :], in_=sink[0].rearrange("(j m) x -> j (m x)", j=2))
 
         k_rows = kT.rearrange("(p t) c -> p t c", t=PACK)
-        k_table = [keep.tile([P, T], F32, name=f"k_table{t}") for t in range(PACK)]
-        for t in range(PACK - 1):
+        k_table = [keep.tile([P, T], F32, name=f"k_table{t}", align_bytes=ROW_START) for t in range(PACK)]
+        for t in range(PACK):
             nc.sync.dma_start(out=k_table[t][:], in_=k_rows[:, t, :])
             if t == 0:
                 nc.sync.dma_start(offsets[:], offs)
-        for piece in PIECES:
-            nc.sync.dma_start(out=k_table[3][:, piece], in_=k_rows[:, 3, piece])
-        q_raw = keep.tile([P, PACK, NQ], F32, name="q_raw")
+        q_raw = keep.tile([P, PACK, NQ], F32, name="q_raw", align_bytes=ROW_START)
         for u in range(2):
             nc.sync.dma_start(out=q_raw[:, 2 * u : 2 * u + 2, :], in_=qT[0].rearrange("(p t) q -> p t q", t=PACK)[:, 2 * u : 2 * u + 2, :])
-        v_table = keep.tile([P, T], F32, name="v_table")
+        v_table = keep.tile([P, T], F32, name="v_table", align_bytes=ROW_START)
         nc.sync.dma_start(out=v_table[:], in_=vT)
         halves = [offsets[:, h * LIST_HALF : (h + 1) * LIST_HALF] for h in range(2)]
 
@@ -86,15 +83,13 @@ def tile_attend_sink_topk_kernel(tc, qT, kT, vT, vs, sink, offs, out):
         for j in range(2):
             nc.scalar.activation(out=lows[j][:, 2:3], in_=turned[:, j : j + 1], func=ACT.Copy, scale=-1.0)
 
-        k_grouped = [keep.tile([P, HALF, PACK], BF16, name=f"k_grouped{h}", align_bytes=64) for h in range(2)]
-        k_low = placed.tile([P, 2, N], F32, name="k_low", align_bytes=64, offset=AT_VS)
-
-        vs_picked = keep.tile([P, N], F32, name="vs_picked")
-        nc.vector.tensor_copy(vs_picked[:], vs_table[:].indirect(offsets[:]))
+        vs_picked = [keep.tile([P, HALF], F32, name=f"vs_picked{h}") for h in range(2)]
+        nc.scalar.activation(out=vs_picked[0][:], in_=vs_table[:].indirect(halves[0]), func=ACT.Copy)
+        nc.vector.tensor_copy(vs_picked[1][:], vs_table[:].indirect(halves[1]))
         vs_row = keep.tile([P, 2, QUARTER], F32, name="vs_row")
         nc.gpsimd.tensor_scalar(
             out=vs_row[:].rearrange("r u (b e) -> r u b e", e=RUN),
-            in0=vs_picked[:, 0:HALF].rearrange("r (b u e) -> r u b e", u=2, e=RUN),
+            in0=vs_picked[0][:].rearrange("r (b u e) -> r u b e", u=2, e=RUN),
             scalar1=1.0,
             scalar2=0.0,
             op0=ALU.mult,
@@ -103,26 +98,15 @@ def tile_attend_sink_topk_kernel(tc, qT, kT, vT, vs, sink, offs, out):
         vs_column = keep.tile([P, PACK], F32, name="vs_column")
         turned = turn_banks.tile([P, PACK, P], F32, name="turned1")
         for t in range(PACK):
-            nc.tensor.transpose(turned[:, t, :], vs_picked[:, HALF + t : N : PACK], ident[:])
+            nc.tensor.transpose(turned[:, t, :], vs_picked[1][:, t:HALF:PACK], ident[:])
         nc.scalar.copy(out=vs_column[:], in_=turned[:, :, 0])
 
-        for t in range(2):
-            nc.vector.tensor_copy(k_low[:, t, :], k_table[t][:].indirect(offsets[:]))
-        pairs = [k_low[:, :, h * HALF : (h + 1) * HALF].rearrange("p t n -> p n t") for h in range(2)]
-        nc.vector.tensor_copy(k_grouped[0][:, :, 0:2], pairs[0])
-        nc.scalar.activation(out=k_grouped[1][:, :, 0:2], in_=pairs[1], func=ACT.Copy)
-        for h in range(2):
-            nc.vector.tensor_copy(k_grouped[h][:, :, 2], k_table[2][:].indirect(halves[h]))
-        k_last = keep.tile([P, T], BF16, name="k_last")
-        on_scalar = slice(PIECES[1].start, PIECES[1].start + CAST_SHARE)
-        on_vector = slice(on_scalar.stop, PIECES[1].stop)
-        for cols in (PIECES[0], on_scalar):
-            nc.scalar.activation(out=k_last[:, cols], in_=k_table[3][:, cols], func=ACT.Copy)
-        nc.vector.tensor_copy(k_last[:, on_vector], k_table[3][:, on_vector])
-        for cols in PIECES[2:]:
-            nc.scalar.activation(out=k_last[:, cols], in_=k_table[3][:, cols], func=ACT.Copy)
-        nc.vector.tensor_copy(k_grouped[1][:, :, 3], k_table[3][:].indirect(halves[1]))
-        nc.scalar.activation(out=k_grouped[0][:, :, 3], in_=k_last[:].indirect(halves[0]), func=ACT.Copy)
+        k_grouped = [
+            placed.tile([P, HALF, PACK], BF16, name=f"k_grouped{h}", align_bytes=64, offset=AT_VS + h * 2 * PACK * HALF) for h in range(2)
+        ]
+        for t in range(PACK):
+            nc.vector.tensor_copy(k_grouped[1][:, :, t], k_table[t][:].indirect(halves[1]))
+            nc.scalar.activation(out=k_grouped[0][:, :, t], in_=k_table[t][:].indirect(halves[0]), func=ACT.Copy)
 
         q_grouped = [keep.tile([P, P, PACK], BF16, name=f"q_grouped{j}", align_bytes=64) for j in range(2)]
         factors = keep.tile([P, 2], F32, name="factors", align_bytes=64)

@@ -26,6 +26,7 @@ RUN = 16
 PER_ROW = T // P
 LIST_HALF = HALF // 16
 
+LOWEST = -3.0e38
 ROW_START = 256
 
 VALUE_SHARE = 256
@@ -106,7 +107,10 @@ def tile_attend_sink_topk_kernel(tc, qT, kT, vT, vs, sink, offs, out):
         ]
         for t in range(PACK):
             nc.vector.tensor_copy(k_grouped[1][:, :, t], k_table[t][:].indirect(halves[1]))
-            nc.scalar.activation(out=k_grouped[0][:, :, t], in_=k_table[t][:].indirect(halves[0]), func=ACT.Copy)
+            step = QUARTER if t == PACK - 1 else HALF
+            for s in range(0, HALF, step):
+                picked = k_table[t][:].indirect(offsets[:, s // 16 : (s + step) // 16])
+                nc.scalar.activation(out=k_grouped[0][:, s : s + step, t], in_=picked, func=ACT.Copy)
 
         q_grouped = [keep.tile([P, P, PACK], BF16, name=f"q_grouped{j}", align_bytes=64) for j in range(2)]
         factors = keep.tile([P, 2], F32, name="factors", align_bytes=64)
@@ -131,16 +135,17 @@ def tile_attend_sink_topk_kernel(tc, qT, kT, vT, vs, sink, offs, out):
             nc.vector.quantize_mx(out=codes.bitcast(FP8X4), scales=scales, in_=grouped.rearrange("p n t -> p (n t)"))
 
         quarters = [slice(0, QUARTER), slice(QUARTER, HALF)]
+        pieces = {1: [slice(0, P), slice(P, QUARTER), quarters[1]], 0: quarters}
         quantise(q_codes[0][:], q_scales[0][:], q_grouped[0][:])
         for h in (1, 0):
-            for cols in quarters:
+            for cols in pieces[h]:
                 quantise(k_codes[h][:, cols], k_scales[:, h, cols], k_grouped[h][:, cols, :])
         quantise(q_codes[1][:], q_scales[1][:], q_grouped[1][:])
         scores = {}
         for j in range(2):
             for h in (1, 0):
                 scores[j, h] = score_banks.tile([P, HALF], F32, name=f"score{j}{h}")
-                for cols in ([slice(0, HALF)] if j else quarters):
+                for cols in ([slice(0, HALF)] if j else pieces[h]):
                     nc.tensor.matmul_mx(
                         out=scores[j, h][:, cols],
                         lhsT=q_codes[j][:].bitcast(FP8X4),
@@ -155,9 +160,9 @@ def tile_attend_sink_topk_kernel(tc, qT, kT, vT, vs, sink, offs, out):
             for h in (1, 0):
                 nc.vector.tensor_reduce(out=lows[j][:, h : h + 1], in_=scores[j, h][:], axis=AX.X, op=ALU.min)
         lowest = [keep.tile([P, 1], F32, name=f"lowest{j}") for j in range(2)]
-        nc.gpsimd.tensor_scalar(
-            out=lowest[0][:], in0=lows[0][:, 0:1], scalar1=lows[0][:, 1:2], scalar2=lows[0][:, 2:3], op0=ALU.min, op1=ALU.min
-        )
+        partly = keep.tile([P, 1], F32, name="partly")
+        nc.gpsimd.tensor_scalar(out=partly[:], in0=lows[0][:, 1:2], scalar1=lows[0][:, 2:3], scalar2=LOWEST, op0=ALU.min, op1=ALU.max)
+        nc.gpsimd.tensor_scalar(out=lowest[0][:], in0=lows[0][:, 0:1], scalar1=partly[:], scalar2=LOWEST, op0=ALU.min, op1=ALU.max)
         nc.vector.tensor_reduce(out=lowest[1][:], in_=lows[1][:], axis=AX.X, op=ALU.min)
 
         v_picked = [
@@ -266,6 +271,6 @@ def tile_attend_sink_topk_kernel(tc, qT, kT, vT, vs, sink, offs, out):
                     start=(n == 0),
                     stop=(n == 1),
                 )
-            result = keep.tile([P, DV], F32, name=f"result{j}")
+            result = keep.tile([P, DV], F32, name=f"result{j}", align_bytes=ROW_START)
             nc.scalar.activation(out=result[:], in_=acc[:], func=ACT.Copy, scale=inverse[:, j : j + 1])
             nc.sync.dma_start(out=out[0][j * P : (j + 1) * P, :], in_=result[:])

@@ -54,11 +54,12 @@ def tile_attend_sink_topk_kernel(tc, qT, kT, vT, vs, sink, offs, out):
         nc.scalar.dma_start(out=sink_rows[0:2, :], in_=sink[0].rearrange("(j m) x -> j (m x)", j=2))
 
         k_rows = kT.rearrange("(p t) c -> p t c", t=PACK)
-        k_table = [keep.tile([P, T], F32, name=f"k_table{t}", align_bytes=ROW_START) for t in range(PACK)]
-        for t in range(PACK):
-            nc.sync.dma_start(out=k_table[t][:], in_=k_rows[:, t, :])
-            if t == 0:
-                nc.sync.dma_start(offsets[:], offs)
+        k_early = keep.tile([P, 2, T], F32, name="k_early", align_bytes=ROW_START)
+        k_late = [keep.tile([P, T], F32, name=f"k_late{t}", align_bytes=ROW_START) for t in range(2)]
+        nc.sync.dma_start(out=k_early[:], in_=k_rows[:, 0:2, :])
+        nc.sync.dma_start(offsets[:], offs)
+        for t in range(2):
+            nc.sync.dma_start(out=k_late[t][:], in_=k_rows[:, 2 + t, :])
         q_raw = keep.tile([P, PACK, NQ], F32, name="q_raw", align_bytes=ROW_START)
         for u in range(2):
             nc.sync.dma_start(out=q_raw[:, 2 * u : 2 * u + 2, :], in_=qT[0].rearrange("(p t) q -> p t q", t=PACK)[:, 2 * u : 2 * u + 2, :])
@@ -76,8 +77,7 @@ def tile_attend_sink_topk_kernel(tc, qT, kT, vT, vs, sink, offs, out):
             turned = turn_banks.tile([P, PACK, P], F32, name=f"turned{b % 4}")
             for c in range(PACK):
                 nc.tensor.transpose(turned[:, c, :], vs_runs[:, b * PACK + c : b * PACK + c + 1].to_broadcast([P, P]), ident[:])
-            leave = nc.vector.tensor_copy if b % 2 else nc.scalar.copy
-            leave(vs_table[:].rearrange("r (p b c) -> r b p c", c=PACK, b=PER_ROW // PACK)[:, b, :, :], turned[:].rearrange("r c p -> r p c"))
+            nc.scalar.copy(vs_table[:].rearrange("r (p b c) -> r b p c", c=PACK, b=PER_ROW // PACK)[:, b, :, :], turned[:].rearrange("r c p -> r p c"))
 
         turned = turn_banks.tile([P, P], F32, name="turned0")
         nc.tensor.transpose(turned[:], sink_rows[:], ident[:])
@@ -85,8 +85,8 @@ def tile_attend_sink_topk_kernel(tc, qT, kT, vT, vs, sink, offs, out):
             nc.scalar.activation(out=lows[j][:, 2:3], in_=turned[:, j : j + 1], func=ACT.Copy, scale=-1.0)
 
         vs_picked = [keep.tile([P, HALF], F32, name=f"vs_picked{h}") for h in range(2)]
-        nc.scalar.activation(out=vs_picked[0][:], in_=vs_table[:].indirect(halves[0]), func=ACT.Copy)
-        nc.vector.tensor_copy(vs_picked[1][:], vs_table[:].indirect(halves[1]))
+        for h in range(2):
+            nc.scalar.activation(out=vs_picked[h][:], in_=vs_table[:].indirect(halves[h]), func=ACT.Copy)
         vs_row = keep.tile([P, 2, QUARTER], F32, name="vs_row")
         nc.gpsimd.tensor_scalar(
             out=vs_row[:].rearrange("r u (b e) -> r u b e", e=RUN),
@@ -101,16 +101,25 @@ def tile_attend_sink_topk_kernel(tc, qT, kT, vT, vs, sink, offs, out):
         for t in range(PACK):
             nc.tensor.transpose(turned[:, t, :], vs_picked[1][:, t:HALF:PACK], ident[:])
         nc.scalar.copy(out=vs_column[:], in_=turned[:, :, 0])
+        vs_down = keep.tile([P, 1], F32, name="vs_down")
+        turned = turn_banks.tile([P, P], F32, name="turned0")
+        nc.tensor.transpose(turned[:], vs_row[:, 1, P:QUARTER], ident[:])
+        nc.scalar.copy(out=vs_down[:], in_=turned[:, 0:1])
+        vs_held = turn_banks.tile([P, P], F32, name="turned2")
+        nc.tensor.transpose(vs_held[:], vs_down[:].to_broadcast([P, P]), ident[:])
 
         k_grouped = [
             placed.tile([P, HALF, PACK], BF16, name=f"k_grouped{h}", align_bytes=64, offset=AT_VS + h * 2 * PACK * HALF) for h in range(2)
         ]
-        for t in range(PACK):
-            nc.vector.tensor_copy(k_grouped[1][:, :, t], k_table[t][:].indirect(halves[1]))
-            step = QUARTER if t == PACK - 1 else HALF
-            for s in range(0, HALF, step):
-                picked = k_table[t][:].indirect(offsets[:, s // 16 : (s + step) // 16])
-                nc.scalar.activation(out=k_grouped[0][:, s : s + step, t], in_=picked, func=ACT.Copy)
+        k_low = keep.tile([P, 2, N], F32, name="k_low")
+        for t in range(2):
+            nc.vector.tensor_copy(k_low[:, t, :], k_early[:, t, :].indirect(offsets[:]))
+        pairs = [k_low[:, :, h * HALF : (h + 1) * HALF].rearrange("p t n -> p n t") for h in range(2)]
+        nc.scalar.activation(out=k_grouped[0][:, :, 0:2], in_=pairs[0], func=ACT.Copy)
+        nc.vector.tensor_copy(k_grouped[1][:, :, 0:2], pairs[1])
+        for t in range(2):
+            nc.vector.tensor_copy(k_grouped[1][:, :, 2 + t], k_late[t][:].indirect(halves[1]))
+            nc.scalar.activation(out=k_grouped[0][:, :, 2 + t], in_=k_late[t][:].indirect(halves[0]), func=ACT.Copy)
 
         q_grouped = [keep.tile([P, P, PACK], BF16, name=f"q_grouped{j}", align_bytes=64) for j in range(2)]
         factors = keep.tile([P, 2], F32, name="factors", align_bytes=64)
@@ -193,8 +202,9 @@ def tile_attend_sink_topk_kernel(tc, qT, kT, vT, vs, sink, offs, out):
         inverse = keep.tile([P, 2], F32, name="inverse")
 
         w_pairs = [keep.tile([P, HALF], BF16, name=f"w_pairs{j}") for j in range(2)]
-        for j in range(2):
-            nc.gpsimd.tensor_tensor(w_pairs[j][:], probs[j, 0][:], vs_row[:].rearrange("p u x -> p (u x)"), ALU.mult)
+        for j, cols in enumerate((slice(0, HALF), slice(0, HALF - P))):
+            nc.gpsimd.tensor_tensor(w_pairs[j][:, cols], probs[j, 0][:, cols], vs_row[:].rearrange("p u x -> p (u x)")[:, cols], ALU.mult)
+        nc.vector.tensor_tensor(w_pairs[1][:, HALF - P : HALF], probs[1, 0][:, HALF - P : HALF], vs_held[:], ALU.mult)
 
         first_grouped = keep.tile([P, 2, P, PACK], BF16, name="first_grouped", align_bytes=64)
         v_grouped = keep.tile([P, P, PACK], BF16, name="v_grouped", align_bytes=64)
@@ -224,7 +234,7 @@ def tile_attend_sink_topk_kernel(tc, qT, kT, vT, vs, sink, offs, out):
 
         turn(
             side_by_side(v_picked[0]) + side_by_side(w_pairs[0]),
-            turn_banks.tile([P, 2, 2, P], F32, name="turned1"),
+            score_banks.tile([P, 2, 2, P], F32, name="score01"),
             first_grouped[:].rearrange("p a e t -> p (a e t)"),
         )
         turn(

@@ -143,18 +143,17 @@ def tile_attend_sink_topk_kernel(tc, qT, kT, vT, vs, sink, offs, out):
         def quantise(codes, scales, grouped):
             nc.vector.quantize_mx(out=codes.bitcast(FP8X4), scales=scales, in_=grouped.rearrange("p n t -> p (n t)"))
 
-        quarters = [slice(0, QUARTER), slice(QUARTER, HALF)]
-        pieces = {1: [slice(0, P), slice(P, QUARTER), quarters[1]], 0: quarters}
+        pieces = [slice(0, QUARTER), slice(QUARTER, QUARTER + P), slice(QUARTER + P, HALF)]
         quantise(q_codes[0][:], q_scales[0][:], q_grouped[0][:])
         for h in (1, 0):
-            for cols in pieces[h]:
+            for cols in pieces:
                 quantise(k_codes[h][:, cols], k_scales[:, h, cols], k_grouped[h][:, cols, :])
         quantise(q_codes[1][:], q_scales[1][:], q_grouped[1][:])
         scores = {}
         for j in range(2):
             for h in (1, 0):
                 scores[j, h] = score_banks.tile([P, HALF], F32, name=f"score{j}{h}")
-                for cols in ([slice(0, HALF)] if j else pieces[h]):
+                for cols in ([slice(0, HALF)] if j else pieces):
                     nc.tensor.matmul_mx(
                         out=scores[j, h][:, cols],
                         lhsT=q_codes[j][:].bitcast(FP8X4),
@@ -258,8 +257,7 @@ def tile_attend_sink_topk_kernel(tc, qT, kT, vT, vs, sink, offs, out):
             quantise(codes[:], scales[:], grouped[:])
             return codes[:], scales[:]
 
-        for j in range(2):
-            w_operand[j, 1] = quantised(f"w{j}1", w_grouped[j, 1])
+        w_operand[0, 1] = quantised("w01", w_grouped[0, 1])
         nc.vector.tensor_reduce(out=total[:], in_=sums[:], axis=AX.X, op=ALU.add)
         quantise(
             first_codes[:].rearrange("p a e -> p (a e)"),
@@ -268,7 +266,8 @@ def tile_attend_sink_topk_kernel(tc, qT, kT, vT, vs, sink, offs, out):
         )
         nc.vector.reciprocal(inverse[:], total[:])
         v_operand[1] = quantised("v1", v_grouped)
-        w_operand[1, 0] = quantised("w10", w_grouped[1, 0])
+        for g in (1, 0):
+            w_operand[1, g] = quantised(f"w1{g}", w_grouped[1, g])
         for j in range(2):
             acc = score_banks.tile([P, DV], F32, name=f"score0{j}")
             for n, g in enumerate((1, 0) if j else (0, 1)):

@@ -143,7 +143,7 @@ def tile_attend_sink_topk_kernel(tc, qT, kT, vT, vs, sink, offs, out):
         def quantise(codes, scales, grouped):
             nc.vector.quantize_mx(out=codes.bitcast(FP8X4), scales=scales, in_=grouped.rearrange("p n t -> p (n t)"))
 
-        pieces = [slice(0, QUARTER), slice(QUARTER, QUARTER + P), slice(QUARTER + P, HALF)]
+        pieces = [slice(c, c + P) for c in range(0, HALF, P)]
         quantise(q_codes[0][:], q_scales[0][:], q_grouped[0][:])
         for h in (1, 0):
             for cols in pieces:
@@ -220,13 +220,14 @@ def tile_attend_sink_topk_kernel(tc, qT, kT, vT, vs, sink, offs, out):
                 w_grouped[j, 1][:], turned[:].rearrange("p t q -> p q t"), vs_column[:].unsqueeze(1).to_broadcast([P, P, PACK]), ALU.mult
             )
 
-        def turn(runs, bank, grouped):
+        def turn(runs, bank, grouped, parts=(slice(0, P),)):
             for n, run in enumerate(runs):
                 nc.tensor.transpose(bank[:, n // 2, n % 2, :], run, ident[:])
-            nc.scalar.copy(
-                out=grouped.bitcast(F32).rearrange("p (a e u) -> p a e u", a=len(runs) // 2, u=2),
-                in_=bank[:].rearrange("p a u e -> p a e u"),
-            )
+            for part in parts:
+                nc.scalar.copy(
+                    out=grouped.bitcast(F32).rearrange("p (a e u) -> p a e u", a=len(runs) // 2, u=2)[:, :, part, :],
+                    in_=bank[:].rearrange("p a u e -> p a e u")[:, :, part, :],
+                )
 
         def side_by_side(source):
             return [source[:].bitcast(F32)[:, u * P : (u + 1) * P] for u in range(2)]
@@ -241,7 +242,13 @@ def tile_attend_sink_topk_kernel(tc, qT, kT, vT, vs, sink, offs, out):
             turn_banks.tile([P, 1, 2, P], F32, name="turned2"),
             v_grouped[:].rearrange("p e t -> p (e t)"),
         )
-        turn(side_by_side(w_pairs[1]), score_banks.tile([P, 1, 2, P], F32, name="score10"), w_grouped[1, 0][:].rearrange("p e t -> p (e t)"))
+        last_parts = (slice(0, P // 2), slice(P // 2, P))
+        turn(
+            side_by_side(w_pairs[1]),
+            score_banks.tile([P, 1, 2, P], F32, name="score10"),
+            w_grouped[1, 0][:].rearrange("p e t -> p (e t)"),
+            last_parts,
+        )
 
         for j in range(2):
             nc.scalar.activation(out=sums[:, j, 2:3], in_=lows[j][:, 2:3], func=ACT.Exp, bias=lowest[j][:], scale=-1.0)
@@ -251,10 +258,11 @@ def tile_attend_sink_topk_kernel(tc, qT, kT, vT, vs, sink, offs, out):
         w_operand = {(0, 0): (first_codes[:, 1, :], first_scales[:, 1, :])}
         v_operand = {0: (first_codes[:, 0, :], first_scales[:, 0, :])}
 
-        def quantised(name, grouped):
+        def quantised(name, grouped, parts=(slice(0, P),)):
             codes = keep.tile([P, P], U32, name=f"{name}_codes", align_bytes=64)
             scales = keep.tile([P, P], U8, name=f"{name}_scales", align_bytes=64)
-            quantise(codes[:], scales[:], grouped[:])
+            for part in parts:
+                quantise(codes[:, part], scales[:, part], grouped[:, part, :])
             return codes[:], scales[:]
 
         w_operand[0, 1] = quantised("w01", w_grouped[0, 1])
@@ -266,8 +274,8 @@ def tile_attend_sink_topk_kernel(tc, qT, kT, vT, vs, sink, offs, out):
         )
         nc.vector.reciprocal(inverse[:], total[:])
         v_operand[1] = quantised("v1", v_grouped)
-        for g in (1, 0):
-            w_operand[1, g] = quantised(f"w1{g}", w_grouped[1, g])
+        w_operand[1, 1] = quantised("w11", w_grouped[1, 1])
+        w_operand[1, 0] = quantised("w10", w_grouped[1, 0], last_parts)
         for j in range(2):
             acc = score_banks.tile([P, DV], F32, name=f"score0{j}")
             for n, g in enumerate((1, 0) if j else (0, 1)):

from contextlib import ExitStack

import concourse.mybir as mybir
from concourse.masks import make_identity

D, DV, NQ, T, N = 512, 128, 256, 4096, 1024

FLOPS = 2 * NQ * N * (D + DV)
BYTES = 4 * (D * T + DV * T + T + D * NQ + NQ + NQ * DV) + 2 * 128 * (N // 16)

F32 = mybir.dt.float32
BF16 = mybir.dt.bfloat16
U32 = mybir.dt.uint32
U16 = mybir.dt.uint16
U8 = mybir.dt.uint8
FP8X4 = mybir.dt.float8_e4m3fn_x4
ALU = mybir.AluOpType
ACT = mybir.ActivationFunctionType
AX = mybir.AxisListType

P = 128
PACK = 4
HALF = 512
QUARTER = HALF // 2
RUN = 16
PER_ROW = T // P
LIST_HALF = HALF // 16

LOWEST = -3.0e38
ROW_START = 256

VALUE_SHARE = 256

AT_PROBS = 2048
AT_VS = 4096
AT_FIRST = 0


def tile_attend_sink_topk_kernel(tc, qT, kT, vT, vs, sink, offs, out):
    nc = tc.nc
    with ExitStack() as ctx:
        lists = ctx.enter_context(tc.tile_pool(name="lists", bufs=1))
        keep = ctx.enter_context(tc.tile_pool(name="keep", bufs=1))
        placed = ctx.enter_context(tc.tile_pool(name="placed", bufs=1))
        score_banks = ctx.enter_context(tc.psum_pool(name="score_banks", bufs=1))
        turn_banks = ctx.enter_context(tc.psum_pool(name="turn_banks", bufs=1))


        offsets = lists.tile([P, N // 16], U16, name="offsets")
        vs_runs = keep.tile([P, PER_ROW], F32, name="vs_runs")
        nc.sync.dma_start(out=vs_runs[:], in_=vs[0].rearrange("(p c) -> p c", c=PER_ROW))
        sink_rows = keep.tile([P, P], F32, name="sink_rows")
        nc.gpsimd.memset(sink_rows[:], 0.0)
        nc.scalar.dma_start(out=sink_rows[0:2, :], in_=sink[0].rearrange("(j m) x -> j (m x)", j=2))

        k_rows = kT.rearrange("(p t) c -> p t c", t=PACK)
        k_early = keep.tile([P, 2, T], F32, name="k_early", align_bytes=ROW_START)
        k_late = [keep.tile([P, T], F32, name=f"k_late{t}", align_bytes=ROW_START) for t in range(2)]
        nc.sync.dma_start(out=k_early[:], in_=k_rows[:, 0:2, :])
        nc.sync.dma_start(offsets[:], offs)
        for t in range(2):
            nc.sync.dma_start(out=k_late[t][:], in_=k_rows[:, 2 + t, :])
        q_raw = keep.tile([P, PACK, NQ], F32, name="q_raw", align_bytes=ROW_START)
        for u in range(2):
            nc.sync.dma_start(out=q_raw[:, 2 * u : 2 * u + 2, :], in_=qT[0].rearrange("(p t) q -> p t q", t=PACK)[:, 2 * u : 2 * u + 2, :])
        v_table = keep.tile([P, T], F32, name="v_table", align_bytes=ROW_START)
        nc.sync.dma_start(out=v_table[:], in_=vT)
        halves = [offsets[:, h * LIST_HALF : (h + 1) * LIST_HALF] for h in range(2)]

        ident = keep.tile([P, P], F32, name="ident")
        make_identity(nc, ident[:])

        lows = [keep.tile([P, 3], F32, name=f"low{j}") for j in range(2)]

        vs_table = placed.tile([P, T], F32, name="vs_table", align_bytes=64, offset=AT_VS)
        for b in range(PER_ROW // PACK):
            turned = turn_banks.tile([P, PACK, P], F32, name=f"turned{b % 4}")
            for c in range(PACK):
                nc.tensor.transpose(turned[:, c, :], vs_runs[:, b * PACK + c : b * PACK + c + 1].to_broadcast([P, P]), ident[:])
            nc.scalar.copy(vs_table[:].rearrange("r (p b c) -> r b p c", c=PACK, b=PER_ROW // PACK)[:, b, :, :], turned[:].rearrange("r c p -> r p c"))

        turned = turn_banks.tile([P, P], F32, name="turned0")
        nc.tensor.transpose(turned[:], sink_rows[:], ident[:])
        for j in range(2):
            nc.scalar.activation(out=lows[j][:, 2:3], in_=turned[:, j : j + 1], func=ACT.Copy, scale=-1.0)

        vs_picked = [keep.tile([P, HALF], F32, name=f"vs_picked{h}") for h in range(2)]
        for h in range(2):
            nc.scalar.activation(out=vs_picked[h][:], in_=vs_table[:].indirect(halves[h]), func=ACT.Copy)
        vs_row = keep.tile([P, 2, QUARTER], F32, name="vs_row")
        nc.gpsimd.tensor_scalar(
            out=vs_row[:].rearrange("r u (b e) -> r u b e", e=RUN),
            in0=vs_picked[0][:].rearrange("r (b u e) -> r u b e", u=2, e=RUN),
            scalar1=1.0,
            scalar2=0.0,
            op0=ALU.mult,
            op1=ALU.add,
        )
        vs_column = keep.tile([P, PACK], F32, name="vs_column")
        turned = turn_banks.tile([P, PACK, P], F32, name="turned1")
        for t in range(PACK):
            nc.tensor.transpose(turned[:, t, :], vs_picked[1][:, t:HALF:PACK], ident[:])
        nc.scalar.copy(out=vs_column[:], in_=turned[:, :, 0])
        vs_down = keep.tile([P, 1], F32, name="vs_down")
        turned = turn_banks.tile([P, P], F32, name="turned0")
        nc.tensor.transpose(turned[:], vs_row[:, 1, P:QUARTER], ident[:])
        nc.scalar.copy(out=vs_down[:], in_=turned[:, 0:1])
        vs_held = turn_banks.tile([P, P], F32, name="turned2")
        nc.tensor.transpose(vs_held[:], vs_down[:].to_broadcast([P, P]), ident[:])

        k_grouped = [
            placed.tile([P, HALF, PACK], BF16, name=f"k_grouped{h}", align_bytes=64, offset=AT_VS + h * 2 * PACK * HALF) for h in range(2)
        ]
        k_low = keep.tile([P, 2, N], F32, name="k_low")
        for t in range(2):
            nc.vector.tensor_copy(k_low[:, t, :], k_early[:, t, :].indirect(offsets[:]))
        pairs = [k_low[:, :, h * HALF : (h + 1) * HALF].rearrange("p t n -> p n t") for h in range(2)]
        nc.scalar.activation(out=k_grouped[0][:, :, 0:2], in_=pairs[0], func=ACT.Copy)
        nc.vector.tensor_copy(k_grouped[1][:, :, 0:2], pairs[1])
        for t in range(2):
            nc.vector.tensor_copy(k_grouped[1][:, :, 2 + t], k_late[t][:].indirect(halves[1]))
            nc.scalar.activation(out=k_grouped[0][:, :, 2 + t], in_=k_late[t][:].indirect(halves[0]), func=ACT.Copy)

        q_grouped = [keep.tile([P, P, PACK], BF16, name=f"q_grouped{j}", align_bytes=64) for j in range(2)]
        factors = keep.tile([P, 2], F32, name="factors", align_bytes=64)
        nc.gpsimd.memset(factors[:, 0:1], -1.0)
        nc.gpsimd.memset(factors[:, 1:2], 0.0)
        for u in range(2):
            nc.gpsimd.tensor_scalar(
                out=q_grouped[0][:, :, 2 * u : 2 * u + 2],
                in0=q_raw[:, 2 * u : 2 * u + 2, 0:P].rearrange("p t m -> p m t"),
                scalar1=factors[:, 0:1],
                scalar2=factors[:, 1:2],
                op0=ALU.mult,
                op1=ALU.add,
            )
        nc.scalar.activation(out=q_grouped[1][:], in_=q_raw[:, :, P:NQ].rearrange("p t m -> p m t"), func=ACT.Copy, scale=-1.0)
        q_codes = [keep.tile([P, P], U32, name=f"q_codes{j}", align_bytes=64) for j in range(2)]
        q_scales = [keep.tile([P, P], U8, name=f"q_scales{j}", align_bytes=64) for j in range(2)]
        k_scales = keep.tile([P, 2, HALF], U8, name="factors", align_bytes=64)
        k_codes = [keep.tile([P, HALF], U32, name=f"k_codes{h}", align_bytes=64) for h in range(2)]

        def quantise(codes, scales, grouped):
            nc.vector.quantize_mx(out=codes.bitcast(FP8X4), scales=scales, in_=grouped.rearrange("p n t -> p (n t)"))

        pieces = [slice(c, c + P) for c in range(0, HALF, P)]
        quantise(q_codes[0][:], q_scales[0][:], q_grouped[0][:])
        for h in (1, 0):
            for cols in pieces:
                quantise(k_codes[h][:, cols], k_scales[:, h, cols], k_grouped[h][:, cols, :])
        quantise(q_codes[1][:], q_scales[1][:], q_grouped[1][:])
        scores = {}
        for j in range(2):
            for h in (1, 0):
                scores[j, h] = score_banks.tile([P, HALF], F32, name=f"score{j}{h}")
                for cols in ([slice(0, HALF)] if j else pieces):
                    nc.tensor.matmul_mx(
                        out=scores[j, h][:, cols],
                        lhsT=q_codes[j][:].bitcast(FP8X4),
                        lhsT_scale=q_scales[j][:],
                        rhs=k_codes[h][:, cols].bitcast(FP8X4),
                        rhs_scale=k_scales[:, h, cols],
                        start=True,
                        stop=True,
                    )

        for j in range(2):
            for h in (1, 0):
                nc.vector.tensor_reduce(out=lows[j][:, h : h + 1], in_=scores[j, h][:], axis=AX.X, op=ALU.min)
        lowest = [keep.tile([P, 1], F32, name=f"lowest{j}") for j in range(2)]
        partly = keep.tile([P, 1], F32, name="partly")
        nc.gpsimd.tensor_scalar(out=partly[:], in0=lows[0][:, 1:2], scalar1=lows[0][:, 2:3], scalar2=LOWEST, op0=ALU.min, op1=ALU.max)
        nc.gpsimd.tensor_scalar(out=lowest[0][:], in0=lows[0][:, 0:1], scalar1=partly[:], scalar2=LOWEST, op0=ALU.min, op1=ALU.max)
        nc.vector.tensor_reduce(out=lowest[1][:], in_=lows[1][:], axis=AX.X, op=ALU.min)

        v_picked = [
            placed.tile([P, HALF], BF16, name="v_first", align_bytes=64, offset=AT_FIRST),
            keep.tile([P, HALF], BF16, name="v_second"),
        ]
        nc.vector.tensor_copy(v_picked[0][:].rearrange("p (u b e) -> p b u e", u=2, e=RUN), v_table[:].indirect(halves[0]))
        cut = LIST_HALF + VALUE_SHARE // 16
        nc.vector.tensor_copy(v_picked[1][:, 0:VALUE_SHARE], v_table[:].indirect(offsets[:, LIST_HALF:cut]))

        sums = keep.tile([P, 2, 3], F32, name="sums")
        probs = {}
        for j in range(2):
            for h in range(2):
                if j or h:
                    probs[j, h] = keep.tile([P, HALF], F32, name=f"probs{j}{h}")
                else:
                    probs[j, h] = placed.tile([P, HALF], F32, name="probs00", align_bytes=64, offset=AT_PROBS)
                if h:
                    laid = probs[j, h][:].rearrange("p (t c i) -> p c t i", t=PACK, i=PACK)
                    read = scores[j, h][:].rearrange("p (c i t) -> p c t i", t=PACK, i=PACK)
                else:
                    laid = probs[j, h][:].rearrange("p (u b e) -> p u b e", u=2, e=RUN)
                    read = scores[j, h][:].rearrange("p (b u e) -> p u b e", u=2, e=RUN)
                nc.scalar.activation(out=laid, in_=read, func=ACT.Exp, bias=lowest[j][:], scale=-1.0, accum_out=sums[:, j, h : h + 1])
        nc.scalar.activation(out=v_picked[1][:, VALUE_SHARE:HALF], in_=v_table[:].indirect(offsets[:, cut : 2 * LIST_HALF]), func=ACT.Copy)
        total = keep.tile([P, 2], F32, name="total")
        inverse = keep.tile([P, 2], F32, name="inverse")

        w_pairs = [keep.tile([P, HALF], BF16, name=f"w_pairs{j}") for j in range(2)]
        for j, cols in enumerate((slice(0, HALF), slice(0, HALF - P))):
            nc.gpsimd.tensor_tensor(w_pairs[j][:, cols], probs[j, 0][:, cols], vs_row[:].rearrange("p u x -> p (u x)")[:, cols], ALU.mult)
        nc.vector.tensor_tensor(w_pairs[1][:, HALF - P : HALF], probs[1, 0][:, HALF - P : HALF], vs_held[:], ALU.mult)

        first_grouped = keep.tile([P, 2, P, PACK], BF16, name="first_grouped", align_bytes=64)
        v_grouped = keep.tile([P, P, PACK], BF16, name="v_grouped", align_bytes=64)
        w_grouped = {
            (1, 0): keep.tile([P, P, PACK], BF16, name="w_grouped10", align_bytes=64),
            (0, 1): placed.tile([P, P, PACK], BF16, name="w_grouped01", align_bytes=64, offset=AT_PROBS),
            (1, 1): placed.tile([P, P, PACK], BF16, name="w_grouped11", align_bytes=64, offset=AT_FIRST),
        }
        for j, bank in enumerate(("turned0", "turned3")):
            turned = turn_banks.tile([P, PACK, P], F32, name=bank)
            for t in range(PACK):
                nc.tensor.transpose(turned[:, t, :], probs[j, 1][:, t * P : (t + 1) * P], ident[:])
            nc.vector.tensor_tensor(
                w_grouped[j, 1][:], turned[:].rearrange("p t q -> p q t"), vs_column[:].unsqueeze(1).to_broadcast([P, P, PACK]), ALU.mult
            )

        def turn(runs, bank, grouped, parts=(slice(0, P),)):
            for n, run in enumerate(runs):
                nc.tensor.transpose(bank[:, n // 2, n % 2, :], run, ident[:])
            for part in parts:
                nc.scalar.copy(
                    out=grouped.bitcast(F32).rearrange("p (a e u) -> p a e u", a=len(runs) // 2, u=2)[:, :, part, :],
                    in_=bank[:].rearrange("p a u e -> p a e u")[:, :, part, :],
                )

        def side_by_side(source):
            return [source[:].bitcast(F32)[:, u * P : (u + 1) * P] for u in range(2)]

        turn(
            side_by_side(v_picked[0]) + side_by_side(w_pairs[0]),
            score_banks.tile([P, 2, 2, P], F32, name="score01"),
            first_grouped[:].rearrange("p a e t -> p (a e t)"),
        )
        turn(
            [v_picked[1][:].bitcast(F32)[:, u:QUARTER:2] for u in range(2)],
            turn_banks.tile([P, 1, 2, P], F32, name="turned2"),
            v_grouped[:].rearrange("p e t -> p (e t)"),
        )
        last_parts = (slice(0, P // 2), slice(P // 2, P))
        turn(
            side_by_side(w_pairs[1]),
            score_banks.tile([P, 1, 2, P], F32, name="score10"),
            w_grouped[1, 0][:].rearrange("p e t -> p (e t)"),
            last_parts,
        )

        for j in range(2):
            nc.scalar.activation(out=sums[:, j, 2:3], in_=lows[j][:, 2:3], func=ACT.Exp, bias=lowest[j][:], scale=-1.0)

        first_codes = keep.tile([P, 2, P], U32, name="first_codes", align_bytes=64)
        first_scales = keep.tile([P, 2, P], U8, name="first_scales", align_bytes=64)
        w_operand = {(0, 0): (first_codes[:, 1, :], first_scales[:, 1, :])}
        v_operand = {0: (first_codes[:, 0, :], first_scales[:, 0, :])}

        def quantised(name, grouped, parts=(slice(0, P),)):
            codes = keep.tile([P, P], U32, name=f"{name}_codes", align_bytes=64)
            scales = keep.tile([P, P], U8, name=f"{name}_scales", align_bytes=64)
            for part in parts:
                quantise(codes[:, part], scales[:, part], grouped[:, part, :])
            return codes[:], scales[:]

        w_operand[0, 1] = quantised("w01", w_grouped[0, 1])
        nc.vector.tensor_reduce(out=total[:], in_=sums[:], axis=AX.X, op=ALU.add)
        quantise(
            first_codes[:].rearrange("p a e -> p (a e)"),
            first_scales[:].rearrange("p a e -> p (a e)"),
            first_grouped[:].rearrange("p a e t -> p (a e) t"),
        )
        nc.vector.reciprocal(inverse[:], total[:])
        v_operand[1] = quantised("v1", v_grouped)
        w_operand[1, 1] = quantised("w11", w_grouped[1, 1])
        w_operand[1, 0] = quantised("w10", w_grouped[1, 0], last_parts)
        for j in range(2):
            acc = score_banks.tile([P, DV], F32, name=f"score0{j}")
            for n, g in enumerate((1, 0) if j else (0, 1)):
                nc.tensor.matmul_mx(
                    out=acc[:],
                    lhsT=w_operand[j, g][0].bitcast(FP8X4),
                    lhsT_scale=w_operand[j, g][1],
                    rhs=v_operand[g][0].bitcast(FP8X4),
                    rhs_scale=v_operand[g][1],
                    start=(n == 0),
                    stop=(n == 1),
                )
            result = keep.tile([P, DV], F32, name=f"result{j}", align_bytes=ROW_START)
            nc.scalar.activation(out=result[:], in_=acc[:], func=ACT.Copy, scale=inverse[:, j : j + 1])
            nc.sync.dma_start(out=out[0][j * P : (j + 1) * P, :], in_=result[:])
